import numpy as np, ml_dtypes
CORES = [3,7,11,15,131,135,139,143]
N = 8
BF = ml_dtypes.bfloat16
def gentries(a):
    return np.ascontiguousarray(a.reshape(8, 16, -1).transpose(0, 2, 1)).reshape(8, -1)
def gtable(e):
    e = np.asarray(e); return np.ascontiguousarray(e.reshape(8, -1, 16).transpose(0, 2, 1)).reshape(128, -1).astype(np.int32)
B0, S, RO, DA = 1280, 192, 3, 512
TS, TE, TC = 12, 10, 11
JUMPS = [4, 1, 6]
W = B0 + RO * S
QC = 0.35
def parts(rng):
    x = rng.integers(0, 256, (N, 8, 16, B0)); x = np.where(rng.random((N, 8, 1, B0)) < 0.02, x >> 4, x)
    par = (np.arange(B0) - 1 - rng.integers(0, B0 >> 4, (N, 8, B0))) % B0
    p = np.zeros((N, 8, 16, B0), np.int64); p[:, :, 0] = np.arange(B0)
    for k in range(1, 16): p[:, :, k] = np.take_along_axis(par, p[:, :, k - 1], 2)
    v = rng.integers(0, B0, (N, 8, S))
    near = np.take_along_axis(v, rng.integers(0, S, (N, 8, B0)), 2)
    c = np.where(rng.random((N, 8, B0)) < 0.5, near, rng.integers(0, B0, (N, 8, B0)))
    c = np.where(rng.random((N, 8, B0)) < QC, c, -1)
    return x, p, c, rng.integers(0, 256, (N, 8, 16, DA)), rng.integers(0, 4096, (N, 8, 16, 16)), v
def pack(x, p, c, d, w, v):
    return {"lab": np.ascontiguousarray(x.reshape(N, 128, B0)).astype(np.float32).astype(BF), "pth": np.ascontiguousarray(p.reshape(N, 128, B0)).astype(np.int32),
            "cov": np.ascontiguousarray(c).astype(np.int32), "act": np.ascontiguousarray(d.reshape(N, 128, DA)).astype(np.float32).astype(BF),
            "wts": np.ascontiguousarray(w.reshape(N, 128, 16)).astype(np.int32), "leaf": np.stack([gtable(a) for a in v])}
def setup_inputs(rng):
    return pack(*parts(rng))
def setup_inputs_spread(rng):
    x, p, c, d, w, v = parts(rng)
    x = np.where(rng.random((N, 8, 1, B0)) < 0.03, (256 * np.exp2(-7 * rng.random((N, 8, 1, B0))) * rng.random(x.shape)).astype(np.int64), x)
    d = (256 * np.exp2(-7 * rng.random((N, 8, 1, DA))) * rng.random(d.shape)).astype(np.int64)
    w = np.exp2(12 * rng.random(w.shape)).astype(np.int64) - 1
    p = np.where(rng.random((N, 8, 1, B0)) < 0.5, rng.integers(0, B0, p.shape), p)
    c = np.where(rng.random(c.shape) < 0.5, c, -1)
    v = (B0 * rng.random(v.shape) ** 3).astype(np.int64)
    return pack(x, p, c, d, w, v)
def setup_inputs_ends(rng):
    x = 255 * (rng.random((N, 8, 16, B0)) < 0.75).astype(np.int64); k = rng.random((N, 8, 1, B0))
    x = np.where(k < 0.01, 0, np.where(k > 0.95, 255, x))
    x[:, 1::2, :, B0 - 1] = 255; x[:, ::2, :, B0 - 1] = 0; x[:, :, :, 2:4] = 255
    d = 255 * (rng.random((N, 8, 16, DA)) < 0.85).astype(np.int64); d[..., 16] = 0; d[..., 0] = 255; d[..., DA - 1] = 255
    w = 4095 * rng.integers(0, 2, (N, 8, 16, 16)); w[..., 15] = 4095; w[..., 2] = 0; w[:, 1::2, :, 0] = 4095
    p = (B0 - 1) * rng.integers(0, 2, (N, 8, 16, B0)); p = np.where(rng.random(p.shape) < 0.28, rng.integers(0, B0, p.shape), p)
    c = np.where(rng.random((N, 8, B0)) < 0.06, B0 - 1, -1); c[:, :, 0] = -1; c[:, :, B0 - 1] = -1; c[:, 5, B0 - 1] = B0 - 1
    v = (B0 - 1) * rng.integers(0, 2, (N, 8, S)); v = np.where(rng.random(v.shape) < 0.3, rng.integers(0, B0, v.shape), v)
    return pack(x, p, c, d, w, v)
def setup_inputs_corners(rng):
    x, p, c, d, w, v = parts(rng); a = np.arange(B0); h = B0 >> 1
    for r in range(N):
        for g in range(8):
            k = (g + r) % 8
            if k == 0: p[r, g] = a
            elif k == 1:
                p[r, g] = np.where(((np.arange(16)[:, None] + a) & 1) == 0, 0, B0 - 1); c[r, g, 0] = -1; c[r, g, B0 - 1] = -1
                v[r, g] = np.where(rng.random(S) < 0.5, v[r, g], (B0 - 1) * rng.integers(0, 2, S))
            elif k == 2: w[r, g] = 0
            elif k == 3:
                c[r, g] = np.where(a >= h, a, -1); p[r, g, :, :h] = p[r, g, :, :h] % h
            elif k == 4:
                x[r, g] = np.where(rng.random((1, B0)) < 0.9, 100, x[r, g]); d[r, g] = np.where(rng.random((1, DA)) < 0.5, 0, d[r, g])
                c[r, g] = np.where(rng.random(B0) < 0.02, rng.integers(0, B0, B0), -1)
            elif k == 5:
                w[r, g] = 4095 * np.eye(16, dtype=np.int64)
                x[r, g] = rng.choice(np.array([0, 1, 2, 255]), (16, B0)); d[r, g] = rng.choice(np.array([0, 1, 255]), (16, DA))
                c[r, g] = np.where(rng.random(B0) < 0.03, c[r, g], -1)
            elif k == 6:
                o = int(rng.integers(0, B0)); v[r, g] = o; c[r, g, p[r, g, :, o]] = -1
            else:
                z = 16 - TS + rng.integers(0, 2, (1, B0)); z[:, B0 - 16:] = 0
                x[r, g] = 100 - (np.argsort(rng.random((16, B0)), axis=0) < z)
                c[r, g] = np.where(rng.random(B0) < 0.05, B0 - 1 - rng.integers(0, 16, B0), -1); c[r, g, B0 - 16:] = -1
    return pack(x, p, c, d, w, v)
def setup_inputs_crowd(rng):
    x, p, c, d, w, v = parts(rng); c[:] = -1
    for r in range(N):
        for g in range(8):
            k = (g + r) % 4; o = rng.permutation(B0)[:S + 4]; y, z, q, b = [int(e) for e in o[:4]]; v[r, g] = o[4:]
            p[r, g] = np.where((p[r, g] == y) | (p[r, g] == z) | (p[r, g] == b), q, p[r, g])
            x[r, g, :, z] = 0; x[r, g, :, b] = 0; c[r, g, y] = z; hit = np.zeros(S, bool)
            if k < 2: hit[:] = True
            if k == 0:
                i = int(rng.integers(0, S)); hit[i] = False
                h = 128 * int(np.sum(w[r, g, :, 0])) & 4095; n = TC + (rng.random(B0) < 0.25).astype(np.int64); n[(h * B0) >> 12] = TC
                low = np.argsort(rng.random((16, B0)), axis=0) < n
                x[r, g] = np.where(low, rng.integers(0, 129, (16, B0)), rng.integers(129, 256, (16, B0)))
                x[r, g, :, z] = 0; x[r, g, :, b] = 0; x[r, g, :, int(v[r, g, i])] = 128; d[r, g, :, h & (DA - 1)] = 0
            if k == 3: hit[0] = True
            if k >= 2:
                t = p[r, g, ::2]; t[:, v[r, g]] = b
            p[r, g, 15, v[r, g][hit]] = y
    return pack(x, p, c, d, w, v)
def setup_inputs_brims(rng):
    x, p, c, d, w, v = parts(rng); turn = int(rng.integers(0, 4))
    for r in range(N):
        for g in range(8):
            k = (g + turn) % 4; t = x[r, g]; u = p[r, g]
            if k == 0:
                b = np.where(rng.random((16, B0)) < 0.85, 192, 64 * rng.integers(0, 4, (16, B0))); b[15] = 1
                t[:] = np.where(rng.random((1, B0)) < 0.75, b, t); t[:, [0, B0 - 1]] = 0
                w[r, g] = 64 * rng.integers(56, 64, (16, 16)); w[r, g, 15] = 4095 * ((np.arange(16) + int(rng.integers(0, 2))) & 1)
                e = np.where(rng.random((16, DA)) < 0.9, 0, 64 * rng.integers(0, 4, (16, DA))); e[15] = rng.integers(0, 2, DA); e[:, [0, DA - 1]] = 0
                d[r, g] = e; c[r, g] = -1
            elif k == 1:
                t[:] = np.where(rng.random((1, B0)) < 0.5, 255 - (rng.random((16, B0)) < 0.2).astype(np.int64), t)
                w[r, g] = 4095 - rng.integers(0, 6, (16, 16)); d[r, g] = d[r, g] * (rng.random((1, DA)) < 0.5); c[r, g] = -1
            elif k == 2:
                o = 1 + rng.permutation(B0 - 1)[:S + 10]; y, z = int(o[0]), int(o[1]); few = o[2:10]; v[r, g] = o[10:]
                m = rng.random(S) < 0.75; m[int(rng.integers(0, S))] = False; wait = v[r, g][m]; go = v[r, g][~m]; n = len(wait)
                u[:] = np.where((u == y) | (u == z), 0, u); u[0, wait] = rng.choice(few, n); u[15, wait] = y; u[:, go] = z
                c[r, g] = -1; c[r, g, y] = z
                t[:, 0] = 255; t[:, y] = 100; t[:, z] = 50; t[:, few] = rng.integers(0, 32, (16, 8))
                t[:, wait] = np.where(rng.random((1, n)) < 0.5, 255, t[:, wait])
                t[0, wait] = np.where(rng.random(n) < 0.5, rng.integers(240, 256, n), rng.integers(0, 240, n)); t[0, go] = 0
                w[r, g, :, :2] = 0; w[r, g, 0, :2] = 16
                d[r, g] = d[r, g] * (rng.random((1, DA)) < 0.3)
    return pack(x, p, c, d, w, v)
def check_inputs(d):
    bad = []
    for k, lo, hi in (("lab", 0, 255), ("pth", 0, B0 - 1), ("cov", -1, B0 - 1), ("act", 0, 255), ("wts", 0, 4095), ("leaf", 0, B0 - 1)):
        a = np.asarray(d[k]).astype(np.float64)
        if not (np.min(a) >= lo and np.max(a) <= hi and np.all(a == np.floor(a))): bad.append("range of " + k)
    return bad
def pick(t, ix):
    return np.take_along_axis(t, ix[:, :, None, :], 3)
def reference(lab, pth, cov, act, wts, leaf):
    x = np.full((N, 8, 16, W), 256, np.int32); x[..., :B0] = lab.astype(np.float32).astype(np.int32).reshape(N, 8, 16, B0)
    p = np.zeros((N, 8, 16, W), np.int64); p[..., :B0] = pth.reshape(N, 8, 16, B0)
    c = np.full((N, 8, W), -1, np.int64); c[..., :B0] = cov
    d = act.astype(np.float32).astype(np.int32).reshape(N, 8, 16, DA)
    w = wts.astype(np.int32).reshape(N, 8, 16, 16).transpose(0, 1, 3, 2)
    v = np.stack([gentries(a) for a in leaf]).astype(np.int64)
    for t in range(RO):
        B = B0 + t * S
        xv = pick(x, v); pv = pick(p, v)
        flat = pv.reshape(N, 8, 16 * S); xp = pick(x, flat).reshape(N, 8, 16, 16, S)
        cp = np.take_along_axis(c, flat, 2); xc = pick(x, np.maximum(cp, 0)).reshape(N, 8, 16, 16, S)
        holds = (cp.reshape(N, 8, 16, S) >= 0) & (np.sum(xp >= xc, axis=2) >= TS)
        susp = np.any(holds, axis=2); live = ~susp; cnt = np.sum(susp, axis=2)
        h = np.matmul(w, xv) & 4095
        xn = np.abs(xv - pick(d, h[:, :, 0] & (DA - 1)))
        q = (h[:, :, 1] * B) >> 12
        e = np.stack([np.take_along_axis(x[(r + JUMPS[t]) % N], q[r][:, None, :], 2) for r in range(N)])
        low = np.sum(xp >= e[:, :, :, None, :], axis=2) < TE
        want = np.any(low, axis=2) & live & (e[:, :, 0] < 256)
        tg = np.where(want, np.take_along_axis(pv, np.argmax(low, axis=2)[:, :, None, :], 2)[:, :, 0], -1)
        cand = ((np.matmul(w, xn) & 4095) * B) >> 12
        xk = pick(x, cand.reshape(N, 8, 16 * S)).reshape(N, 8, 16, 16, S)
        fit = np.sum(xn[:, :, :, None, :] >= xk, axis=2) >= (TC + (cnt & 1))[:, :, None, None]
        cn = np.where(np.any(fit, axis=2), np.take_along_axis(cand, np.argmax(fit, axis=2)[:, :, None, :], 2)[:, :, 0], -1)
        new = np.broadcast_to(B + np.arange(S), (N, 8, S))
        for r in range(N):
            for g in range(8):
                s = np.nonzero(tg[r, g] >= 0)[0]
                u, first = np.unique(tg[r, g][s], return_index=True); s = s[first]
                x[r, g][:, u] = np.maximum(x[r, g][:, u], e[r, g][:, s])
        x[..., B:B + S] = np.where(live[:, :, None, :], xn, 256)
        p[..., B:B + S] = np.where(live[:, :, None, :], np.concatenate([new[:, :, None, :], pv[:, :, :15]], axis=2), 0)
        c[..., B:B + S] = np.where(live, cn, -1)
        v = np.where(live, new, v)
    return {"yx": x.reshape(N, 128, W).astype(np.float32).astype(BF), "yp": np.ascontiguousarray(p[..., B0:]).reshape(N, 128, RO * S).astype(np.float32),
            "yc": np.ascontiguousarray(c[..., B0:]).astype(np.float32), "yv": np.stack([gtable(a) for a in v]).astype(np.float32)}

@@ -1,0 +1,647 @@
+from concourse.bass import DstId, RemoteDMATransfer
+from concourse.mybir import AluOpType as A, AxisListType, ActivationFunctionType as F
+
+B0, S, RO, DA = 1280, 192, 3, 512
+JUMPS = [4, 1, 6]
+O = 208
+CW = 192
+BS = [B0 + S * t for t in range(RO + 1)]
+
+SCRATCH = {}
+
+
+def _sb(name, shape, d):
+    SCRATCH[name] = ("sbuf", [128] + shape, d)
+
+
+for _t in range(4):
+    _sb("tab%d" % _t, [O + BS[_t]], "bfloat16")
+for _t in range(3):
+    _sb("rep%d" % _t, [O + BS[_t]], "bfloat16")
+    for _n in ("tb", "ch", "hx"):
+        _sb("%s%d" % (_n, _t), [BS[_t]], "bfloat16")
+    for _n in ("xp", "xk", "ce", "cc"):
+        _sb("%s%d" % (_n, _t), [S * 16], "bfloat16")
+    _sb("eq%d" % _t, [1248], "bfloat16")
+_sb("tm", [16], "bfloat16")
+for _n in ("dd", "zz", "ee", "fl", "sg", "lo", "fi", "vals", "du", "hn"):
+    _sb(_n, [3 * S], "bfloat16")
+for _n in ("xh", "se", "sc"):
+    _sb(_n, [3 * S], "float16")
+for _n in ("pv", "cf", "ypb", "ycb"):
+    _sb(_n, [3 * S], "float32")
+for _n in ("ci", "cj"):
+    _sb(_n, [3 * S], "int32")
+for _n in ("pl", "cl"):
+    _sb(_n, [3 * S], "uint16")
+for _n in ("hi", "hj"):
+    _sb(_n, [72], "int32")
+for _n in ("al", "ql", "tgl", "off", "vl"):
+    _sb(_n, [36], "uint16")
+for _n in ("bc", "t2", "nw", "nb", "pre", "mm", "t1"):
+    _sb(_n, [36], "float32")
+_sb("ab", [12, S], "float32")
+_sb("prd", [12], "float32")
+_sb("i8", [S], "bfloat16")
+_sb("vf", [48], "float32")
+_sb("covl", [104], "uint16")
+_sb("rvals", [2 * S], "bfloat16")
+_sb("roff", [24], "uint16")
+_sb("acts", [DA], "bfloat16")
+_sb("pths", [B0], "int32")
+_sb("wt", [16], "int32")
+_sb("wa", [32], "int32")
+_sb("wf", [32], "float32")
+_sb("leafs", [12], "int32")
+_sb("covt", [5, 16], "int32")
+_sb("covm", [5, 32], "float32")
+_sb("covx", [5, 32], "float32")
+_sb("covs", [5, 16], "float32")
+_sb("isf", [S], "float32")
+_sb("pi", [8], "int32")
+_sb("col", [24], "float32")
+_sb("ai", [8], "int32")
+_sb("sl", [12], "float32")
+_sb("s16", [12], "float32")
+_sb("prc", [12], "float32")
+for _n in ("o32", "b1", "bo", "e32"):
+    _sb(_n, [144], "float32")
+for _t in (1, 2):
+    _sb("tac%d" % _t, [O + BS[_t]], "bfloat16")
+for _n in ("ta", "tc", "i32", "s32"):
+    _sb(_n, [128], "float32")
+for _n in ("bok", "idn", "ineg", "ip", "im", "tr", "wh", "wl"):
+    _sb(_n, [128], "bfloat16")
+_sb("boh", [128], "float16")
+for _n in ("eb", "ebn"):
+    _sb(_n, [144], "bfloat16")
+for _n in ("ebh", "w0h", "w1h"):
+    _sb(_n, [144], "float16")
+_sb("g8", [8], "float16")
+for _n in ("is16", "ones"):
+    _sb(_n, [S], "bfloat16")
+_sb("cm", [512], "bfloat16")
+POOL = ["P0", "P1", "P2", "P3"]
+for _n in POOL + ["KB", "CE", "CC", "M1"]:
+    SCRATCH[_n] = ("psum", [128, 512], "float32")
+
+NDMA = 36
+SEMAPHORES = ["pe", "dve", "act", "pool", "sent"] + ["d%d" % i for i in range(NDMA)] + ["a%d" % i for i in range(8)]
+
+EST = dict(cyc=1.04, pcy=0.55, gat=1.6, sca=3.8, hop=110.0, own=70.0, fv=60.0, fa=90.0, rlat=2500.0, rbw=55.0, look=120.0)
+PLAN = [dict(zip(("xp", "xk", "ce", "cc", "ho", "ee", "dd"), _p.split("/"))) for _p in
+        "vaavav/avaaav/avvvav/vavvaa/vvaa/a/a avavva/avavva/vvvaaa/vaavaa/vmav/a/a avaaav/vaaavv/aavvvv/aaavva/vaav/v/a".split()]
+ORDER = ["0a020c0m00030n050406080o0701090b180d0q0p0s0e0t0r0f1i1m1l0v0g2b0z2a2j100l2f2e121n132d1o0i142g2c0w1p1d2n2h172p0j112i152q2z0k320h162o331a2w0u30341e3519311c2x1b0x1g1q1f360y2r2y5m2l2m3j3i3l3k3s3g3h3x1r1s3m2s1t2t202u1z37432v2k1x4944381j453e461k471h1v4a213t26483y253u295n4b1u23223v1y3n24281w41273z4c3f3q4d39403o3a3b3w3p3c424e5u5p4j5q5s3r5v4f3d4i5w5r4k5x4g4h5t604l4m625y4p61644q4y664n4r4w4o5e63584x5j4u595f4s5z4v504z5c4t54515a55525b565365575d5g675h5i5l5k685o6i6u766a6j9o6k6z6v6r69706b6w6s717f726x736m6t6l6y6c7n6n6d7l6f7k6o6e6q747g7m757i7w6p7u7877807j7x7p7z797v81827r7h7a837o7q7t6g7b7c6h7s7d857e7y9t9s849r868l9v8d8k879u9w9x8m8b9y8e8h8f8n8c8g898i8o8a8j8r9p8s88a29c8pa9948t8q8y929z959l9a8z969d8u9ba79390978v8w91988x9g9e99aa9h9f9i9ja09ka39n9ma8a19qawb8abala5a4axatb1a6ayamb2aubhb3acazavb4adb0aeb5aoblboanafbkapagaqasbiaibmahbrb6bnc2bpb7btb9arc3bsbxc1babuc4bwbbbybjbcajbqbzakc5bdc6bec0bfdndockbvdrdqdtdsdvcjducle3bgcedwcmc7e4cndpcqc8coccc9crcpd1csczdyd2dbd0dxcte1cve5d7d9cwd3d8dzd5cudddccxd6cad4dfe6cydgdadedhe0e7didjdkcfe2cge9cbdmdle8cieaebcdecchedee"]
+
+
+def build(g, core, T, topo, rank):
+    ops = []
+    cores = T.cores
+    N = len(cores)
+    V, ACT, PE = g.vector, g.scalar, g.tensor
+    nd = [0]
+    na = [0]
+    CYC, GAT, SCA = EST["cyc"], EST["gat"], EST["sca"]
+
+    def add(eng, fn, r, w, cost, bank=None, grp=None, lat=0.0, sem=None, cnt=0, loc=0):
+        o = dict(eng=eng, fn=fn, r=list(r), w=list(w), cost=cost, bank=bank, grp=grp, lat=lat, sem=sem, cnt=cnt, loc=loc)
+        if isinstance(bank, dict):
+            bank["n"] += 1
+        ops.append(o)
+
+    def dv(fn, r, w, n, bank=None):
+        add("dve", lambda: [fn()], r, w, EST["fv"] + max(64, n) * CYC, bank)
+
+    def ac(fn, r, w, n, bank=None):
+        add("act", lambda: [fn()], r, w, EST["fa"] + max(64, n) * CYC, bank)
+
+    def pe(fn, cyc, r, w, bank, grp=None):
+        add("pe", lambda: [PE.matmul(*m) for m in fn()], r, w, cyc * EST["pcy"], bank, grp, lat=80.0)
+
+    def po(fn, r, w, n):
+        add("pool", lambda: [fn()], r, w, 170 + 2 * n * CYC)
+
+    def tile():
+        return dict(n=0, b=None)
+
+    def P(tl):
+        return T[tl["b"]]
+
+    def dma(q, out, in_, r, w, nbytes):
+        s = "d%d" % nd[0]
+        nd[0] += 1
+        eng = g.sync if q == "sp" else g.scalar
+        add(q, lambda: [eng.dma_start(out, in_)], r, w, 80.0, lat=1700 + nbytes / 220.0, sem=s, cnt=16)
+
+    def send(t, pairs, r, w, nbytes):
+        dst = cores[(rank - JUMPS[t]) % N]
+        src = cores[(rank + JUMPS[t]) % N]
+        s = "a%d" % na[0]
+        na[0] += 1
+        rid, pid = topo.addr(dst, core)
+        en = topo.engines(core, dst)
+
+        def fn():
+            if len(pairs) == 1:
+                g.remote_dma(pairs[0][0], pairs[0][1], T.sem[s], T.sem.sent, pid, rid, topo.mask(core, dst))
+            else:
+                h = len(en) // len(pairs)
+                tr = [RemoteDMATransfer(dst_ids=[DstId(rid=rid, pnc=pid)],
+                                        dma_engine_mask=sum(1 << e for e in en[i * h:(i + 1) * h]),
+                                        remote_sem=T.sem[s], src=p[1], dst=p[0]) for i, p in enumerate(pairs)]
+                g.remote_dma_fused(tr, local_sem=T.sem.sent)
+            return []
+        add("pool", fn, r, w, 500.0, lat=EST["rlat"] + nbytes / EST["rbw"], sem=s, cnt=len(topo.engines(src, core)), loc=len(en))
+
+    def ts(out, in0, s1, op0, s2=None, op1=None):
+        if op1 is None:
+            return V.tensor_scalar(out, in0, s1, None, op0)
+        return V.tensor_scalar(out, in0, s1, s2, op0, op1)
+
+    def lin(out, in_, r, w, n, scale=1.0, bias=0.0, f=None):
+        ac(lambda: ACT.activation(out, in_, f or F.Identity, bias=bias, scale=scale), r, w, n)
+
+    tab = [T["tab%d" % t] for t in range(4)]
+    rep = [T["rep%d" % t] for t in range(3)]
+    col = T.col
+    dma("sp", tab[0][:, O:O + B0], T.lab[:], [], ["tab0"], 330e3)
+    dma("act", T.leafs[:], T.leaf[:], [], ["leafs"], 6e3)
+    dma("act", T.wt[:], T.wts[:], [], ["wt"], 8e3)
+    for b in range(5):
+        dma("act" if b < 2 else "sp", T.covt[:, b, :], T.cov[:, 256 * b:256 * b + 256], [], ["covt%d" % b], 8e3)
+    if "v" in PLAN[0]["ho"][0:3]:
+        dma("act", tab[1][:, O:O + B0], T.lab[:], [], ["tab1c"], 500e3)
+    dma("sp", T.acts[:], T.act[:], [], ["acts"], 700e3)
+    dma("sp", T.pths[:], T.pth[:], [], ["pths"], 1300e3)
+    if "v" not in PLAN[0]["ho"][0:3]:
+        dma("sp", tab[1][:, O:O + B0], T.lab[:], ["pths"], ["tab1c"], 330e3)
+    K, PO, PEV, CB, W0, W1, K0, YB, AC, FB = 0, 2, 3, 5, 6, 7, 11, 8, 12, 16
+
+    def c1(i):
+        return col[:, i:i + 1]
+    po(lambda: g.iota(T.pi[:, 0:1], [[0, 1]], 0, 1), [], ["pi0"], 1)
+    po(lambda: g.iota(T.o32[:], [[0, 144]], 1, 0, allow_small_or_imprecise_dtypes=True), [], ["o32"], 144)
+    po(lambda: g.affine_select(T.b1[:], T.o32[:], [[-16, 9], [0, 16]], A.is_ge, 0.0, 0, 1), ["o32"], ["b1"], 144)
+    po(lambda: g.affine_select(T.bo[:], T.b1[:], [[16, 9], [0, 16]], A.is_ge, 0.0, 15, -1), ["b1"], ["bo"], 144)
+    po(lambda: g.affine_select(T.e32[:], T.bo[:], [[0, 9], [1, 16]], A.is_equal, 0.0, -15, 0), ["bo"], ["e32"], 144)
+    po(lambda: g.affine_select(T.i32[:], T.o32[:, 0:128], [[1, 128]], A.is_equal, 0.0, 0, -1), ["o32"], ["i32"], 128)
+    po(lambda: g.affine_select(T.s32[:], T.bo[:, 0:128], [[1, 128]], A.is_equal, 0.0, -1, -1), ["bo"], ["s32"], 128)
+    po(lambda: g.affine_select(T.ta[:], T.bo[:, 0:128], [[1, 128]], A.is_ge, 0.0, 0, -1), ["bo"], ["ta"], 128)
+    po(lambda: g.affine_select(T.tc[:], T.ta[:], [[1, 128]], A.not_equal, -1.0, 0, -1), ["ta"], ["tc"], 128)
+    po(lambda: g.iota(T.s16[:], [[16, 12]], 0, 0, allow_small_or_imprecise_dtypes=True), [], ["s16"], 12)
+    po(lambda: g.iota(T.isf[:], [[1, S]], 0, 0, allow_small_or_imprecise_dtypes=True), [], ["isf"], S)
+    dv(lambda: V.memset(tab[0][:, CW:O], 512.0), [], ["sen0"], 16)
+    dv(lambda: V.memset(tab[1][:, CW:O], 512.0), [], ["sen1"], 16)
+    dv(lambda: V.memset(T.cm[:], -0.6875), [], ["cm"], 256)
+    dv(lambda: ts(T.pi[:, 1:2], T.pi[:, 0:1], 15, A.bitwise_and), ["pi0"], ["pi1"], 1)
+    dv(lambda: ts(T.pi[:, 2:3], T.pi[:, 0:1], 4, A.arith_shift_right, 1, A.bitwise_and), ["pi0"], ["pi2"], 1)
+    dv(lambda: V.tensor_copy(c1(K), T.pi[:, 1:2]), ["pi1"], ["K"], 1)
+    dv(lambda: V.tensor_copy(c1(PO), T.pi[:, 2:3]), ["pi2"], ["PO"], 1)
+    dv(lambda: ts(c1(PEV), T.pi[:, 2:3], -1.0, A.mult, 1.0, A.add), ["pi2"], ["PEV"], 1)
+    lin(c1(CB), c1(K), ["K"], ["CB"], 1, -2048.0, -4095.0)
+    lin(c1(K0), c1(K), ["K"], ["K0"], 1, -1.0, 1.0, F.Relu)
+    for t in range(3):
+        lin(c1(YB + t), c1(K0), ["K0"], ["YB%d" % t], 1, float(BS[t]), -2048.0)
+    lin(T.bok[:], T.bo[:, 0:128], ["bo"], ["bok"], 128, 4096.0)
+    lin(T.eb[:], T.e32[:], ["e32"], ["eb"], 144)
+    lin(T.ebn[:], T.e32[:], ["e32"], ["ebn"], 144, -256.0)
+    lin(T.idn[:], T.i32[:], ["i32"], ["idn"], 128)
+    lin(T.ineg[:], T.i32[:], ["i32"], ["ineg"], 128, -1.0)
+    lin(T.ip[:], T.i32[:], ["i32"], ["ip"], 128, 2048.0)
+    lin(T.im[:], T.i32[:], ["i32"], ["im"], 128, -2048.0)
+    lin(T.tr[:], T.tc[:], ["tc"], ["tr"], 128, -2048.0)
+    lin(T.is16[:], T.isf[:], ["isf"], ["is16"], S, 1.0 / 16)
+    add("act", lambda: [ACT.activation(T.ones[:, 0:144], T.o32[:], F.Sigmoid, scale=128.0)], ["o32"], ["ones0"], 1600.0)
+    lin(T.ones[:, 144:S], T.ones[:, 0:S - 144], ["ones0"], ["ones"], 48)
+    lin(T.sl[:], T.s16[:], ["s16", "K"], ["sl"], 12, 1.0, c1(K))
+    lin(T.prc[:], T.sl[:], ["sl"], ["prc"], 12, 1.0, float(1 - O))
+    if any(p["dd"] == "a" for p in PLAN):
+        lin(T.prd[:], T.sl[:], ["sl"], ["prd"], 12, -4096.0)
+        lin(T.i8[:], T.isf[:], ["isf"], ["i8"], S, 1.0 / 512)
+    for t in range(3):
+        lin(T.nw[:, 12 * t:12 * t + 12], T.sl[:], ["sl"], ["nw%d" % t], 12, 1.0, float(BS[t] - 4096))
+    dv(lambda: ts(T.tm[:], T.isf[:, 0:16], c1(K), A.is_le, -4096.0, A.mult), ["isf", "K"], ["tm"], 16)
+    dv(lambda: V.tensor_copy(T.boh[:], T.bo[:, 0:128]), ["bo"], ["boh"], 128)
+    dv(lambda: V.tensor_copy(T.ebh[:], T.eb[:]), ["eb"], ["ebh"], 72)
+    dv(lambda: V.tensor_copy(T.g8[:], T.bo[:, 0:128:16]), ["bo"], ["g8"], 8)
+    dv(lambda: ts(T.ai[:, 0:1], T.wt[:, 0:1], 8.0, A.mult, 2048.0, A.add), ["wt"], ["ai0"], 1)
+    dv(lambda: ts(T.ai[:, 1:2], T.wt[:, 1:2], 2048.0, A.add), ["wt"], ["ai1"], 1)
+    dv(lambda: ts(T.pi[:, 4:6], T.ai[:, 0:2], 4095, A.bitwise_and), ["ai0", "ai1"], ["pi4"], 2)
+    dv(lambda: ts(col[:, W0:W0 + 2], T.pi[:, 4:6], -2048.0, A.add), ["pi4"], ["W"], 2)
+    dv(lambda: ts(T.w0h[:], T.e32[:], c1(W0), A.mult), ["e32", "W"], ["w0h"], 144)
+    dv(lambda: ts(T.w1h[:], T.e32[:], c1(W1), A.mult), ["e32", "W"], ["w1h"], 144)
+    dv(lambda: ts(T.wa[:, 0:16], T.wt[:], 4032, A.bitwise_and), ["wt"], ["wa"], 16)
+    dv(lambda: ts(T.wa[:, 16:32], T.wt[:], 63, A.bitwise_and), ["wt"], ["wb"], 16)
+    dv(lambda: V.tensor_copy(T.wf[:], T.wa[:]), ["wa", "wb"], ["wf"], 32)
+    for j in range(8):
+        lin(T.wh[:, 16 * j:16 * j + 16], T.wf[:, 0:16], ["wf", "bo"], ["wh%d" % j], 16, T.bo[:, 16 * j:16 * j + 1])
+        lin(T.wl[:, 16 * j:16 * j + 16], T.wf[:, 16:32], ["wf", "bo"], ["wl%d" % j], 16, T.bo[:, 16 * j:16 * j + 1])
+    wk = ["wh%d" % j for j in range(8)] + ["wl%d" % j for j in range(8)]
+    ct = ["covt%d" % b for b in range(5)]
+    dv(lambda: ts(T.covm[:, :, 0:16], T.covt[:], 16.0, A.add, c1(PEV), A.mult), ct + ["PEV"], ["covm0"], 80)
+    dv(lambda: ts(T.covm[:, :, 16:32], T.covt[:], 16.0, A.add, c1(PO), A.mult), ct + ["PO"], ["covm1"], 80)
+    for b in range(5):
+        dv(lambda b=b: V.transpose(T.covx[:, b, :], T.covm[:, b, :]), ["covm0", "covm1"], ["covx%d" % b], 32)
+    dv(lambda: V.tensor_tensor(T.covs[:], T.covx[:, :, 0:16], T.covx[:, :, 16:32], A.add),
+       ["covx%d" % b for b in range(5)], ["covs"], 160)
+    dv(lambda: V.tensor_copy(T.covl[:, 0:80], T.covs[:]), ["covs"], ["covl"], 80)
+    dv(lambda: V.tensor_copy(T.vl[:, 0:12], T.leafs[:]), ["leafs"], ["vl0"], 12)
+    dv(lambda: V.tensor_copy(T.vf[:, 0:12], T.leafs[:]), ["leafs"], ["vf0"], 12)
+    dv(lambda: V.tensor_copy(T.pv[:, 0:S], T.pths[:].indirect(T.vl[:, 0:12])), ["pths", "vl0"], ["pv0"], S * GAT)
+    dv(lambda: V.tensor_copy(T.pl[:, 0:S], T.pv[:, 0:S]), ["pv0"], ["pl0"], S)
+
+    def E(buf, j):
+        return buf[:, 15 - j:143 - j]
+
+    def one_round(t):
+        B = BS[t]
+        c = B // 64
+        plan = PLAN[t]
+        k = lambda n: "%s_%d" % (n, t)
+        X = lambda buf: buf[:, S * t:S * t + S]
+        L = lambda buf: buf[:, 12 * t:12 * t + 12]
+        XJ = lambda buf, j: buf[:, S * t + j:S * t + S:16]
+        tk = ["tab0", "sen0"] if t == 0 else ["tab%d" % t, "new%d" % t]
+        win = tab[t][:, O:O + B]
+        cwin = tab[t][:, CW:O + B]
+        nxt = tab[t + 1]
+        tb, ch, hx, xp, xk, ce, cc, eq = [T["%s%d" % (n, t)] for n in ("tb", "ch", "hx", "xp", "xk", "ce", "cc", "eq")]
+        if t == 0:
+            send(0, [(rep[0][:, O:O + B], win)], tk, ["rep0"], 256 * B)
+        if t < 2:
+            send(t + 1, [(rep[t + 1][:, O:O + B], win)], tk, ["repc%d" % (t + 1)], 256 * B * (2 if t == 0 else 1))
+        if t > 0:
+            dma("sp", nxt[:, CW:O + B], cwin, tk, ["tab%dc" % (t + 1)], 256 * B)
+        dv(lambda: V.tensor_copy(X(T.xh), win.indirect(L(T.vl))), tk + ["vl%d" % t], [k("xh")], S * GAT)
+        for h, wm in enumerate((T.w0h, T.w1h)):
+            pe(lambda h=h, wm=wm: [(T.M1[:, 384 + 12 * h:396 + 12 * h], E(wm, j), XJ(T.xh, j), j == 0, j == 15) for j in range(16)],
+               1024, [k("xh"), "w%dh" % h], ["HL%d" % h], "M1")
+        hi, hj = T.hi[:, 24 * t:24 * t + 24], T.hj[:, 24 * t:24 * t + 24]
+        dv(lambda: V.tensor_copy(hi, T.M1[:, 384:408]), ["HL0", "HL1"], [k("hi")], 24, "M1")
+        dv(lambda: ts(hj, hi, 4095, A.bitwise_and), [k("hi")], [k("hj")], 24)
+        dv(lambda: ts(L(T.al), T.hj[:, 24 * t:24 * t + 12], 0.125, A.mult), [k("hj")], [k("al")], 12)
+        dv(lambda: ts(L(T.ql), T.hj[:, 24 * t + 12:24 * t + 24], c / 64.0, A.mult, -63 / 128.0, A.add), [k("hj")], [k("ql")], 12)
+
+        def hold(i, a, b):
+            n = 16 * (b - a)
+            lk = ["covl"] if i < 3 else ["cvl%d" % u for u in range(t)]
+            lab = tab[t][:, O + 16 * a:O + 16 * b]
+            gat = cwin.indirect(T.covl[:, a:b])
+            if plan["ho"][i] == "v":
+                two, tw = (nxt, ["tab1c"]) if t == 0 else (T["tac%d" % t], ["tac%d" % t] + (["tan%d" % t] if i == 3 else []))
+                dv(lambda: V.tensor_tensor(ch[:, 16 * a:16 * b], gat, two[:, O + 16 * a:O + 16 * b], A.is_le),
+                   tk + lk + tw, [k("ch%d" % i)], n * GAT)
+            else:
+                ac(lambda: ACT.activation(hx[:, 16 * a:16 * b], gat, F.Copy), tk + lk, [k("hx%d" % i)], n * GAT)
+                d = tile()
+                pe(lambda: [(P(d)[:, 0:n], T.idn[:], lab, True, False), (P(d)[:, 0:n], T.ineg[:], hx[:, 16 * a:16 * b], False, True)],
+                   2 * n, [k("hx%d" % i), "idn", "ineg"], [k("hd%d" % i)], d)
+                if plan["ho"][i] == "a":
+                    ac(lambda: ACT.activation(ch[:, 16 * a:16 * b], P(d)[:, 0:n], F.Sigmoid, bias=128.0, scale=256.0),
+                       [k("hd%d" % i), "ones0"], [k("ch%d" % i)], n, d)
+                else:
+                    dv(lambda: ts(ch[:, 16 * a:16 * b], P(d)[:, 0:n], 0.0, A.is_ge), [k("hd%d" % i)], [k("ch%d" % i)], n, d)
+            h = tile()
+            pe(lambda: [(P(h)[:, 0:n], T.bok[:], T.cm[:, 0:n], True, False), (P(h)[:, 0:n], T.bok[:], ch[:, 16 * a:16 * b], False, True)],
+               2 * n, [k("ch%d" % i), "bok", "cm"], [k("hv%d" % i)], h)
+            if i < 3:
+                dv(lambda: V.tensor_tensor(tb[:, 16 * a:16 * b], P(h)[:, 0:n], lab, A.max), [k("hv%d" % i)], [k("tb%d" % i)], n, h)
+            else:
+                dma("sp", tb[:, B0:B], lab, tk, [k("tb3")], 256 * n)
+                ac(lambda: ACT.activation(T.hn[:, S * t - S:S * t - S + n], P(h)[:, 0:n], F.Relu), [k("hv3")], [k("hn")], n, h)
+        chunks = [(0, 32), (32, 64), (64, 80)] + ([(80, 80 + 12 * t)] if t else [])
+        for i, (a, b) in enumerate(chunks):
+            hold(i, a, b)
+        tbk = [k("tb%d" % i) for i in range(len(chunks))]
+        dv(lambda: V.tensor_tensor(X(T.dd), T.acts[:].indirect(L(T.al)), X(T.xh), A.subtract),
+           ["acts", k("al"), k("xh")], [k("dd")], S * GAT)
+        ac(lambda: ACT.activation(X(T.zz), X(T.dd), F.Abs), [k("dd")], [k("zz")], S)
+        hc = tile()
+        pe(lambda: [(P(hc)[:, 0:S], T.wh[:], X(T.zz), True, False), (P(hc)[:, 0:S], T.wl[:], X(T.zz), False, True)],
+           2 * S, [k("zz")] + wk, [k("HC")], hc)
+        dv(lambda: V.tensor_copy(X(T.ci), P(hc)[:, 0:S]), [k("HC")], [k("ci")], S, hc)
+        dv(lambda: ts(X(T.cj), X(T.ci), 4095, A.bitwise_and), [k("ci")], [k("cj")], S)
+        dv(lambda: ts(X(T.cl), X(T.cj), c / 64.0, A.mult, -63 / 128.0, A.add), [k("cj")], [k("cl")], S)
+        dv(lambda: V.tensor_copy(X(T.cf), X(T.cl)), [k("cl")], [k("cf")], S)
+        rk = ["rep0"]
+        if t > 0:
+            dv(lambda: V.tensor_copy(rep[t][:, 0:O + BS[t - 1]].indirect(T.roff[:, 12 * t - 12:12 * t]),
+                                     T.rvals[:, S * t - S:S * t]),
+               ["repc%d" % t, "rv%d" % t, "ro%d" % t], ["rep%d" % t], S * SCA)
+            rk = ["rep%d" % t, "rv%d" % t]
+        if plan["ee"] == "a":
+            ac(lambda: ACT.activation(X(T.ee), rep[t][:, O:O + B].indirect(L(T.ql)), F.Copy), rk + [k("ql")], [k("ee")], S * GAT)
+        else:
+            dv(lambda: V.tensor_copy(X(T.ee), rep[t][:, O:O + B].indirect(L(T.ql))), rk + [k("ql")], [k("ee")], S * GAT)
+        ac(lambda: ACT.activation(X(T.fl), X(T.ee), F.Relu, bias=-510.0, scale=2.0), [k("ee")], [k("fl")], S)
+
+        def gather(engs, out, window, lst, r, key):
+            for i, e in enumerate(engs):
+                o, w = out[:, 512 * i:512 * i + 512], window.indirect(lst[:, S * t + 32 * i:S * t + 32 * i + 32])
+                if e == "a":
+                    ac(lambda o=o, w=w: ACT.activation(o, w, F.Copy), r, [k(key + str(i))], 512 * GAT)
+                else:
+                    dv(lambda o=o, w=w: V.tensor_copy(o, w), r, [k(key + str(i))], 512 * GAT)
+
+        def compare(u, src, sk, vec, vk, out, ok, op, bank):
+            s0 = 64 * u
+            v = vec[:, S * t + s0:S * t + s0 + 64]
+            sks = [k(sk + str(2 * u)), k(sk + str(2 * u + 1))]
+            engs = plan[ok][2 * u:2 * u + 2]
+            ls, lv = (T.idn, T.ineg) if op == A.is_ge else (T.ineg, T.idn)
+            if "v" in engs:
+                r8 = tile()
+                pe(lambda: [(P(r8)[:, j:512:8], T.idn[:], v, True, True) for j in range(8)], 512, [vk, "idn", sks[0]],
+                   [k("R%s%d" % (ok, u))], r8)
+
+            def half(h):
+                o = out[:, 1024 * u + h:1024 * u + 1024:2]
+                key = k("%s%d%d" % (ok, u, h))
+                if engs[h] == "v":
+                    dv(lambda: V.tensor_tensor(o, src[:, 1024 * u + h:1024 * u + 1024:2], P(r8)[:], op),
+                       [k("R%s%d" % (ok, u))] + sks, [key], 512, r8)
+                else:
+                    d = tile()
+
+                    def mms():
+                        m = []
+                        for j in range(8):
+                            m.append((P(d)[:, j:512:8], lv[:], v, True, False))
+                            m.append((P(d)[:, j:512:8], ls[:], src[:, 1024 * u + 2 * j + h:1024 * u + 1024:16], False, True))
+                        return m
+                    pe(mms, 1024, [vk, "idn", "ineg"] + sks, ["D" + key], d)
+                    ac(lambda: ACT.activation(o, P(d)[:], F.Sigmoid, bias=128.0, scale=256.0), ["D" + key, "ones0"], [key], 512, d)
+            half(0)
+            half(1)
+            pe(lambda: [(T[bank][:, s0:s0 + 64], E(T.eb, j), out[:, 1024 * u + j:1024 * u + 1024:16], j == 0, j == 15) for j in range(16)],
+               1024, [k("%s%d0" % (ok, u)), k("%s%d1" % (ok, u)), "eb"], ["%s%d" % (bank, u)], bank)
+
+        gather(plan["xp"], xp, tb[:], T.pl, tbk + ["pl%d" % t], "xp")
+        for u in range(3):
+            pe(lambda u=u: [(T.KB[:, 64 * u:64 * u + 64], T.bok[:], xp[:, 1024 * u + j:1024 * u + 1024:16], j == 0, j == 15 and t == 0) for j in range(16)] +
+               [(T.KB[:, 64 * u:64 * u + 64], T.bok[:], T.hn[:, S * (t - 1 + j) + 64 * u:S * (t - 1 + j) + 64 * u + 64], False, j == t - 1)
+                for j in range(t)],
+               1024 + 64 * t, [k("xp%d" % (2 * u)), k("xp%d" % (2 * u + 1)), "bok"] + ([k("hn")] if t else []), ["V%d" % u], "KB")
+            compare(u, xp, "xp", T.ee, k("ee"), ce, "ce", A.is_ge, "CE")
+        sg = X(T.sg)
+        ac(lambda: ACT.activation(sg, T.KB[:, 0:S], F.Sign, bias=-65400.5, scale=1.0 / 4096, accum_out=c1(AC + t)),
+           ["V0", "V1", "V2"], [k("sg")], S + 130, "KB")
+        dv(lambda: ts(T.ai[:, 2 + t:3 + t], c1(AC + t), 0.5, A.mult, 96.0, A.add), [k("sg")], [k("a1")], 1)
+        dv(lambda: ts(T.ai[:, 5 + t:6 + t], T.ai[:, 2 + t:3 + t], 1, A.bitwise_and), [k("a1")], [k("a2")], 1)
+        dv(lambda: ts(c1(FB + t), T.ai[:, 5 + t:6 + t], -1.0, A.mult, -10.5, A.add), [k("a2")], [k("fb")], 1)
+        nl = tile()
+        pe(lambda: [(P(nl)[:, 0:S], T.idn[:], X(T.zz), True, False), (P(nl)[:, 0:S], T.ip[:], sg, False, True)],
+           2 * S, [k("zz"), k("sg"), "idn", "ip"], [k("NL")], nl)
+        dv(lambda: ts(nxt[:, O + B:O + B + S], P(nl)[:, 0:S], 2048.0, A.add, 256.0, A.min), [k("NL")], ["new%d" % (t + 1)], S, nl)
+        pe(lambda: [(T.M1[:, 416:428], T.i32[:], L(T.nw), True, False)] +
+           [(T.M1[:, 416:428], E(T.ebn, j), XJ(T.sg, j), False, j == 15) for j in range(16)],
+           1280, [k("sg"), "ebn", "i32", "nw%d" % t], ["LL"], "M1")
+        vn = T.vf[:, 12 * t + 12:12 * t + 24]
+        dv(lambda: V.tensor_tensor(vn, T.M1[:, 416:428], L(T.vf), A.max), ["LL", "vf%d" % t], ["vf%d" % (t + 1)], 12, "M1")
+        u1 = tile()
+        pe(lambda: [(P(u1)[:, 0:S], T.s32[:], X(T.pv), True, False), (P(u1)[:, 0:S], E(T.eb, 0), T.is16[:], False, False),
+                    (P(u1)[:, 0:S], T.im[:], sg, False, True)], 6 * S, ["pv%d" % t, k("sg"), "s32", "eb", "is16", "im"], [k("U1")], u1)
+        ac(lambda: ACT.activation(X(T.ypb), P(u1)[:, 0:S], F.Relu, bias=c1(YB + t)), [k("U1"), "YB%d" % t], [k("yp")], S, u1)
+        dma("sp", T.yp[:, S * t:S * t + S], X(T.ypb), [k("yp")], [], 98e3)
+        if t < 2:
+            dv(lambda: V.tensor_copy(T.vl[:, 12 * t + 12:12 * t + 24], vn), ["vf%d" % (t + 1)], ["vl%d" % (t + 1)], 12)
+            u2 = tile()
+            pe(lambda: [(P(u2)[:, 0:S], T.i32[:], X(T.pv), True, False), (P(u2)[:, 0:S], T.im[:], T.ones[:], False, False),
+                        (P(u2)[:, 0:S], T.ip[:], sg, False, True)], 6 * S, ["pv%d" % t, k("U1"), "i32", "ones", "im", "ip"], [k("U2")], u2)
+            pn = T.pv[:, S * t + S:S * t + 2 * S]
+            dv(lambda: V.tensor_tensor(pn, P(u2)[:, 0:S], X(T.ypb), A.max), [k("U2"), k("yp")], ["pv%d" % (t + 1)], S, u2)
+            dv(lambda: V.tensor_copy(T.pl[:, S * t + S:S * t + 2 * S], pn), ["pv%d" % (t + 1)], ["pl%d" % (t + 1)], S)
+        else:
+            dma("sp", T.yv[:], vn, ["vf3"], [], 6e3)
+            dma("sp", T.yx[:, B:B + S], nxt[:, O + B:O + B + S], ["new3"], [], 49e3)
+        ac(lambda: ACT.activation(X(T.lo), T.CE[:, 0:S], F.Sign, bias=9.5, scale=-1.0), ["CE0", "CE1", "CE2"], [k("lo")], S, "CE")
+        pe(lambda: [(T.M1[:, 0:S], T.i32[:], X(T.pv), True, False), (T.M1[:, 0:S], T.im[:], X(T.fl), False, False),
+                    (T.M1[:, 0:S], T.im[:], sg, False, False)], 6 * S, ["pv%d" % t, k("sg"), k("fl"), k("ce20"), "i32", "im"], ["UE"], "M1", "open")
+        pe(lambda: [(T.M1[:, 0:S], T.tr[:], X(T.lo), False, True)], S, ["UE", k("lo"), "tr"], ["UE2"], "M1", "close")
+        dv(lambda: ts(X(T.se), T.M1[:, 0:S], c1(CB), A.add, 0.0, A.max), ["UE", "UE2", "CB"], [k("se")], S, "M1")
+        pe(lambda: [(T.CE[:, 384:396], E(T.ebh, j), XJ(T.se, j), j == 0, j == 15) for j in range(16)], 1024, [k("se"), "ebh"], ["TL"], "CE")
+        if plan["dd"] == "v":
+            dv(lambda: V.tensor_copy(L(T.bc), T.CE[:, 384:396]), ["TL"], [k("bc")], 12, "CE")
+        dv(lambda: ts(L(T.tgl), T.CE[:, 384:396], 15.0, A.add), ["TL"], [k("tgl")], 12, "CE")
+        dv(lambda: V.tensor_tensor(X(T.vals), cwin.indirect(L(T.tgl)), X(T.ee), A.max), tk + [k("tgl"), k("ee")], [k("vals")], S * GAT)
+
+        def equal(hs, e0):
+            r = tile()
+            at = [sum(S - 16 * x for x in hs[:i]) for i in range(len(hs))]
+
+            def mms():
+                m = []
+                for h, a in zip(hs, at):
+                    m.append((P(r)[:, a:a + S - 16 * h], T.boh[:], T.se[:, S * t + 16 * h:S * t + S], True, False))
+                    m.append((P(r)[:, a:a + 16], T.idn[:], T.tm[:], False, True))
+                return m
+            pe(mms, sum(64 + max(64, S - 16 * h) for h in hs), [k("se"), "boh", "idn", "tm"], [k("KR%d" % hs[0])], r)
+            for h, a in zip(hs, at):
+                n = S - 16 * h
+                dv(lambda h=h, a=a, n=n: ts(eq[:, e0 + a:e0 + a + n], P(r)[:, a:a + n], T.bc[:, 12 * t + h:12 * t + h + 1], A.is_equal),
+                   [k("KR%d" % hs[0]), k("bc")], [k("eq%d" % h)], n, r)
+            return [(h, e0 + a) for h, a in zip(hs, at)]
+        if plan["dd"] == "v":
+            sets = [equal([0, 1, 3], 0), equal([2, 4, 5, 6, 11], 512), equal([7, 8, 9, 10], 1024)]
+            for i, st in enumerate(sets):
+                pe(lambda i=i, st=st: [(T.KB[:, S + 16 * h:2 * S], T.bok[:], eq[:, a:a + S - 16 * h], h == 0, h == 10) for h, a in st],
+                   sum(max(64, S - 16 * h) for h, a in st), [k("eq%d" % h) for h, a in st] + ["bok"] + (["DR%d" % (i - 1)] if i else []),
+                   ["DR%d" % i], "KB", ("open", "more", "close")[i])
+            ac(lambda: ACT.activation(X(T.du), T.KB[:, S:2 * S], F.Sigmoid, bias=-128.0, scale=1.0 / 16), ["DR0", "DR1", "DR2"], [k("du")], S, "KB")
+            pe(lambda: [(T.CE[:, 400:412], T.i32[:], L(T.bc), True, False)] +
+               [(T.CE[:, 400:412], E(T.ebn, j), XJ(T.du, j), False, j == 15) for j in range(16)],
+               1280, [k("du"), k("bc"), "ebn", "i32"], ["DL"], "CE")
+            dv(lambda: V.tensor_tensor(L(T.t2), T.CE[:, 400:412], T.prc[:], A.max), ["DL", "prc"], [k("t2")], 12, "CE")
+        else:
+            pe(lambda: [(T.KB[:, S:2 * S], T.idn[:], T.i8[:], True, False), (T.KB[:, S:2 * S], T.boh[:], X(T.se), False, True)],
+               2 * S, [k("se"), "boh", "idn", "i8"], ["DR0", "DR1", "DR2"], "KB")
+            ac(lambda: ACT.activation(L(T.nb), T.CE[:, 384:396], F.Identity, scale=-2097152.0), ["TL"], [k("nb")], 12, "CE")
+            dv(lambda: V.tensor_tensor(L(T.pre), T.CE[:, 384:396], T.prd[:], A.add), ["TL", "prd"], [k("pre")], 12, "CE")
+            for h in range(11, -1, -1):
+                n = 16 * h + 16
+                ac(lambda h=h, n=n: ACT.activation(T.ab[:, h, 0:n], T.KB[:, S:S + n], F.Abs, bias=T.nb[:, 12 * t + h:12 * t + h + 1],
+                                                   scale=2097152.0), ["DR0", k("nb")], ["ab%d" % h], n, "KB")
+                dv(lambda h=h, n=n: V.tensor_reduce(T.mm[:, 12 * t + h:12 * t + h + 1], T.ab[:, h, 0:n], AxisListType.X, A.min),
+                   ["ab%d" % h], [k("mm%d" % h)], n)
+            dv(lambda: V.tensor_tensor(L(T.t1), L(T.pre), L(T.mm), A.add), [k("pre")] + [k("mm%d" % h) for h in range(12)], [k("t1")], 24)
+            dv(lambda: V.tensor_tensor(L(T.t2), L(T.t1), T.prc[:], A.max), [k("t1"), "prc"], [k("t2")], 24)
+        dv(lambda: ts(L(T.off), L(T.t2), float(O - 1), A.add), [k("t2")], [k("off")], 12)
+        if t < 2:
+            send(t + 1, [(rep[t + 1][:, O + B:O + B + S], nxt[:, O + B:O + B + S]), (T.rvals[:, S * t:S * t + S], X(T.vals))],
+                 ["new%d" % (t + 1), k("vals")], ["rv%d" % (t + 1)], 98e3)
+            send(t + 1, [(T.roff[:, 12 * t:12 * t + 12], L(T.off))], [k("off")], ["ro%d" % (t + 1)], 3e3)
+        dv(lambda: V.tensor_copy(nxt[:, 0:O + B].indirect(L(T.off)), X(T.vals)),
+           ["tab%dc" % (t + 1), "sen1", k("off"), k("vals")], ["tab%d" % (t + 1)], S * SCA)
+        if t < 2 and "v" in PLAN[t + 1]["ho"]:
+            two = T["tac%d" % (t + 1)]
+            dma("sp", two[:, O:O + B], win, tk + ["pths"], ["tad%d" % t], 256 * B)
+            dma("sp", two[:, O + B:O + B + S], nxt[:, O + B:O + B + S], ["new%d" % (t + 1)], ["tan%d" % (t + 1)], 49e3)
+            dv(lambda: V.tensor_copy(two[:, 0:O + B].indirect(L(T.off)), X(T.vals)),
+               ["tad%d" % t, k("off"), k("vals")], ["tac%d" % (t + 1)], S * SCA)
+        if t == 2:
+            h = B // 2
+            dma("sp", T.yx[:, 0:h], nxt[:, O:O + h], ["tab3"], [], 256 * B)
+            dma("act", T.yx[:, h:B], nxt[:, O + h:O + B], ["tab3"], [], 256 * B)
+        gather(plan["xk"], xk, win, T.cl, tk + [k("cl")], "xk")
+        for u in range(3):
+            compare(u, xk, "xk", T.zz, k("zz"), cc, "cc", A.is_le, "CC")
+        ac(lambda: ACT.activation(X(T.fi), T.CC[:, 0:S], F.Sign, bias=c1(FB + t)), ["CC0", "CC1", "CC2", k("fb")], [k("fi")], S, "CC")
+        pe(lambda: [(T.M1[:, S:2 * S], T.i32[:], X(T.cf), True, False), (T.M1[:, S:2 * S], T.im[:], sg, False, False)],
+           5 * S, [k("cf"), k("sg"), "CC0", "CC1", "CC2", k("fb"), "i32", "im"], ["UC"], "M1", "open")
+        pe(lambda: [(T.M1[:, S:2 * S], T.tr[:], X(T.fi), False, True)], S, ["UC", k("fi"), "tr"], ["UC2"], "M1", "close")
+        dv(lambda: ts(X(T.sc), T.M1[:, S:2 * S], c1(CB), A.add, 0.0, A.max), ["UC", "UC2", "CB"], [k("sc")], S, "M1")
+        if t < 2:
+            pe(lambda: [(T.CC[:, 384:396], E(T.ebh, j), XJ(T.sc, j), j == 0, j == 15) for j in range(16)], 1024, [k("sc"), "ebh"], ["CL"], "CC")
+            dv(lambda: ts(T.covl[:, 80 + 12 * t:92 + 12 * t], T.CC[:, 384:396], 15.0, A.add), ["CL"], ["cvl%d" % t], 12, "CC")
+        pe(lambda: [(T.CC[0:8, S:2 * S], T.g8[:], X(T.sc), True, True)], S, [k("sc"), "g8"], ["CR"], "CC")
+        ac(lambda: ACT.activation(T.ycb[0:8, S * t:S * t + S], T.CC[0:8, S:2 * S], F.Identity, bias=-1.0), ["CR"], [k("yc")], S, "CC")
+        dma("sp", T.yc[:, S * t:S * t + S], T.ycb[0:8, S * t:S * t + S], [k("yc")], [], 6e3)
+
+    for t in range(RO):
+        one_round(t)
+    return ops
+
+
+def schedule(ops, given=None):
+    n = len(ops)
+    HOP, OWN, LOOK = EST["hop"], EST["own"], EST["look"]
+    lastw, readers = {}, {}
+    for i, o in enumerate(ops):
+        d = set()
+        for key in o["r"]:
+            d.add(lastw[key])
+        for key in o["w"]:
+            if key in lastw:
+                d.add(lastw[key])
+            d.update(readers.get(key, ()))
+        d.discard(i)
+        o["dep"] = d
+        for key in o["r"]:
+            readers.setdefault(key, []).append(i)
+        for key in o["w"]:
+            lastw[key] = i
+            readers[key] = []
+    succ = [[] for _ in range(n)]
+    for i, o in enumerate(ops):
+        for j in o["dep"]:
+            succ[j].append(i)
+    pr = [0.0] * n
+    for i in range(n - 1, -1, -1):
+        pr[i] = ops[i]["cost"] + ops[i]["lat"] + max([pr[j] + HOP for j in succ[i]] + [0.0])
+    if given is not None:
+        pr = given
+    fixed = [int(ORDER[0][i:i + 2], 36) for i in range(0, len(ORDER[0]), 2)]
+    left = [len(o["dep"]) for o in ops]
+    ready = [i for i in range(n) if left[i] == 0]
+    free = {}
+    lastb, lock = {}, set()
+    idle = list(POOL)
+    order = []
+    base = {}
+
+    def after(o, j):
+        p = ops[j]
+        same = p["eng"] == o["eng"] and p["sem"] is None
+        return p["end"] + ((0.0 if o["eng"] == "pe" else OWN) if same else HOP)
+
+    def bank_of(o):
+        b = o["bank"]
+        if isinstance(b, dict):
+            if b["b"] is not None:
+                return b["b"]
+            return min(idle, key=lambda q: ops[lastb[q]]["end"] if q in lastb else 0.0) if idle else "none"
+        return b
+
+    def when(i):
+        o = ops[i]
+        if i not in base:
+            base[i] = max([after(o, j) for j in o["dep"]] + [0.0])
+        b = bank_of(o)
+        if b in lastb and ops[lastb[b]]["eng"] != o["eng"]:
+            return max(base[i], after(o, lastb[b]))
+        return base[i]
+
+    while ready:
+        cand = [i for i in ready if bank_of(ops[i]) != "none" and
+                not (ops[i]["eng"] == "pe" and ops[i]["grp"] not in ("more", "close") and bank_of(ops[i]) in lock)]
+        if fixed:
+            cand = [fixed[len(order)]]
+        at = dict((i, max(when(i), free.get(ops[i]["eng"], 0.0))) for i in cand)
+        first = min(cand, key=lambda i: (at[i], -pr[i]))
+        e = ops[first]["eng"]
+        i = max([j for j in cand if ops[j]["eng"] == e and at[j] <= at[first] + LOOK], key=lambda j: (pr[j], -j))
+        o = ops[i]
+        o["start"] = at[i]
+        free[e] = at[i] + o["cost"]
+        o["end"] = free[e] + o["lat"]
+        b = bank_of(o)
+        if b is not None:
+            if isinstance(o["bank"], dict):
+                if o["bank"]["b"] is None:
+                    o["bank"]["b"] = b
+                    idle.remove(b)
+                o["bank"]["n"] -= 1
+                if o["bank"]["n"] == 0:
+                    idle.append(b)
+            if b in lastb and ops[lastb[b]]["eng"] != e:
+                o["dep"].add(lastb[b])
+            lastb[b] = i
+            if o["grp"] == "open":
+                lock.add(b)
+            if o["grp"] == "close":
+                lock.discard(b)
+        order.append(i)
+        ready.remove(i)
+        for j in succ[i]:
+            left[j] -= 1
+            if left[j] == 0:
+                ready.append(j)
+    return order
+
+
+def rank_program(g, core, T, topo):
+    rank = T.rank_of(core)
+    if rank is None:
+        return
+    ops = build(g, core, T, topo, rank)
+    order = schedule(ops)
+    queue = {"pe": g.tensor, "dve": g.vector, "act": g.scalar, "pool": g, "sp": g.sync}
+    know = dict((e, {}) for e in queue)
+    total = {}
+    for i in order:
+        o = ops[i]
+        e = o["eng"]
+        kn = know[e]
+        need = {}
+        for j in o["dep"]:
+            s, c = ops[j]["ev"]
+            if s not in need or need[s][0] < c:
+                need[s] = (c, ops[j])
+        for s, (c, p) in sorted(need.items(), key=lambda x: -x[1][1]["end"]):
+            if kn.get(s, 0) >= c or (e == "pe" and s == "pe"):
+                continue
+            queue[e].wait_ge(T.sem[s], c)
+            for s2, c2 in p["clock"].items():
+                if kn.get(s2, 0) < c2:
+                    kn[s2] = c2
+        ins = o["fn"]()
+        if o["loc"]:
+            total["sent"] = total.get("sent", 0) + o["loc"]
+            total[o["sem"]] = o["cnt"]
+            o["ev"] = (o["sem"], o["cnt"])
+            o["clock"] = {o["sem"]: o["cnt"]}
+            continue
+        if o["sem"] is not None:
+            ins[0].then_inc(T.sem[o["sem"]], 16)
+            total[o["sem"]] = 16
+            o["ev"] = (o["sem"], 16)
+        else:
+            for x in ins:
+                x.then_inc(T.sem[e], 1)
+            total[e] = total.get(e, 0) + len(ins)
+            o["ev"] = (e, total[e])
+        o["clock"] = dict(kn)
+        o["clock"][o["ev"][0]] = o["ev"][1]
+    for s in sorted(total):
+        if max(know[e].get(s, 0) for e in know) < total[s]:
+            (g.sync if s[1:].isdigit() and s[0] == "d" else g).wait_ge(T.sem[s], total[s])

@@ -1,11 +1,15 @@
 from concourse.bass import DstId, RemoteDMATransfer
-from concourse.mybir import AluOpType as A, AxisListType, ActivationFunctionType as F
+from concourse.mybir import AluOpType as A, ActivationFunctionType as F
 
 B0, S, RO, DA = 1280, 192, 3, 512
 JUMPS = [4, 1, 6]
-O = 208
-CW = 192
+O = 80
+CW = 64
 BS = [B0 + S * t for t in range(RO + 1)]
+BASE = 65536.0
+C = BASE + 256.5
+TW = 416
+MW = 208
 
 SCRATCH = {}
 
@@ -22,13 +26,13 @@ for _t in range(3):
         _sb("%s%d" % (_n, _t), [BS[_t]], "bfloat16")
     for _n in ("xp", "xk", "ce", "cc"):
         _sb("%s%d" % (_n, _t), [S * 16], "bfloat16")
-    _sb("eq%d" % _t, [1248], "bfloat16")
-_sb("tm", [16], "bfloat16")
-for _n in ("dd", "zz", "ee", "fl", "sg", "lo", "fi", "vals", "du", "hn"):
+    _sb("ex%d" % _t, [S * 4], "float32")
+    _sb("ptr%d" % _t, [TW], "float32")
+for _n in ("xh", "dd", "zz", "ee", "fl", "sg", "lo", "fi", "ax", "hl"):
     _sb(_n, [3 * S], "bfloat16")
-for _n in ("xh", "se", "sc"):
+for _n in ("se", "sc", "pv", "cf"):
     _sb(_n, [3 * S], "float16")
-for _n in ("pv", "cf", "ypb", "ycb"):
+for _n in ("ypb", "ycb"):
     _sb(_n, [3 * S], "float32")
 for _n in ("ci", "cj"):
     _sb(_n, [3 * S], "int32")
@@ -36,62 +40,71 @@ for _n in ("pl", "cl"):
     _sb(_n, [3 * S], "uint16")
 for _n in ("hi", "hj"):
     _sb(_n, [72], "int32")
-for _n in ("al", "ql", "tgl", "off", "vl"):
+for _n in ("al", "ql", "tgl", "vl"):
     _sb(_n, [36], "uint16")
-for _n in ("bc", "t2", "nw", "nb", "pre", "mm", "t1"):
+for _n in ("t1", "s36"):
     _sb(_n, [36], "float32")
-_sb("ab", [12, S], "float32")
-_sb("prd", [12], "float32")
-_sb("i8", [S], "bfloat16")
-_sb("vf", [48], "float32")
-_sb("covl", [104], "uint16")
-_sb("rvals", [2 * S], "bfloat16")
+_sb("nw", [36], "float16")
+_sb("off", [36], "uint16")
 _sb("roff", [24], "uint16")
+_sb("vf", [12], "float32")
+_sb("covl", [104], "uint16")
+_sb("msg", [3 * MW], "float16")
+_sb("rmsg", [2 * MW], "float16")
 _sb("acts", [DA], "bfloat16")
 _sb("pths", [B0], "int32")
 _sb("wt", [16], "int32")
-_sb("wa", [32], "int32")
-_sb("wf", [32], "float32")
+for _n in ("wa", "wb"):
+    _sb(_n, [17], "int32")
+_sb("wf", [17], "float32")
+_sb("kl", [8], "uint16")
 _sb("leafs", [12], "int32")
 _sb("covt", [5, 16], "int32")
 _sb("covm", [5, 32], "float32")
 _sb("covx", [5, 32], "float32")
 _sb("covs", [5, 16], "float32")
-_sb("isf", [S], "float32")
 _sb("pi", [8], "int32")
 _sb("col", [24], "float32")
 _sb("ai", [8], "int32")
-_sb("sl", [12], "float32")
-_sb("s16", [12], "float32")
-_sb("prc", [12], "float32")
-for _n in ("o32", "b1", "bo", "e32"):
-    _sb(_n, [144], "float32")
-for _t in (1, 2):
-    _sb("tac%d" % _t, [O + BS[_t]], "bfloat16")
-for _n in ("ta", "tc", "i32", "s32"):
-    _sb(_n, [128], "float32")
-for _n in ("bok", "idn", "ineg", "ip", "im", "tr", "wh", "wl"):
-    _sb(_n, [128], "bfloat16")
-_sb("boh", [128], "float16")
-for _n in ("eb", "ebn"):
+_sb("pk", [12], "int32")
+for _n in ("sl", "pa", "pb", "pc"):
+    _sb(_n, [12], "float32")
+_sb("own", [12], "uint16")
+for _n in ("b1", "bo", "eb", "ebn"):
     _sb(_n, [144], "bfloat16")
-for _n in ("ebh", "w0h", "w1h"):
+for _n in ("bok", "bon", "idn", "ineg", "i4p", "i4n", "ta", "tc", "tr", "sh", "warm"):
+    _sb(_n, [128], "bfloat16")
+_sb("wm", [128], "float16")
+for _n in ("w0h", "w1h"):
     _sb(_n, [144], "float16")
-_sb("g8", [8], "float16")
-for _n in ("is16", "ones"):
+_sb("g8", [8], "bfloat16")
+for _n in ("isf", "is16", "ones"):
     _sb(_n, [S], "bfloat16")
+for _n in ("mk", "d1", "ab", "run"):
+    _sb(_n, [4 * S], "bfloat16")
 _sb("cm", [512], "bfloat16")
 POOL = ["P0", "P1", "P2", "P3"]
 for _n in POOL + ["KB", "CE", "CC", "M1"]:
     SCRATCH[_n] = ("psum", [128, 512], "float32")
 
-NDMA = 36
-SEMAPHORES = ["pe", "dve", "act", "pool", "sent"] + ["d%d" % i for i in range(NDMA)] + ["a%d" % i for i in range(8)]
+NDMA = 30
+SEMAPHORES = ["pe", "dve", "act", "pool", "sent"] + ["d%d" % i for i in range(NDMA)] + ["a%d" % i for i in range(10)]
 
-EST = dict(cyc=1.04, pcy=0.55, gat=1.6, sca=3.8, hop=110.0, own=70.0, fv=60.0, fa=90.0, rlat=2500.0, rbw=55.0, look=120.0)
-PLAN = [dict(zip(("xp", "xk", "ce", "cc", "ho", "ee", "dd"), _p.split("/"))) for _p in
-        "vaavav/avaaav/avvvav/vavvaa/vvaa/a/a avavva/avavva/vvvaaa/vaavaa/vmav/a/a avaaav/vaaavv/aavvvv/aaavva/vaav/v/a".split()]
-ORDER = ["0a020c0m00030n050406080o0701090b180d0q0p0s0e0t0r0f1i1m1l0v0g2b0z2a2j100l2f2e121n132d1o0i142g2c0w1p1d2n2h172p0j112i152q2z0k320h162o331a2w0u30341e3519311c2x1b0x1g1q1f360y2r2y5m2l2m3j3i3l3k3s3g3h3x1r1s3m2s1t2t202u1z37432v2k1x4944381j453e461k471h1v4a213t26483y253u295n4b1u23223v1y3n24281w41273z4c3f3q4d39403o3a3b3w3p3c424e5u5p4j5q5s3r5v4f3d4i5w5r4k5x4g4h5t604l4m625y4p61644q4y664n4r4w4o5e63584x5j4u595f4s5z4v504z5c4t54515a55525b565365575d5g675h5i5l5k685o6i6u766a6j9o6k6z6v6r69706b6w6s717f726x736m6t6l6y6c7n6n6d7l6f7k6o6e6q747g7m757i7w6p7u7877807j7x7p7z797v81827r7h7a837o7q7t6g7b7c6h7s7d857e7y9t9s849r868l9v8d8k879u9w9x8m8b9y8e8h8f8n8c8g898i8o8a8j8r9p8s88a29c8pa9948t8q8y929z959l9a8z969d8u9ba79390978v8w91988x9g9e99aa9h9f9i9ja09ka39n9ma8a19qawb8abala5a4axatb1a6ayamb2aubhb3acazavb4adb0aeb5aoblboanafbkapagaqasbiaibmahbrb6bnc2bpb7btb9arc3bsbxc1babuc4bwbbbybjbcajbqbzakc5bdc6bec0bfdndockbvdrdqdtdsdvcjducle3bgcedwcmc7e4cndpcqc8coccc9crcpd1csczdyd2dbd0dxcte1cve5d7d9cwd3d8dzd5cudddccxd6cad4dfe6cydgdadedhe0e7didjdkcfe2cge9cbdmdle8cieaebcdecchedee"]
+EST = dict(cyc=0.86, pcy=0.43, gat=1.56, sca=3.8, hop=170.0, own=130.0, fv=10.0, fa=10.0, rlat=3000.0, rbw=50.0,
+           dlat=2200.0, dbw=220.0, push=100.0)
+PLAN = [{"pa": "w1 v3 v1 w3 a2 m3 a2 w1", "xk": "aaaaaa", "cc": "avvvaa", "hg": "aaaa", "ht": "vava", "one": "vvava"},
+        {"pa": "v2 a2 a2 v1 v4 v1 v4", "xk": "avaaaa", "cc": "avvvaa", "hg": "aava", "ht": "aaaa", "one": "avaav"},
+        {"pa": "v2 a2 v2 a1 a2 a1 v1 v4 v1", "xk": "aavaav", "cc": "avvvaa", "hg": "aava", "ht": "aaaa", "one": "aaava"}]
+FIRST = {}
+U16 = True
+
+ORDER = ["UE DA PT+ TL hj ee+ hi cl DB xp xh HL ee ex tls tb3+ al ql sg PT fb ch cf HC a dd zz hx UF ce new se vals KB hv+ pl cc EP hd tb ptr cj CE D t yp hd+ tgl sc vl ci hv LL tab+ UF+ Dcc pl+ ptr+ lo UC tls+ tb+ off run HC+ xk hj++ HC++ ab cl+ NL tab U sg+ TL+ NL++ ch+ lo+ cvl", "D fi- pv- dd Dce- run off NL U CL- se xh+ hi+ ch+ CC- vf- HL UC Dce zz UE+ ax- DA hj cj hx3 UE ql vals dd+ xh hx vl ex+ fl ch3 ro rep EP lo+ ex tgl Dcc vals+ al hi xp ce hd3 KB UF+ fb CL DB ab al+ t ax+ pl+ CE yp R- yc- fi LL xk hv3 PT+ cf se+ cc new ql+ cvl U+ TL+", "ab new tab zz vf- a- sc- CC- HL hx vf CR-- hd3 R fl cc ptr pv- cj cf ch3 sc t hv D hx3 ce tb3 ro rep xk DA DB CR EP KB xp tls CE ee sg cl ci- tgl off tb fi ax- CR- UC ci run Dce CC vl a LL hd yc- R- yc Dcc hv3 fb yp"]
+PLAN = [{"pa": "w4 m1 w4 m1 w2 m2 a2", "xk": "aaaaaa", "cc": "aaavaa", "hg": "aavv", "ht": "vaaa", "one": "vvvvv"}, {"pa": "a2 v2 a1 v4 v3 a1 v1 a1 v1", "xk": "vaaaaa", "cc": "aavvav", "hg": "aava", "ht": "aaaa", "one": "vvaaa"}, {"pa": "a1 v4 a1 a2 v3 v1 v2 m2", "xk": "aavaav", "cc": "aavvaa", "hg": "avaa", "ht": "aava", "one": "aaava"}]
+ORDER = ["off HL hv cl ce rep+ vals zz xh xp HC yp lo DA+ pl hx cl+ NL al cj hj vl EP ql hd tls dd+ run xp+ CC KB ee sc dd a ptr t+ ro+ hd3++ se+ tgl CL CE ex ab t xk++ ex++ se tb DB+ tgl+ HL+ hi PT pl+ TL UE sg tb3++ tls+ ch3+ rep++ ci vf UC fi tab PT+ DB al+ hj++ D ch ql+ cc hj+ ci+ CR pv Dcc fb HC+ UF cvl zz+ DA xk ch+ LL R UC+ hv3++ hd3+", "HL+ U- cc fl cj new ee+ xh ee ax hv ptr off ce fl+ UE cf- pv KB Dcc U hx hd NL hv3 hx3 ch+ lo sc ab ro+ al+ hi+ new- DB+ fb TL UF DA+ tb3 CE D EP cf+ yc+ ex cf vals Dcc+ LL Dce pl+ hi tls+ sg ax- yp run tb+ UF+ new+ CL xk hd+ R+ tab vf+ zz+ sg+ TL+", "sc EP tb- vf- Dce-- ptr yc-- ql vl- KB cvl- Dce ax run CC- xh fi- HC R- a- UE hx ch3 hx3 lo cc PT dd CR- se ci cj ce hv xp U t CE vl D cl yp CC CR tgl UC LL a yc- off fi tab vals fb NL ab"]
+PLAN = [{"pa": "a1 w1 w4 m1 m2 a2 v1 x2 w2", "xk": "avaava", "cc": "vaaaaa", "hg": "avav", "ht": "vaaa", "one": "avava"}, {"pa": "v1 a2 v2 a2 v4 v4 v1", "xk": "aavaaa", "cc": "vaaaav", "hg": "aava", "ht": "aaaa", "one": "vaavv"}, {"pa": "v1 a2 v4 v2 a2 a2 v2 v1", "xk": "aaaava", "cc": "vvaava", "hg": "aava", "ht": "avaa", "one": "avava"}]
+ORDER = ["al+ cj hl HC ee tls UE ax ab lo pv EP yp ci ex+ hi+ HL dd xh hv DB UF PT hj tgl TL+ al cc ql hi DA NL+ CR hd+ zz vals ch sg ce hd R+ hx xh+ cf D off pl run PT++ KB cj++ hd3+ t xp fl+ CL+ CE se cl+ a tab", "run R- tls vals hj off vl- HC tb- ce+ ex- ci UF zz+ TL- cl- rep fb- vf- fi- new- ch3 hv3 yc- cj se zz hv U- LL- Dce- xk- ax+ CC- ax DA cvl- ptr lo D+ tab pl hv3+ ptr- KB ce hx sc- ex+ fb hl cl+ tb3 tgl tb ql+ UC- xh+ UE+ CE hj+ t+ U Dcc- EP ch3+ DA+ DB+ HL xp D new ee hx3 hd3+ tab+ CC DB dd se+ fi+ fi HL+ tls+ xp+ hd+ ci+ off+ t ee+ ql CL- dd+ ch Dce rep+ TL+ ab+ sg CR ptr+ LL", "LL vl tb UC UC- new a- xk- ab- UE- hv CC CE cvl- hx3 KB cc- HC pl yp- U ch pv- fl sc NL-- CR sg Dcc- vf- cf- Dce vl- hl EP hx al hi PT- lo sc- xk vals NL UF Dcc tgl cf cc tb3 a yc- vf yp fb R run yc"]
+PLAN = [{"pa": "w3 a2 w3 w1 w1 m2 a2 a2", "xk": "aaavav", "cc": "aavvva", "hs": "16 32 32", "hg": "afafa", "ht": "aaaaa", "hn": "av", "one": "avava"}, {"pa": "v2 a2 v2 x2 a1 v2 v2 a1 v1 v1", "xk": "aavaaa", "cc": "vvaava", "hs": "20 20 20 20", "hg": "aaafv", "ht": "aaaav", "hn": "aa", "one": "vaaav"}, {"pa": "v3 a2 v1 a1 a1 a1 v1 a1 v1 v4", "xk": "avaaaa", "cc": "vvvaaa", "hs": "16 24 24 16", "hg": "faaav", "ht": "aaaaa", "hn": "av", "one": "vvaav"}]
+ORDER = ["ci+ ci xh ql ptr fb R++ HC tb+ Dce ee ex+ HL pl+ UC ce DA+ zz+ xp+ PT tb hl+ cj vl+ ch hl++ xp UC+ ptr+ UF DA ax hx UE ex zz hm+ ch+ tab hv HC+ hj+ UE+ hd+ hm NL D ab lo off hj new ql+ cl dd xh+ al hi pl vals+ LL tgl+ CL al+ vals hv+ hd++ hl run ab+ UF+ fl++ a Dcc++ fi cp yp tgl hk TL EP CE sc xk cvl hj++ fi+ se KB cc", "sg hn+ zz+ hd- hi+ U+ vl- off+ ptr+ ax Dce KB fl sg- D lo cp9 cf- cp9+ U- cp R Dcc- CC- ch9 se hk+ HL rep ab+ hi R- hx EP cj cl tab UE+ ch+ ee run lo+ TL hk ax+ CE hn DA+ CR+ pl+ run+ ce pv- tab+ off yp NL cp+ vals+ cvl xk CR- cl+ ee+ ci+ PT LL Dcc Dce+ fb vl+ sc+ hv9+ a CC HL+ dd+ CE+ D+ hv9 cc pv HC+", "al xh ch9 U- new ex yc-- fb fi cf- rep hx xp TL sg hv sc- hm ql ce PT UF CR- se NL UC cc cj KB new- CL- xk CC yc LL a EP tb cf tgl yc- dd- yp"]
 
 
 def build(g, core, T, topo, rank):
@@ -101,28 +114,30 @@ def build(g, core, T, topo, rank):
     V, ACT, PE = g.vector, g.scalar, g.tensor
     nd = [0]
     na = [0]
-    CYC, GAT, SCA = EST["cyc"], EST["gat"], EST["sca"]
+    now = [-1]
+    GAT, SCA = "gat", "sca"
 
-    def add(eng, fn, r, w, cost, bank=None, grp=None, lat=0.0, sem=None, cnt=0, loc=0):
-        o = dict(eng=eng, fn=fn, r=list(r), w=list(w), cost=cost, bank=bank, grp=grp, lat=lat, sem=sem, cnt=cnt, loc=loc)
+    def add(eng, fn, r, w, n, kind=None, bank=None, grp=None, sem=None, cnt=0, loc=0, calls=1):
+        o = dict(eng=eng, fn=fn, r=list(r), w=list(w), n=n, kind=kind, bank=bank, grp=grp, sem=sem, cnt=cnt, loc=loc, calls=calls,
+                 t=now[0])
         if isinstance(bank, dict):
-            bank["n"] += 1
+            bank["ops"].append(len(ops))
         ops.append(o)
 
-    def dv(fn, r, w, n, bank=None):
-        add("dve", lambda: [fn()], r, w, EST["fv"] + max(64, n) * CYC, bank)
+    def dv(fn, r, w, n, bank=None, kind=None):
+        add("dve", lambda: [fn()], r, w, n, kind, bank)
 
-    def ac(fn, r, w, n, bank=None):
-        add("act", lambda: [fn()], r, w, EST["fa"] + max(64, n) * CYC, bank)
+    def ac(fn, r, w, n, bank=None, kind=None):
+        add("act", lambda: [fn()], r, w, n, kind, bank)
 
     def pe(fn, cyc, r, w, bank, grp=None):
-        add("pe", lambda: [PE.matmul(*m) for m in fn()], r, w, cyc * EST["pcy"], bank, grp, lat=80.0)
+        add("pe", lambda: [PE.matmul(*m) for m in fn()], r, w, cyc, None, bank, grp)
 
     def po(fn, r, w, n):
-        add("pool", lambda: [fn()], r, w, 170 + 2 * n * CYC)
+        add("pool", lambda: [fn()], r, w, n)
 
     def tile():
-        return dict(n=0, b=None)
+        return dict(ops=[], b=None)
 
     def P(tl):
         return T[tl["b"]]
@@ -131,7 +146,7 @@ def build(g, core, T, topo, rank):
         s = "d%d" % nd[0]
         nd[0] += 1
         eng = g.sync if q == "sp" else g.scalar
-        add(q, lambda: [eng.dma_start(out, in_)], r, w, 80.0, lat=1700 + nbytes / 220.0, sem=s, cnt=16)
+        add(q, lambda: [eng.dma_start(out, in_)], r, w, nbytes, "dma", sem=s, cnt=16)
 
     def send(t, pairs, r, w, nbytes):
         dst = cores[(rank - JUMPS[t]) % N]
@@ -151,7 +166,7 @@ def build(g, core, T, topo, rank):
                                         remote_sem=T.sem[s], src=p[1], dst=p[0]) for i, p in enumerate(pairs)]
                 g.remote_dma_fused(tr, local_sem=T.sem.sent)
             return []
-        add("pool", fn, r, w, 500.0, lat=EST["rlat"] + nbytes / EST["rbw"], sem=s, cnt=len(topo.engines(src, core)), loc=len(en))
+        add("pool", fn, r, w, nbytes, "send", sem=s, cnt=len(topo.engines(src, core)), loc=len(en))
 
     def ts(out, in0, s1, op0, s2=None, op1=None):
         if op1 is None:
@@ -161,99 +176,100 @@ def build(g, core, T, topo, rank):
     def lin(out, in_, r, w, n, scale=1.0, bias=0.0, f=None):
         ac(lambda: ACT.activation(out, in_, f or F.Identity, bias=bias, scale=scale), r, w, n)
 
+    def fetch(e, out, window, r, w, n):
+        if e == "a":
+            ac(lambda: ACT.activation(out, window, F.Copy), r, w, n, kind=GAT)
+        else:
+            dv(lambda: V.tensor_copy(out, window), r, w, n, kind=GAT)
+
+    def scatter(window, offs, vals, r, w):
+        for h in (8, 4, 0):
+            dv(lambda h=h: V.tensor_copy(window.indirect(offs[:, h:h + 4]), vals[:, 16 * h:16 * h + 64]), r, w, 64, kind=SCA)
+
     tab = [T["tab%d" % t] for t in range(4)]
     rep = [T["rep%d" % t] for t in range(3)]
     col = T.col
     dma("sp", tab[0][:, O:O + B0], T.lab[:], [], ["tab0"], 330e3)
     dma("act", T.leafs[:], T.leaf[:], [], ["leafs"], 6e3)
     dma("act", T.wt[:], T.wts[:], [], ["wt"], 8e3)
-    for b in range(5):
-        dma("act" if b < 2 else "sp", T.covt[:, b, :], T.cov[:, 256 * b:256 * b + 256], [], ["covt%d" % b], 8e3)
-    if "v" in PLAN[0]["ho"][0:3]:
-        dma("act", tab[1][:, O:O + B0], T.lab[:], [], ["tab1c"], 500e3)
-    dma("sp", T.acts[:], T.act[:], [], ["acts"], 700e3)
+    dma("act", T.covt[:], T.cov[:], [], ["covt"], 200e3)
+    dma("sp", T.acts[:], T.act[:], [], ["acts"], 600e3)
     dma("sp", T.pths[:], T.pth[:], [], ["pths"], 1300e3)
-    if "v" not in PLAN[0]["ho"][0:3]:
-        dma("sp", tab[1][:, O:O + B0], T.lab[:], ["pths"], ["tab1c"], 330e3)
-    K, PO, PEV, CB, W0, W1, K0, YB, AC, FB = 0, 2, 3, 5, 6, 7, 11, 8, 12, 16
+    K, PO, PEV, K0, PP, YB, AC, FB = 0, 2, 3, 4, 5, 8, 12, 16
 
     def c1(i):
         return col[:, i:i + 1]
+    bo = T.bo[:, 0:128]
+    dv(lambda: V.memset(T.ones[:], 1.0), [], ["ones"], S / 2)
     po(lambda: g.iota(T.pi[:, 0:1], [[0, 1]], 0, 1), [], ["pi0"], 1)
-    po(lambda: g.iota(T.o32[:], [[0, 144]], 1, 0, allow_small_or_imprecise_dtypes=True), [], ["o32"], 144)
-    po(lambda: g.affine_select(T.b1[:], T.o32[:], [[-16, 9], [0, 16]], A.is_ge, 0.0, 0, 1), ["o32"], ["b1"], 144)
+    po(lambda: g.iota(T.s36[:], [[S, 3], [16, 12]], 0, 0, allow_small_or_imprecise_dtypes=True), [], ["s36"], 36)
+    po(lambda: g.affine_select(T.b1[:], T.ones[:, 0:144], [[-16, 9], [0, 16]], A.is_ge, 0.0, 0, 1), ["ones"], ["b1"], 144)
     po(lambda: g.affine_select(T.bo[:], T.b1[:], [[16, 9], [0, 16]], A.is_ge, 0.0, 15, -1), ["b1"], ["bo"], 144)
-    po(lambda: g.affine_select(T.e32[:], T.bo[:], [[0, 9], [1, 16]], A.is_equal, 0.0, -15, 0), ["bo"], ["e32"], 144)
-    po(lambda: g.affine_select(T.i32[:], T.o32[:, 0:128], [[1, 128]], A.is_equal, 0.0, 0, -1), ["o32"], ["i32"], 128)
-    po(lambda: g.affine_select(T.s32[:], T.bo[:, 0:128], [[1, 128]], A.is_equal, 0.0, -1, -1), ["bo"], ["s32"], 128)
-    po(lambda: g.affine_select(T.ta[:], T.bo[:, 0:128], [[1, 128]], A.is_ge, 0.0, 0, -1), ["bo"], ["ta"], 128)
+    po(lambda: g.affine_select(T.eb[:], T.bo[:], [[0, 9], [1, 16]], A.is_equal, 0.0, -15, 0), ["bo"], ["eb"], 144)
+    po(lambda: g.affine_select(T.idn[:], T.ones[:, 0:128], [[1, 128]], A.is_equal, 0.0, 0, -1), ["ones"], ["idn"], 128)
+    po(lambda: g.affine_select(T.sh[:], bo, [[1, 128]], A.is_equal, 0.0, -1, -1), ["bo"], ["sh"], 128)
+    po(lambda: g.affine_select(T.ta[:], bo, [[1, 128]], A.is_ge, 0.0, 0, -1), ["bo"], ["ta"], 128)
     po(lambda: g.affine_select(T.tc[:], T.ta[:], [[1, 128]], A.not_equal, -1.0, 0, -1), ["ta"], ["tc"], 128)
-    po(lambda: g.iota(T.s16[:], [[16, 12]], 0, 0, allow_small_or_imprecise_dtypes=True), [], ["s16"], 12)
     po(lambda: g.iota(T.isf[:], [[1, S]], 0, 0, allow_small_or_imprecise_dtypes=True), [], ["isf"], S)
-    dv(lambda: V.memset(tab[0][:, CW:O], 512.0), [], ["sen0"], 16)
-    dv(lambda: V.memset(tab[1][:, CW:O], 512.0), [], ["sen1"], 16)
+    for x in range(3):
+        po(lambda x=x: g.iota(T.ab[:, 256 * x:256 * x + 256], [[0, 4], [1, 64]], -48, 0, allow_small_or_imprecise_dtypes=True),
+           [], ["pidx%d" % x], 256)
+        po(lambda x=x: g.iota(T.run[:, 256 * x:256 * x + 256], [[16, 4], [0, 64]], 0, 0, allow_small_or_imprecise_dtypes=True),
+           [], ["spare%d" % x], 256)
+    for t in range(2):
+        dv(lambda t=t: V.memset(tab[t][:, 0:O], 512.0), [], ["sen%d" % t], 16)
     dv(lambda: V.memset(T.cm[:], -0.6875), [], ["cm"], 256)
     dv(lambda: ts(T.pi[:, 1:2], T.pi[:, 0:1], 15, A.bitwise_and), ["pi0"], ["pi1"], 1)
     dv(lambda: ts(T.pi[:, 2:3], T.pi[:, 0:1], 4, A.arith_shift_right, 1, A.bitwise_and), ["pi0"], ["pi2"], 1)
     dv(lambda: V.tensor_copy(c1(K), T.pi[:, 1:2]), ["pi1"], ["K"], 1)
     dv(lambda: V.tensor_copy(c1(PO), T.pi[:, 2:3]), ["pi2"], ["PO"], 1)
-    dv(lambda: ts(c1(PEV), T.pi[:, 2:3], -1.0, A.mult, 1.0, A.add), ["pi2"], ["PEV"], 1)
-    lin(c1(CB), c1(K), ["K"], ["CB"], 1, -2048.0, -4095.0)
+    lin(c1(PEV), c1(PO), ["PO"], ["PEV"], 1, -1.0, 1.0)
     lin(c1(K0), c1(K), ["K"], ["K0"], 1, -1.0, 1.0, F.Relu)
     for t in range(3):
-        lin(c1(YB + t), c1(K0), ["K0"], ["YB%d" % t], 1, float(BS[t]), -2048.0)
-    lin(T.bok[:], T.bo[:, 0:128], ["bo"], ["bok"], 128, 4096.0)
-    lin(T.eb[:], T.e32[:], ["e32"], ["eb"], 144)
-    lin(T.ebn[:], T.e32[:], ["e32"], ["ebn"], 144, -256.0)
-    lin(T.idn[:], T.i32[:], ["i32"], ["idn"], 128)
-    lin(T.ineg[:], T.i32[:], ["i32"], ["ineg"], 128, -1.0)
-    lin(T.ip[:], T.i32[:], ["i32"], ["ip"], 128, 2048.0)
-    lin(T.im[:], T.i32[:], ["i32"], ["im"], 128, -2048.0)
-    lin(T.tr[:], T.tc[:], ["tc"], ["tr"], 128, -2048.0)
+        lin(c1(YB + t), c1(K0), ["K0"], ["YB%d" % t], 1, float(BS[t]))
+    for name, src, scale in (("bok", "bo", 16384.0), ("bon", "bo", -4096.0), ("ineg", "idn", -1.0),
+                             ("i4p", "idn", 4096.0), ("i4n", "idn", -4096.0), ("tr", "tc", -4096.0)):
+        lin(T[name][:], T[src][:, 0:128], [src], [name], 128, scale)
+    lin(T.ebn[:], T.eb[:], ["eb"], ["ebn"], 144, -256.0)
     lin(T.is16[:], T.isf[:], ["isf"], ["is16"], S, 1.0 / 16)
-    add("act", lambda: [ACT.activation(T.ones[:, 0:144], T.o32[:], F.Sigmoid, scale=128.0)], ["o32"], ["ones0"], 1600.0)
-    lin(T.ones[:, 144:S], T.ones[:, 0:S - 144], ["ones0"], ["ones"], 48)
-    lin(T.sl[:], T.s16[:], ["s16", "K"], ["sl"], 12, 1.0, c1(K))
-    lin(T.prc[:], T.sl[:], ["sl"], ["prc"], 12, 1.0, float(1 - O))
-    if any(p["dd"] == "a" for p in PLAN):
-        lin(T.prd[:], T.sl[:], ["sl"], ["prd"], 12, -4096.0)
-        lin(T.i8[:], T.isf[:], ["isf"], ["i8"], S, 1.0 / 512)
-    for t in range(3):
-        lin(T.nw[:, 12 * t:12 * t + 12], T.sl[:], ["sl"], ["nw%d" % t], 12, 1.0, float(BS[t] - 4096))
-    dv(lambda: ts(T.tm[:], T.isf[:, 0:16], c1(K), A.is_le, -4096.0, A.mult), ["isf", "K"], ["tm"], 16)
-    dv(lambda: V.tensor_copy(T.boh[:], T.bo[:, 0:128]), ["bo"], ["boh"], 128)
-    dv(lambda: V.tensor_copy(T.ebh[:], T.eb[:]), ["eb"], ["ebh"], 72)
-    dv(lambda: V.tensor_copy(T.g8[:], T.bo[:, 0:128:16]), ["bo"], ["g8"], 8)
-    dv(lambda: ts(T.ai[:, 0:1], T.wt[:, 0:1], 8.0, A.mult, 2048.0, A.add), ["wt"], ["ai0"], 1)
-    dv(lambda: ts(T.ai[:, 1:2], T.wt[:, 1:2], 2048.0, A.add), ["wt"], ["ai1"], 1)
-    dv(lambda: ts(T.pi[:, 4:6], T.ai[:, 0:2], 4095, A.bitwise_and), ["ai0", "ai1"], ["pi4"], 2)
-    dv(lambda: ts(col[:, W0:W0 + 2], T.pi[:, 4:6], -2048.0, A.add), ["pi4"], ["W"], 2)
-    dv(lambda: ts(T.w0h[:], T.e32[:], c1(W0), A.mult), ["e32", "W"], ["w0h"], 144)
-    dv(lambda: ts(T.w1h[:], T.e32[:], c1(W1), A.mult), ["e32", "W"], ["w1h"], 144)
-    dv(lambda: ts(T.wa[:, 0:16], T.wt[:], 4032, A.bitwise_and), ["wt"], ["wa"], 16)
-    dv(lambda: ts(T.wa[:, 16:32], T.wt[:], 63, A.bitwise_and), ["wt"], ["wb"], 16)
-    dv(lambda: V.tensor_copy(T.wf[:], T.wa[:]), ["wa", "wb"], ["wf"], 32)
-    for j in range(8):
-        lin(T.wh[:, 16 * j:16 * j + 16], T.wf[:, 0:16], ["wf", "bo"], ["wh%d" % j], 16, T.bo[:, 16 * j:16 * j + 1])
-        lin(T.wl[:, 16 * j:16 * j + 16], T.wf[:, 16:32], ["wf", "bo"], ["wl%d" % j], 16, T.bo[:, 16 * j:16 * j + 1])
-    wk = ["wh%d" % j for j in range(8)] + ["wl%d" % j for j in range(8)]
-    ct = ["covt%d" % b for b in range(5)]
+    lin(T.g8[:], T.bo[:, 0:128:16], ["bo"], ["g8"], 8)
+    ac(lambda: ACT.activation(T.warm[:, 0:16], T.ones[:, 0:16], F.Sigmoid), ["ones"], ["warm"], 16, kind="first")
+    lin(T.sl[:], T.s36[:, 0:12], ["s36", "K"], ["sl"], 12, 1.0, c1(K))
+    dv(lambda: ts(T.nw[:], T.s36[:], c1(K), A.add, float(B0), A.add), ["s36", "K"], ["nw"], 36)
+    dv(lambda: ts(T.mk[:], T.ab[:], c1(K), A.is_ge, 4096.0, A.mult), ["pidx0", "pidx1", "pidx2", "K"], ["mk0", "ab0", "ab1"], 2 * S)
+    add("dve", lambda: [V.memset(T.mk[:, 64 * h:64 * h + 48 - 16 * h], 4096.0) for h in range(3)], ["mk0"], ["mk"], 192, calls=3)
+    dv(lambda: ts(T.d1[:], T.run[:], c1(K), A.add), ["spare0", "spare1", "spare2", "K"], ["d0", "run"], 2 * S)
+    dv(lambda: V.memset(T.d1[:, 63:4 * S:64], 4096.0), ["d0"], ["d1"], 12)
+    dv(lambda: V.tensor_tensor(T.pi[:, 3:4], T.pi[:, 0:1], T.pi[:, 2:3], A.add), ["pi0", "pi2"], ["pi3"], 1)
+    dv(lambda: ts(T.pi[:, 4:5], T.pi[:, 3:4], 1, A.bitwise_and), ["pi3"], ["pi4"], 1)
+    dv(lambda: ts(c1(PP), T.pi[:, 4:5], float(TW // 2), A.mult), ["pi4"], ["PP"], 1)
+    dv(lambda: ts(T.pk[:], T.sl[:], 1.0 / 12, A.mult, -5.5 / 12, A.add), ["sl"], ["pk"], 12)
+    dv(lambda: ts(T.pa[:], T.pk[:], float(1 - S), A.mult, c1(PP), A.add), ["pk", "PP"], ["pa"], 12)
+    lin(T.pb[:], T.sl[:], ["sl"], ["pb"], 12, 16.0)
+    dv(lambda: V.tensor_tensor(T.pc[:], T.pa[:], T.pb[:], A.add), ["pa", "pb"], ["pc"], 24)
+    dv(lambda: V.tensor_copy(T.own[:], T.pc[:]), ["pc"], ["perm"], 12)
+    dv(lambda: ts(T.wa[:, 0:16], T.wt[:], 2048.0, A.add), ["wt"], ["wa0"], 16)
+    dv(lambda: ts(T.wa[:, 16:17], T.wt[:, 0:1], 8.0, A.mult, 2048.0, A.add), ["wt"], ["wa1"], 1)
+    dv(lambda: ts(T.wb[:], T.wa[:], 4095, A.bitwise_and), ["wa0", "wa1"], ["wb"], 17)
+    dv(lambda: ts(T.wf[:], T.wb[:], -2048.0, A.add), ["wb"], ["wf"], 17)
+    dv(lambda: ts(T.w0h[:], T.eb[:], T.wf[:, 16:17], A.mult), ["eb", "wf"], ["w0h"], 72)
+    dv(lambda: ts(T.w1h[:], T.eb[:], T.wf[:, 1:2], A.mult), ["eb", "wf"], ["w1h"], 72)
+    dv(lambda: ts(T.kl[:], T.s36[:, 0:8], 0.0, A.mult, c1(K), A.add), ["s36", "K"], ["kl"], 8)
+    dv(lambda: V.tensor_tensor(T.wm[:], T.wf[:, 0:16].indirect(T.kl[:]), bo, A.mult), ["wf", "kl", "bo"], ["wm"], 128, kind=GAT)
+    ct = ["covt"]
     dv(lambda: ts(T.covm[:, :, 0:16], T.covt[:], 16.0, A.add, c1(PEV), A.mult), ct + ["PEV"], ["covm0"], 80)
     dv(lambda: ts(T.covm[:, :, 16:32], T.covt[:], 16.0, A.add, c1(PO), A.mult), ct + ["PO"], ["covm1"], 80)
-    for b in range(5):
-        dv(lambda b=b: V.transpose(T.covx[:, b, :], T.covm[:, b, :]), ["covm0", "covm1"], ["covx%d" % b], 32)
-    dv(lambda: V.tensor_tensor(T.covs[:], T.covx[:, :, 0:16], T.covx[:, :, 16:32], A.add),
-       ["covx%d" % b for b in range(5)], ["covs"], 160)
-    dv(lambda: V.tensor_copy(T.covl[:, 0:80], T.covs[:]), ["covs"], ["covl"], 80)
+    dv(lambda: V.transpose(T.covx[:], T.covm[:]), ["covm0", "covm1"], ["covx"], 160)
+    dv(lambda: V.tensor_tensor(T.covs[:], T.covx[:, :, 0:16], T.covx[:, :, 16:32], A.add), ["covx"], ["covs"], 160)
+    add("dve", lambda: [V.tensor_copy(T.covl[:, u:80:5], T.covs[:, u, :]) for u in range(5)], ["covs"], ["covl"], 64 * 5, calls=5)
     dv(lambda: V.tensor_copy(T.vl[:, 0:12], T.leafs[:]), ["leafs"], ["vl0"], 12)
-    dv(lambda: V.tensor_copy(T.vf[:, 0:12], T.leafs[:]), ["leafs"], ["vf0"], 12)
-    dv(lambda: V.tensor_copy(T.pv[:, 0:S], T.pths[:].indirect(T.vl[:, 0:12])), ["pths", "vl0"], ["pv0"], S * GAT)
-    dv(lambda: V.tensor_copy(T.pl[:, 0:S], T.pv[:, 0:S]), ["pv0"], ["pl0"], S)
+    dv(lambda: V.tensor_copy(T.pv[:, 0:S], T.pths[:].indirect(T.vl[:, 0:12])), ["pths", "vl0"], ["pv0"], S, kind=GAT)
 
     def E(buf, j):
         return buf[:, 15 - j:143 - j]
 
     def one_round(t):
+        now[0] = t
         B = BS[t]
         c = B // 64
         plan = PLAN[t]
@@ -265,236 +281,275 @@ def build(g, core, T, topo, rank):
         win = tab[t][:, O:O + B]
         cwin = tab[t][:, CW:O + B]
         nxt = tab[t + 1]
-        tb, ch, hx, xp, xk, ce, cc, eq = [T["%s%d" % (n, t)] for n in ("tb", "ch", "hx", "xp", "xk", "ce", "cc", "eq")]
+        tb, ch, hx, xp, xk, ce, cc, ex, ptr = [T["%s%d" % (n, t)] for n in ("tb", "ch", "hx", "xp", "xk", "ce", "cc", "ex", "ptr")]
         if t == 0:
             send(0, [(rep[0][:, O:O + B], win)], tk, ["rep0"], 256 * B)
-        if t < 2:
-            send(t + 1, [(rep[t + 1][:, O:O + B], win)], tk, ["repc%d" % (t + 1)], 256 * B * (2 if t == 0 else 1))
-        if t > 0:
-            dma("sp", nxt[:, CW:O + B], cwin, tk, ["tab%dc" % (t + 1)], 256 * B)
-        dv(lambda: V.tensor_copy(X(T.xh), win.indirect(L(T.vl))), tk + ["vl%d" % t], [k("xh")], S * GAT)
+            dma("sp", nxt[:, O:O + B], win, tk + ["rep0"], ["tab1c"], 256 * B)
+        else:
+            dma("sp", nxt[:, 0:O + B], tab[t][:, 0:O + B], tk, ["tab%dc" % (t + 1)], 256 * B)
+        pt = tile()
+        pe(lambda: [(P(pt)[:, a:a + n], T.idn[:], T.pv[:, S * t:S * t + n], True, True)
+                    for a, n in ((0, S), (S, 16), (TW // 2, S), (TW - 16, 16))], 2 * S + 128, ["pv%d" % t, "idn"], [k("PT")], pt)
+        dv(lambda: V.transpose(ptr[:], P(pt)[:, 0:TW]), [k("PT")], [k("ptr")], TW, pt)
+        dv(lambda: V.tensor_copy(X(T.pl), ptr[:].indirect(T.own[:])), [k("ptr"), "perm"], [k("pl")], S, kind=GAT)
+        fetch(plan["one"][0], X(T.xh), win.indirect(L(T.vl)), tk + ["vl%d" % t], [k("xh")], S)
         for h, wm in enumerate((T.w0h, T.w1h)):
-            pe(lambda h=h, wm=wm: [(T.M1[:, 384 + 12 * h:396 + 12 * h], E(wm, j), XJ(T.xh, j), j == 0, j == 15) for j in range(16)],
+            pe(lambda h=h, wm=wm: [(T.M1[:, 400 + 12 * h:412 + 12 * h], E(wm, j), XJ(T.xh, j), j == 0, j == 15) for j in range(16)],
                1024, [k("xh"), "w%dh" % h], ["HL%d" % h], "M1")
-        hi, hj = T.hi[:, 24 * t:24 * t + 24], T.hj[:, 24 * t:24 * t + 24]
-        dv(lambda: V.tensor_copy(hi, T.M1[:, 384:408]), ["HL0", "HL1"], [k("hi")], 24, "M1")
-        dv(lambda: ts(hj, hi, 4095, A.bitwise_and), [k("hi")], [k("hj")], 24)
+        for h, (a, b) in enumerate((("hi", "hj"), ("hk", "hm"))):
+            hi, hj = T.hi[:, 24 * t + 12 * h:24 * t + 12 * h + 12], T.hj[:, 24 * t + 12 * h:24 * t + 12 * h + 12]
+            dv(lambda h=h, hi=hi: V.tensor_copy(hi, T.M1[:, 400 + 12 * h:412 + 12 * h]), ["HL%d" % h], [k(a)], 12, "M1")
+            dv(lambda hi=hi, hj=hj: ts(hj, hi, 4095, A.bitwise_and), [k(a)], [k(b)], 12)
         dv(lambda: ts(L(T.al), T.hj[:, 24 * t:24 * t + 12], 0.125, A.mult), [k("hj")], [k("al")], 12)
-        dv(lambda: ts(L(T.ql), T.hj[:, 24 * t + 12:24 * t + 24], c / 64.0, A.mult, -63 / 128.0, A.add), [k("hj")], [k("ql")], 12)
+        dv(lambda: ts(L(T.ql), T.hj[:, 24 * t + 12:24 * t + 24], c / 64.0, A.mult, -63 / 128.0, A.add), [k("hm")], [k("ql")], 12)
 
         def hold(i, a, b):
             n = 16 * (b - a)
-            lk = ["covl"] if i < 3 else ["cvl%d" % u for u in range(t)]
+            eg, et = ("f", plan["hn"][0]) if i == 9 else (plan["hg"][i], plan["ht"][i])
+            lk = ["covl"] if i < 9 else ["cvl%d" % u for u in range(t)]
             lab = tab[t][:, O + 16 * a:O + 16 * b]
-            gat = cwin.indirect(T.covl[:, a:b])
-            if plan["ho"][i] == "v":
-                two, tw = (nxt, ["tab1c"]) if t == 0 else (T["tac%d" % t], ["tac%d" % t] + (["tan%d" % t] if i == 3 else []))
-                dv(lambda: V.tensor_tensor(ch[:, 16 * a:16 * b], gat, two[:, O + 16 * a:O + 16 * b], A.is_le),
-                   tk + lk + tw, [k("ch%d" % i)], n * GAT)
+            gat, mine, out = cwin.indirect(T.covl[:, a:b]), tb[:, 16 * a:16 * b], ch[:, 16 * a:16 * b]
+            if eg == "f":
+                if et == "a":
+                    ac(lambda: ACT.activation(mine, lab, F.Copy), tk, [k("cp%d" % i)], n)
+                else:
+                    dv(lambda: V.tensor_copy(mine, lab), tk, [k("cp%d" % i)], n / 2)
+                dv(lambda: V.tensor_tensor(out, gat, mine, A.is_le), tk + lk + [k("cp%d" % i)], [k("ch%d" % i)], n, kind=GAT)
             else:
-                ac(lambda: ACT.activation(hx[:, 16 * a:16 * b], gat, F.Copy), tk + lk, [k("hx%d" % i)], n * GAT)
+                fetch(eg, hx[:, 16 * a:16 * b], gat, tk + lk, [k("hx%d" % i)], n)
                 d = tile()
                 pe(lambda: [(P(d)[:, 0:n], T.idn[:], lab, True, False), (P(d)[:, 0:n], T.ineg[:], hx[:, 16 * a:16 * b], False, True)],
                    2 * n, [k("hx%d" % i), "idn", "ineg"], [k("hd%d" % i)], d)
-                if plan["ho"][i] == "a":
-                    ac(lambda: ACT.activation(ch[:, 16 * a:16 * b], P(d)[:, 0:n], F.Sigmoid, bias=128.0, scale=256.0),
-                       [k("hd%d" % i), "ones0"], [k("ch%d" % i)], n, d)
+                if et == "a":
+                    ac(lambda: ACT.activation(out, P(d)[:, 0:n], F.Sigmoid, bias=128.0, scale=256.0),
+                       [k("hd%d" % i), "warm"], [k("ch%d" % i)], n, d)
                 else:
-                    dv(lambda: ts(ch[:, 16 * a:16 * b], P(d)[:, 0:n], 0.0, A.is_ge), [k("hd%d" % i)], [k("ch%d" % i)], n, d)
+                    dv(lambda: ts(out, P(d)[:, 0:n], 0.0, A.is_ge), [k("hd%d" % i)], [k("ch%d" % i)], n, d)
             h = tile()
-            pe(lambda: [(P(h)[:, 0:n], T.bok[:], T.cm[:, 0:n], True, False), (P(h)[:, 0:n], T.bok[:], ch[:, 16 * a:16 * b], False, True)],
+            pe(lambda: [(P(h)[:, 0:n], T.bok[:], T.cm[:, 0:n], True, False), (P(h)[:, 0:n], T.bok[:], out, False, True)],
                2 * n, [k("ch%d" % i), "bok", "cm"], [k("hv%d" % i)], h)
-            if i < 3:
-                dv(lambda: V.tensor_tensor(tb[:, 16 * a:16 * b], P(h)[:, 0:n], lab, A.max), [k("hv%d" % i)], [k("tb%d" % i)], n, h)
+            if i < 9:
+                dv(lambda: V.tensor_tensor(mine, P(h)[:, 0:n], lab, A.max), [k("hv%d" % i)], [k("tb%d" % i)], n, h)
+            elif plan["hn"][1] == "a":
+                ac(lambda: ACT.activation(hx[:, B0:B], P(h)[:, 0:n], F.Sigmoid, bias=-128.0), [k("hv9"), "warm"], [k("hn")], n, h)
             else:
-                dma("sp", tb[:, B0:B], lab, tk, [k("tb3")], 256 * n)
-                ac(lambda: ACT.activation(T.hn[:, S * t - S:S * t - S + n], P(h)[:, 0:n], F.Relu), [k("hv3")], [k("hn")], n, h)
-        chunks = [(0, 32), (32, 64), (64, 80)] + ([(80, 80 + 12 * t)] if t else [])
-        for i, (a, b) in enumerate(chunks):
-            hold(i, a, b)
-        tbk = [k("tb%d" % i) for i in range(len(chunks))]
-        dv(lambda: V.tensor_tensor(X(T.dd), T.acts[:].indirect(L(T.al)), X(T.xh), A.subtract),
-           ["acts", k("al"), k("xh")], [k("dd")], S * GAT)
-        ac(lambda: ACT.activation(X(T.zz), X(T.dd), F.Abs), [k("dd")], [k("zz")], S)
+                dv(lambda: ts(hx[:, B0:B], P(h)[:, 0:n], 128.0, A.is_ge), [k("hv9")], [k("hn")], n, h)
+        a = 0
+        for i, n in enumerate(plan["hs"].split()):
+            hold(i, a, a + int(n))
+            a += int(n)
+        tbk = [k("tb%d" % j) for j in range(i + 1)]
+        if t:
+            hold(9, 80, 80 + 12 * t)
+        hn = [hx[:, B0 + S * u:B0 + S * u + S] for u in range(t)]
+        hk = [k("hn")] if t else []
+        if plan["one"][1] == "v":
+            dv(lambda: V.tensor_tensor(X(T.dd), T.acts[:].indirect(L(T.al)), X(T.xh), A.subtract),
+               ["acts", k("al"), k("xh")], [k("dd")], S, kind=GAT)
+            ac(lambda: ACT.activation(X(T.zz), X(T.dd), F.Abs), [k("dd")], [k("zz")], S)
+        else:
+            fetch("a", X(T.ax), T.acts[:].indirect(L(T.al)), ["acts", k("al")], [k("ax")], S)
+            dz = tile()
+            pe(lambda: [(P(dz)[:, 0:S], T.idn[:], X(T.xh), True, False), (P(dz)[:, 0:S], T.ineg[:], X(T.ax), False, True)],
+               2 * S, [k("ax"), k("xh"), "idn", "ineg"], [k("dd")], dz)
+            ac(lambda: ACT.activation(X(T.zz), P(dz)[:, 0:S], F.Abs), [k("dd")], [k("zz")], S, dz)
         hc = tile()
-        pe(lambda: [(P(hc)[:, 0:S], T.wh[:], X(T.zz), True, False), (P(hc)[:, 0:S], T.wl[:], X(T.zz), False, True)],
-           2 * S, [k("zz")] + wk, [k("HC")], hc)
+        pe(lambda: [(P(hc)[:, 0:S], T.wm[:], X(T.zz), True, True)], S, [k("zz"), "wm"], [k("HC")], hc)
         dv(lambda: V.tensor_copy(X(T.ci), P(hc)[:, 0:S]), [k("HC")], [k("ci")], S, hc)
         dv(lambda: ts(X(T.cj), X(T.ci), 4095, A.bitwise_and), [k("ci")], [k("cj")], S)
         dv(lambda: ts(X(T.cl), X(T.cj), c / 64.0, A.mult, -63 / 128.0, A.add), [k("cj")], [k("cl")], S)
-        dv(lambda: V.tensor_copy(X(T.cf), X(T.cl)), [k("cl")], [k("cf")], S)
+        dv(lambda: V.tensor_copy(X(T.cf), X(T.cl)), [k("cl")], [k("cf")], S / 2)
         rk = ["rep0"]
         if t > 0:
-            dv(lambda: V.tensor_copy(rep[t][:, 0:O + BS[t - 1]].indirect(T.roff[:, 12 * t - 12:12 * t]),
-                                     T.rvals[:, S * t - S:S * t]),
-               ["repc%d" % t, "rv%d" % t, "ro%d" % t], ["rep%d" % t], S * SCA)
-            rk = ["rep%d" % t, "rv%d" % t]
-        if plan["ee"] == "a":
-            ac(lambda: ACT.activation(X(T.ee), rep[t][:, O:O + B].indirect(L(T.ql)), F.Copy), rk + [k("ql")], [k("ee")], S * GAT)
+            got = T.rmsg[:, MW * t - MW:MW * t]
+            scatter(rep[t][:, 0:O + BS[t - 1]], T.roff[:, 12 * t - 12:12 * t], got, ["repc%d" % t, "rv%d" % t, "ro%d" % t], ["rep%d" % t])
+            rk = ["rep%d" % t, "rn%d" % t]
+        ans = rep[t][:, O:O + B].indirect(L(T.ql))
+        if plan["one"][2] == "a":
+            ac(lambda: ACT.activation(ex[:, 0:S], ans, F.Identity, bias=C, scale=-1.0), rk + [k("ql")], [k("ex1")], S, kind=GAT)
         else:
-            dv(lambda: V.tensor_copy(X(T.ee), rep[t][:, O:O + B].indirect(L(T.ql))), rk + [k("ql")], [k("ee")], S * GAT)
-        ac(lambda: ACT.activation(X(T.fl), X(T.ee), F.Relu, bias=-510.0, scale=2.0), [k("ee")], [k("fl")], S)
+            dv(lambda: ts(ex[:, 0:S], ans, -1.0, A.mult, C, A.add), rk + [k("ql")], [k("ex1")], S, kind=GAT)
+        lin(X(T.ee), ex[:, 0:S], [k("ex1")], [k("ee")], S, -1.0, C)
+        if t > 0:
+            lin(X(T.fl), ex[:, 0:S], [k("ex1")], [k("fl")], S, -1.0, C - 255, F.Relu)
+        pieces = [(p[0], int(p[1])) for p in plan["pa"].split()]
+        if any(e in "mw" for e, n in pieces):
+            ac(lambda: ACT.activation(T.M1[:, S:2 * S], ex[:, 0:S], F.Copy), [k("ex1")], ["EP"], S, "M1")
+        wide = max([n for e, n in pieces if e == "v"] + [0])
+        for n in (1, 2):
+            if wide > n and plan["one"][4] == "a":
+                lin(ex[:, n * S:2 * n * S], ex[:, 0:n * S], [k("ex%d" % n)], [k("ex%d" % (2 * n))], n * S)
+            elif wide > n:
+                po(lambda n=n: g.affine_select(ex[:, n * S:2 * n * S], ex[:, 0:n * S], [[0, n * S]], A.is_ge, 0.0, 0, 0),
+                   [k("ex%d" % n)], [k("ex%d" % (2 * n))], n * S)
+        if t < 2:
+            send(t + 1, [(rep[t + 1][:, O:O + B], win)], tk + ([] if t else tbk), ["repc%d" % (t + 1)], 256 * B)
 
-        def gather(engs, out, window, lst, r, key):
-            for i, e in enumerate(engs):
-                o, w = out[:, 512 * i:512 * i + 512], window.indirect(lst[:, S * t + 32 * i:S * t + 32 * i + 32])
-                if e == "a":
-                    ac(lambda o=o, w=w: ACT.activation(o, w, F.Copy), r, [k(key + str(i))], 512 * GAT)
-                else:
-                    dv(lambda o=o, w=w: V.tensor_copy(o, w), r, [k(key + str(i))], 512 * GAT)
+        done = dict(CE=0, KB=0)
 
-        def compare(u, src, sk, vec, vk, out, ok, op, bank):
+        def count(bank, k0, n, key):
+            def mms():
+                m = []
+                for p in range(k0, k0 + n):
+                    done[bank] += 1
+                    m.append((T[bank][:, 0:S], E(T.eb, p) if bank == "CE" else bo, ce[:, S * p:S * p + S],
+                              done[bank] == 1, done[bank] == 16))
+                return m
+            pe(mms, n * S, [key, "eb", "bo"], ["%s%d" % (bank, p) for p in range(k0, k0 + n)], bank)
+
+        def path(e, k0, n):
+            old = k0 >= t
+            gat = tb[:, 0:B0 if old else B].indirect(T.pl[:, S * t + 12 * k0:S * t + 12 * (k0 + n)])
+            r = tbk + [k("pl")] + ([] if old else [k("cp9")])
+            o = ce[:, S * k0:S * (k0 + n)]
+            key = k("ce%d" % k0)
+            if e == "v":
+                dv(lambda: V.tensor_tensor(o, gat, ex[:, 0:S * n], A.add), r + [k("ex%d" % (4 if n == 3 else n))], [key], S * n, kind=GAT)
+            elif e in "mw":
+                fetch("a" if e == "m" else "v", xp[:, S * k0:S * (k0 + n)], gat, r, [k("xp%d" % k0)], S * n)
+                for p in range(k0, k0 + n):
+                    dv(lambda p=p: V.tensor_tensor(ce[:, S * p:S * p + S], xp[:, S * p:S * p + S], T.M1[:, S:2 * S], A.add),
+                       [k("xp%d" % k0), "EP"], [k("ce%d" % p)], S, "M1")
+                    count("CE", p, 1, k("ce%d" % p))
+                return
+            else:
+                fetch("a" if e == "a" else "v", xp[:, S * k0:S * (k0 + n)], gat, r, [k("xp%d" % k0)], S * n)
+                d = tile()
+
+                def mms():
+                    m = []
+                    for p in range(n):
+                        m.append((P(d)[:, S * p:S * p + S], T.ineg[:], X(T.ee), True, False))
+                        m.append((P(d)[:, S * p:S * p + S], T.idn[:], xp[:, S * (k0 + p):S * (k0 + p + 1)], False, True))
+                    return m
+                pe(mms, 2 * S * n, [k("xp%d" % k0), k("ee"), "idn", "ineg"], ["D" + key], d)
+                ac(lambda: ACT.activation(o, P(d)[:, 0:S * n], F.Identity, bias=C), ["D" + key], [key], S * n, d)
+            count("CE", k0, n, key)
+        top = 16
+        for e, n in pieces:
+            top -= n
+            path(e, top, n)
+        cek = ["CE%d" % p for p in range(16)]
+        low, high = 16 * BASE + 9.5 * 512, 16 * BASE + 256 * 512
+        if plan["one"][3] == "a":
+            ac(lambda: ACT.activation(X(T.lo), T.CE[:, 0:S], F.Sigmoid, bias=low / 2, scale=-0.5), cek + ["warm"], [k("lo")], S, "CE")
+            ac(lambda: ACT.activation(X(T.hl), T.CE[:, 0:S], F.Sigmoid, bias=-high / 2, scale=0.5), cek + ["warm"], [k("hl")], S, "CE")
+        else:
+            dv(lambda: ts(X(T.lo), T.CE[:, 0:S], low, A.is_lt), cek, [k("lo")], S, "CE")
+            dv(lambda: ts(X(T.hl), T.CE[:, 0:S], high, A.is_ge), cek, [k("hl")], S, "CE")
+        sg = X(T.sg)
+        pe(lambda: [(T.KB[:, 0:S], T.idn[:], x, u == 0, False) for u, x in enumerate(hn)] + [(T.KB[:, 0:S], bo, X(T.hl), t == 0, True)],
+           S * (1 + t), [k("hl"), "bo", "idn"] + hk, ["KB"], "KB")
+        ac(lambda: ACT.activation(sg, T.KB[:, 0:S], F.Sigmoid, bias=-128.0, scale=256.0, accum_out=c1(AC + t)),
+           ["KB", "warm"], [k("sg")], S + 24, "KB")
+        dv(lambda: V.tensor_copy(T.ai[:, 2 + t:3 + t], c1(AC + t)), [k("sg")], [k("a1")], 1)
+        dv(lambda: ts(T.ai[:, 5 + t:6 + t], T.ai[:, 2 + t:3 + t], 1, A.bitwise_and), [k("a1")], [k("a2")], 1)
+        dv(lambda: ts(c1(FB + t), T.ai[:, 5 + t:6 + t], -256.0, A.mult, -2688.0, A.add), [k("a2")], [k("fb")], 1)
+        nl = tile()
+        pe(lambda: [(P(nl)[:, 0:S], T.idn[:], X(T.zz), True, False), (P(nl)[:, 0:S], T.i4p[:], sg, False, True)],
+           2 * S, [k("zz"), k("sg"), "idn", "i4p"], [k("NL")], nl)
+        dv(lambda: ts(nxt[:, O + B:O + B + S], P(nl)[:, 0:S], 256.0, A.min), [k("NL")], ["new%d" % (t + 1)], S, nl)
+        u1 = tile()
+        pe(lambda: [(P(u1)[:, 0:S], T.sh[:], X(T.pv), True, False), (P(u1)[:, 0:S], E(T.eb, 0), T.is16[:], False, False),
+                    (P(u1)[:, 0:S], T.i4n[:], sg, False, True)], 3 * S, ["pv%d" % t, k("sg"), "sh", "eb", "is16", "i4n"], [k("U1")], u1)
+        ac(lambda: ACT.activation(X(T.ypb), P(u1)[:, 0:S], F.Relu, bias=c1(YB + t)), [k("U1"), "YB%d" % t], [k("yp")], S, u1)
+        dma("sp", T.yp[:, S * t:S * t + S], X(T.ypb), [k("yp")], [], 98e3)
+        if t < 2:
+            u2 = tile()
+            pe(lambda: [(P(u2)[:, 0:S], T.idn[:], X(T.pv), True, False), (P(u2)[:, 0:S], T.i4n[:], T.ones[:], False, False),
+                        (P(u2)[:, 0:S], T.i4p[:], sg, False, True)], 3 * S, ["pv%d" % t, k("U1"), "idn", "ones", "i4n", "i4p"], [k("U2")], u2)
+            dv(lambda: V.tensor_tensor(T.pv[:, S * t + S:S * t + 2 * S], P(u2)[:, 0:S], X(T.ypb), A.max),
+               [k("U2"), k("yp")], ["pv%d" % (t + 1)], S, u2)
+        else:
+            dma("sp", T.yx[:, B:B + S], nxt[:, O + B:O + B + S], ["new3"], [], 49e3)
+        first = [(T.idn[:], X(T.pv))] + ([(T.i4n[:], X(T.fl))] if t else []) + [(T.i4n[:], x) for x in hn]
+        pe(lambda: [(T.M1[:, 0:S], a, b, i == 0, False) for i, (a, b) in enumerate(first)], S * len(first),
+           ["pv%d" % t, "idn", "i4n", k("hi"), k("hk")] + ([k("fl")] if t else []) + hk, ["UE"], "M1")
+        pe(lambda: [(T.M1[:, 0:S], T.tr[:], X(T.lo), False, False), (T.M1[:, 0:S], T.bon[:], X(T.hl), False, True)], 2 * S,
+           ["UE", k("lo"), k("hl"), "tr", "bon"], ["UF"], "M1")
+        dv(lambda: ts(X(T.se), T.M1[:, 0:S], O - 4096.0, A.add, 0.0, A.max), ["UE", "UF"], [k("se")], S, "M1")
+        pe(lambda: [(T.M1[:, 424:436], T.idn[:], L(T.nw), True, False)] +
+           [(T.M1[:, 424:436], E(T.ebn, j), XJ(T.sg, j), False, j == 15) for j in range(16)],
+           1088, ["UF", k("sg"), "ebn", "idn", "nw"], ["LL"], "M1")
+        vn = T.vl[:, 12 * t + 12:12 * t + 24] if t < 2 else T.vf[:]
+        dv(lambda: V.tensor_tensor(vn, T.M1[:, 424:436], L(T.vl), A.max), ["LL", "vl%d" % t], ["vl%d" % (t + 1)], 12, "M1")
+        if t == 2:
+            dma("sp", T.yv[:], vn, ["vl3"], [], 6e3)
+        tl = T.M1[:, 384:396]
+        pe(lambda: [(tl, E(T.eb, j), XJ(T.se, j), j == 0, j == 15) for j in range(16)], 1024, [k("se"), "eb"], ["TL"], "M1")
+        dv(lambda: V.tensor_tensor(L(T.tgl), tl, T.d1[:, 0:4 * S:64], A.max), ["TL", "d1"], [k("tgl")], 12, "M1")
+        vals, cols = T.msg[:, MW * t:MW * t + S], T.msg[:, MW * t + S:MW * t + S + 12]
+        dv(lambda: V.tensor_tensor(vals, tab[t][:, 0:O + B].indirect(L(T.tgl)), X(T.ee), A.max),
+           tk + [k("tgl"), k("ee")], [k("vals")], S, kind=GAT)
+        for x, (bank, keys) in enumerate((("CE", cek), ("KB", ["KB"]))):
+            hs = range(6 * x, 6 * x + 6)
+            pe(lambda x=x, bank=bank: [(T[bank][:, 0:2 * S], T.idn[:], T.mk[:, 2 * S * x:2 * S * x + 2 * S], True, False)], 2 * S,
+               ["idn", "mk"], [k("D%d" % x)] + keys, bank)
+            pe(lambda bank=bank, hs=hs: [(T[bank][:, 64 * (h % 6) + 48 - 16 * min(h, 3):64 * (h % 6) + 64], bo,
+                                          T.se[:, S * t + 16 * max(h - 3, 0):S * t + 16 * h + 16], False, h == hs[-1]) for h in hs],
+               384, ["TL", k("D%d" % x), k("se"), "bo"], [k("DA%d" % x)], bank)
+            add("dve", lambda bank=bank, hs=hs: [ts(T.ab[:, 64 * h:64 * h + 64], T[bank][:, 64 * (h % 6):64 * (h % 6) + 64], tl[:, h:h + 1],
+                                                    A.not_equal, 4096.0, A.mult) for h in hs],
+                ["TL", k("DA%d" % x)] + keys, ["ab%d" % x], 2 * S, bank="M1", calls=6)
+        dv(lambda: V.tensor_tensor_scan(T.run[:], T.ab[:], T.d1[:], 4096.0, A.min, A.max), ["ab0", "ab1", "d1"], ["run"], 2 * S)
+        off = L(T.off)
+        dv(lambda: V.tensor_tensor(off, T.run[:, 62:4 * S:64], L(T.tgl), A.min), ["run", k("tgl")], [k("off")], 24)
+        if t < 2:
+            send(t + 1, [(rep[t + 1][:, O + B:O + B + S], nxt[:, O + B:O + B + S])], ["new%d" % (t + 1)], ["rn%d" % (t + 1)], 49e3)
+            send(t + 1, [(T.rmsg[:, MW * t:MW * t + S], vals)], [k("vals")], ["rv%d" % (t + 1)], 49e3)
+            send(t + 1, [(L(T.roff), off)], [k("off")], ["ro%d" % (t + 1)], 3e3)
+        scatter(nxt[:, 0:O + B], off, vals, ["tab%dc" % (t + 1), "sen1", k("off"), k("vals")], ["tab%d" % (t + 1)])
+        if t == 2:
+            dma("sp", T.yx[:, 0:B], nxt[:, O:O + B], ["tab3"], [], 256 * B)
+
+        def compare(u):
             s0 = 64 * u
-            v = vec[:, S * t + s0:S * t + s0 + 64]
-            sks = [k(sk + str(2 * u)), k(sk + str(2 * u + 1))]
-            engs = plan[ok][2 * u:2 * u + 2]
-            ls, lv = (T.idn, T.ineg) if op == A.is_ge else (T.ineg, T.idn)
+            v = T.zz[:, S * t + s0:S * t + s0 + 64]
+            sks = [k("xk%d" % (2 * u)), k("xk%d" % (2 * u + 1))]
+            engs = plan["cc"][2 * u:2 * u + 2]
             if "v" in engs:
                 r8 = tile()
-                pe(lambda: [(P(r8)[:, j:512:8], T.idn[:], v, True, True) for j in range(8)], 512, [vk, "idn", sks[0]],
-                   [k("R%s%d" % (ok, u))], r8)
+                pe(lambda: [(P(r8)[:, j:512:8], T.idn[:], v, True, True) for j in range(8)], 512, [k("zz"), "idn", sks[0]],
+                   [k("R%d" % u)], r8)
 
             def half(h):
-                o = out[:, 1024 * u + h:1024 * u + 1024:2]
-                key = k("%s%d%d" % (ok, u, h))
+                o = cc[:, 1024 * u + h:1024 * u + 1024:2]
+                key = k("cc%d%d" % (u, h))
                 if engs[h] == "v":
-                    dv(lambda: V.tensor_tensor(o, src[:, 1024 * u + h:1024 * u + 1024:2], P(r8)[:], op),
-                       [k("R%s%d" % (ok, u))] + sks, [key], 512, r8)
+                    dv(lambda: V.tensor_tensor(o, xk[:, 1024 * u + h:1024 * u + 1024:2], P(r8)[:], A.is_le),
+                       [k("R%d" % u)] + sks, [key], 512, r8)
                 else:
                     d = tile()
 
                     def mms():
                         m = []
                         for j in range(8):
-                            m.append((P(d)[:, j:512:8], lv[:], v, True, False))
-                            m.append((P(d)[:, j:512:8], ls[:], src[:, 1024 * u + 2 * j + h:1024 * u + 1024:16], False, True))
+                            m.append((P(d)[:, j:512:8], T.idn[:], v, True, False))
+                            m.append((P(d)[:, j:512:8], T.ineg[:], xk[:, 1024 * u + 2 * j + h:1024 * u + 1024:16], False, True))
                         return m
-                    pe(mms, 1024, [vk, "idn", "ineg"] + sks, ["D" + key], d)
-                    ac(lambda: ACT.activation(o, P(d)[:], F.Sigmoid, bias=128.0, scale=256.0), ["D" + key, "ones0"], [key], 512, d)
+                    pe(mms, 1024, [k("zz"), "idn", "ineg"] + sks, ["D" + key], d)
+                    ac(lambda: ACT.activation(o, P(d)[:], F.Sigmoid, bias=128.0, scale=256.0), ["D" + key, "warm"], [key], 512, d)
             half(0)
             half(1)
-            pe(lambda: [(T[bank][:, s0:s0 + 64], E(T.eb, j), out[:, 1024 * u + j:1024 * u + 1024:16], j == 0, j == 15) for j in range(16)],
-               1024, [k("%s%d0" % (ok, u)), k("%s%d1" % (ok, u)), "eb"], ["%s%d" % (bank, u)], bank)
-
-        gather(plan["xp"], xp, tb[:], T.pl, tbk + ["pl%d" % t], "xp")
+            pe(lambda: [(T.CC[:, s0:s0 + 64], E(T.eb, j), cc[:, 1024 * u + j:1024 * u + 1024:16], j == 0, j == 15) for j in range(16)],
+               1024, [k("cc%d0" % u), k("cc%d1" % u), "eb"], ["CC%d" % u], "CC")
+        for i, e in enumerate(plan["xk"]):
+            fetch(e, xk[:, 512 * i:512 * i + 512], win.indirect(T.cl[:, S * t + 32 * i:S * t + 32 * i + 32]),
+                  tk + [k("cl")], [k("xk%d" % i)], 512)
         for u in range(3):
-            pe(lambda u=u: [(T.KB[:, 64 * u:64 * u + 64], T.bok[:], xp[:, 1024 * u + j:1024 * u + 1024:16], j == 0, j == 15 and t == 0) for j in range(16)] +
-               [(T.KB[:, 64 * u:64 * u + 64], T.bok[:], T.hn[:, S * (t - 1 + j) + 64 * u:S * (t - 1 + j) + 64 * u + 64], False, j == t - 1)
-                for j in range(t)],
-               1024 + 64 * t, [k("xp%d" % (2 * u)), k("xp%d" % (2 * u + 1)), "bok"] + ([k("hn")] if t else []), ["V%d" % u], "KB")
-            compare(u, xp, "xp", T.ee, k("ee"), ce, "ce", A.is_ge, "CE")
-        sg = X(T.sg)
-        ac(lambda: ACT.activation(sg, T.KB[:, 0:S], F.Sign, bias=-65400.5, scale=1.0 / 4096, accum_out=c1(AC + t)),
-           ["V0", "V1", "V2"], [k("sg")], S + 130, "KB")
-        dv(lambda: ts(T.ai[:, 2 + t:3 + t], c1(AC + t), 0.5, A.mult, 96.0, A.add), [k("sg")], [k("a1")], 1)
-        dv(lambda: ts(T.ai[:, 5 + t:6 + t], T.ai[:, 2 + t:3 + t], 1, A.bitwise_and), [k("a1")], [k("a2")], 1)
-        dv(lambda: ts(c1(FB + t), T.ai[:, 5 + t:6 + t], -1.0, A.mult, -10.5, A.add), [k("a2")], [k("fb")], 1)
-        nl = tile()
-        pe(lambda: [(P(nl)[:, 0:S], T.idn[:], X(T.zz), True, False), (P(nl)[:, 0:S], T.ip[:], sg, False, True)],
-           2 * S, [k("zz"), k("sg"), "idn", "ip"], [k("NL")], nl)
-        dv(lambda: ts(nxt[:, O + B:O + B + S], P(nl)[:, 0:S], 2048.0, A.add, 256.0, A.min), [k("NL")], ["new%d" % (t + 1)], S, nl)
-        pe(lambda: [(T.M1[:, 416:428], T.i32[:], L(T.nw), True, False)] +
-           [(T.M1[:, 416:428], E(T.ebn, j), XJ(T.sg, j), False, j == 15) for j in range(16)],
-           1280, [k("sg"), "ebn", "i32", "nw%d" % t], ["LL"], "M1")
-        vn = T.vf[:, 12 * t + 12:12 * t + 24]
-        dv(lambda: V.tensor_tensor(vn, T.M1[:, 416:428], L(T.vf), A.max), ["LL", "vf%d" % t], ["vf%d" % (t + 1)], 12, "M1")
-        u1 = tile()
-        pe(lambda: [(P(u1)[:, 0:S], T.s32[:], X(T.pv), True, False), (P(u1)[:, 0:S], E(T.eb, 0), T.is16[:], False, False),
-                    (P(u1)[:, 0:S], T.im[:], sg, False, True)], 6 * S, ["pv%d" % t, k("sg"), "s32", "eb", "is16", "im"], [k("U1")], u1)
-        ac(lambda: ACT.activation(X(T.ypb), P(u1)[:, 0:S], F.Relu, bias=c1(YB + t)), [k("U1"), "YB%d" % t], [k("yp")], S, u1)
-        dma("sp", T.yp[:, S * t:S * t + S], X(T.ypb), [k("yp")], [], 98e3)
+            compare(u)
+        ac(lambda: ACT.activation(X(T.fi), T.CC[:, 0:S], F.Sigmoid, bias=c1(FB + t), scale=256.0),
+           ["CC0", "CC1", "CC2", k("fb"), "warm"], [k("fi")], S, "CC")
+        pe(lambda: [(T.CC[:, S:2 * S], T.idn[:], X(T.cf), True, False), (T.CC[:, S:2 * S], T.i4n[:], sg, False, False),
+                    (T.CC[:, S:2 * S], T.tr[:], X(T.fi), False, True)],
+           3 * S, [k("cf"), k("sg"), k("fi"), "idn", "i4n", "tr"], ["UC"], "CC")
+        dv(lambda: ts(X(T.sc), T.CC[:, S:2 * S], -4095.0, A.add, 0.0, A.max), ["UC"], [k("sc")], S, "CC")
         if t < 2:
-            dv(lambda: V.tensor_copy(T.vl[:, 12 * t + 12:12 * t + 24], vn), ["vf%d" % (t + 1)], ["vl%d" % (t + 1)], 12)
-            u2 = tile()
-            pe(lambda: [(P(u2)[:, 0:S], T.i32[:], X(T.pv), True, False), (P(u2)[:, 0:S], T.im[:], T.ones[:], False, False),
-                        (P(u2)[:, 0:S], T.ip[:], sg, False, True)], 6 * S, ["pv%d" % t, k("U1"), "i32", "ones", "im", "ip"], [k("U2")], u2)
-            pn = T.pv[:, S * t + S:S * t + 2 * S]
-            dv(lambda: V.tensor_tensor(pn, P(u2)[:, 0:S], X(T.ypb), A.max), [k("U2"), k("yp")], ["pv%d" % (t + 1)], S, u2)
-            dv(lambda: V.tensor_copy(T.pl[:, S * t + S:S * t + 2 * S], pn), ["pv%d" % (t + 1)], ["pl%d" % (t + 1)], S)
-        else:
-            dma("sp", T.yv[:], vn, ["vf3"], [], 6e3)
-            dma("sp", T.yx[:, B:B + S], nxt[:, O + B:O + B + S], ["new3"], [], 49e3)
-        ac(lambda: ACT.activation(X(T.lo), T.CE[:, 0:S], F.Sign, bias=9.5, scale=-1.0), ["CE0", "CE1", "CE2"], [k("lo")], S, "CE")
-        pe(lambda: [(T.M1[:, 0:S], T.i32[:], X(T.pv), True, False), (T.M1[:, 0:S], T.im[:], X(T.fl), False, False),
-                    (T.M1[:, 0:S], T.im[:], sg, False, False)], 6 * S, ["pv%d" % t, k("sg"), k("fl"), k("ce20"), "i32", "im"], ["UE"], "M1", "open")
-        pe(lambda: [(T.M1[:, 0:S], T.tr[:], X(T.lo), False, True)], S, ["UE", k("lo"), "tr"], ["UE2"], "M1", "close")
-        dv(lambda: ts(X(T.se), T.M1[:, 0:S], c1(CB), A.add, 0.0, A.max), ["UE", "UE2", "CB"], [k("se")], S, "M1")
-        pe(lambda: [(T.CE[:, 384:396], E(T.ebh, j), XJ(T.se, j), j == 0, j == 15) for j in range(16)], 1024, [k("se"), "ebh"], ["TL"], "CE")
-        if plan["dd"] == "v":
-            dv(lambda: V.tensor_copy(L(T.bc), T.CE[:, 384:396]), ["TL"], [k("bc")], 12, "CE")
-        dv(lambda: ts(L(T.tgl), T.CE[:, 384:396], 15.0, A.add), ["TL"], [k("tgl")], 12, "CE")
-        dv(lambda: V.tensor_tensor(X(T.vals), cwin.indirect(L(T.tgl)), X(T.ee), A.max), tk + [k("tgl"), k("ee")], [k("vals")], S * GAT)
-
-        def equal(hs, e0):
-            r = tile()
-            at = [sum(S - 16 * x for x in hs[:i]) for i in range(len(hs))]
-
-            def mms():
-                m = []
-                for h, a in zip(hs, at):
-                    m.append((P(r)[:, a:a + S - 16 * h], T.boh[:], T.se[:, S * t + 16 * h:S * t + S], True, False))
-                    m.append((P(r)[:, a:a + 16], T.idn[:], T.tm[:], False, True))
-                return m
-            pe(mms, sum(64 + max(64, S - 16 * h) for h in hs), [k("se"), "boh", "idn", "tm"], [k("KR%d" % hs[0])], r)
-            for h, a in zip(hs, at):
-                n = S - 16 * h
-                dv(lambda h=h, a=a, n=n: ts(eq[:, e0 + a:e0 + a + n], P(r)[:, a:a + n], T.bc[:, 12 * t + h:12 * t + h + 1], A.is_equal),
-                   [k("KR%d" % hs[0]), k("bc")], [k("eq%d" % h)], n, r)
-            return [(h, e0 + a) for h, a in zip(hs, at)]
-        if plan["dd"] == "v":
-            sets = [equal([0, 1, 3], 0), equal([2, 4, 5, 6, 11], 512), equal([7, 8, 9, 10], 1024)]
-            for i, st in enumerate(sets):
-                pe(lambda i=i, st=st: [(T.KB[:, S + 16 * h:2 * S], T.bok[:], eq[:, a:a + S - 16 * h], h == 0, h == 10) for h, a in st],
-                   sum(max(64, S - 16 * h) for h, a in st), [k("eq%d" % h) for h, a in st] + ["bok"] + (["DR%d" % (i - 1)] if i else []),
-                   ["DR%d" % i], "KB", ("open", "more", "close")[i])
-            ac(lambda: ACT.activation(X(T.du), T.KB[:, S:2 * S], F.Sigmoid, bias=-128.0, scale=1.0 / 16), ["DR0", "DR1", "DR2"], [k("du")], S, "KB")
-            pe(lambda: [(T.CE[:, 400:412], T.i32[:], L(T.bc), True, False)] +
-               [(T.CE[:, 400:412], E(T.ebn, j), XJ(T.du, j), False, j == 15) for j in range(16)],
-               1280, [k("du"), k("bc"), "ebn", "i32"], ["DL"], "CE")
-            dv(lambda: V.tensor_tensor(L(T.t2), T.CE[:, 400:412], T.prc[:], A.max), ["DL", "prc"], [k("t2")], 12, "CE")
-        else:
-            pe(lambda: [(T.KB[:, S:2 * S], T.idn[:], T.i8[:], True, False), (T.KB[:, S:2 * S], T.boh[:], X(T.se), False, True)],
-               2 * S, [k("se"), "boh", "idn", "i8"], ["DR0", "DR1", "DR2"], "KB")
-            ac(lambda: ACT.activation(L(T.nb), T.CE[:, 384:396], F.Identity, scale=-2097152.0), ["TL"], [k("nb")], 12, "CE")
-            dv(lambda: V.tensor_tensor(L(T.pre), T.CE[:, 384:396], T.prd[:], A.add), ["TL", "prd"], [k("pre")], 12, "CE")
-            for h in range(11, -1, -1):
-                n = 16 * h + 16
-                ac(lambda h=h, n=n: ACT.activation(T.ab[:, h, 0:n], T.KB[:, S:S + n], F.Abs, bias=T.nb[:, 12 * t + h:12 * t + h + 1],
-                                                   scale=2097152.0), ["DR0", k("nb")], ["ab%d" % h], n, "KB")
-                dv(lambda h=h, n=n: V.tensor_reduce(T.mm[:, 12 * t + h:12 * t + h + 1], T.ab[:, h, 0:n], AxisListType.X, A.min),
-                   ["ab%d" % h], [k("mm%d" % h)], n)
-            dv(lambda: V.tensor_tensor(L(T.t1), L(T.pre), L(T.mm), A.add), [k("pre")] + [k("mm%d" % h) for h in range(12)], [k("t1")], 24)
-            dv(lambda: V.tensor_tensor(L(T.t2), L(T.t1), T.prc[:], A.max), [k("t1"), "prc"], [k("t2")], 24)
-        dv(lambda: ts(L(T.off), L(T.t2), float(O - 1), A.add), [k("t2")], [k("off")], 12)
-        if t < 2:
-            send(t + 1, [(rep[t + 1][:, O + B:O + B + S], nxt[:, O + B:O + B + S]), (T.rvals[:, S * t:S * t + S], X(T.vals))],
-                 ["new%d" % (t + 1), k("vals")], ["rv%d" % (t + 1)], 98e3)
-            send(t + 1, [(T.roff[:, 12 * t:12 * t + 12], L(T.off))], [k("off")], ["ro%d" % (t + 1)], 3e3)
-        dv(lambda: V.tensor_copy(nxt[:, 0:O + B].indirect(L(T.off)), X(T.vals)),
-           ["tab%dc" % (t + 1), "sen1", k("off"), k("vals")], ["tab%d" % (t + 1)], S * SCA)
-        if t < 2 and "v" in PLAN[t + 1]["ho"]:
-            two = T["tac%d" % (t + 1)]
-            dma("sp", two[:, O:O + B], win, tk + ["pths"], ["tad%d" % t], 256 * B)
-            dma("sp", two[:, O + B:O + B + S], nxt[:, O + B:O + B + S], ["new%d" % (t + 1)], ["tan%d" % (t + 1)], 49e3)
-            dv(lambda: V.tensor_copy(two[:, 0:O + B].indirect(L(T.off)), X(T.vals)),
-               ["tad%d" % t, k("off"), k("vals")], ["tac%d" % (t + 1)], S * SCA)
-        if t == 2:
-            h = B // 2
-            dma("sp", T.yx[:, 0:h], nxt[:, O:O + h], ["tab3"], [], 256 * B)
-            dma("act", T.yx[:, h:B], nxt[:, O + h:O + B], ["tab3"], [], 256 * B)
-        gather(plan["xk"], xk, win, T.cl, tk + [k("cl")], "xk")
-        for u in range(3):
-            compare(u, xk, "xk", T.zz, k("zz"), cc, "cc", A.is_le, "CC")
-        ac(lambda: ACT.activation(X(T.fi), T.CC[:, 0:S], F.Sign, bias=c1(FB + t)), ["CC0", "CC1", "CC2", k("fb")], [k("fi")], S, "CC")
-        pe(lambda: [(T.M1[:, S:2 * S], T.i32[:], X(T.cf), True, False), (T.M1[:, S:2 * S], T.im[:], sg, False, False)],
-           5 * S, [k("cf"), k("sg"), "CC0", "CC1", "CC2", k("fb"), "i32", "im"], ["UC"], "M1", "open")
-        pe(lambda: [(T.M1[:, S:2 * S], T.tr[:], X(T.fi), False, True)], S, ["UC", k("fi"), "tr"], ["UC2"], "M1", "close")
-        dv(lambda: ts(X(T.sc), T.M1[:, S:2 * S], c1(CB), A.add, 0.0, A.max), ["UC", "UC2", "CB"], [k("sc")], S, "M1")
-        if t < 2:
-            pe(lambda: [(T.CC[:, 384:396], E(T.ebh, j), XJ(T.sc, j), j == 0, j == 15) for j in range(16)], 1024, [k("sc"), "ebh"], ["CL"], "CC")
+            pe(lambda: [(T.CC[:, 384:396], E(T.eb, j), XJ(T.sc, j), j == 0, j == 15) for j in range(16)], 1024, [k("sc"), "eb"], ["CL"], "CC")
             dv(lambda: ts(T.covl[:, 80 + 12 * t:92 + 12 * t], T.CC[:, 384:396], 15.0, A.add), ["CL"], ["cvl%d" % t], 12, "CC")
-        pe(lambda: [(T.CC[0:8, S:2 * S], T.g8[:], X(T.sc), True, True)], S, [k("sc"), "g8"], ["CR"], "CC")
-        ac(lambda: ACT.activation(T.ycb[0:8, S * t:S * t + S], T.CC[0:8, S:2 * S], F.Identity, bias=-1.0), ["CR"], [k("yc")], S, "CC")
+        cr = tile()
+        pe(lambda: [(P(cr)[0:8, 0:S], T.g8[:], X(T.sc), True, True)], S, [k("sc"), "g8"], [k("CR")], cr)
+        ac(lambda: ACT.activation(T.ycb[0:8, S * t:S * t + S], P(cr)[0:8, 0:S], F.Identity, bias=-1.0), [k("CR")], [k("yc")], S, cr)
         dma("sp", T.yc[:, S * t:S * t + S], T.ycb[0:8, S * t:S * t + S], [k("yc")], [], 6e3)
 
     for t in range(RO):
@@ -502,11 +557,29 @@ def build(g, core, T, topo, rank):
     return ops
 
 
-def schedule(ops, given=None):
+def price(o, e):
+    n, kind, eng = o["n"], o["kind"], o["eng"]
+    if kind == "dma":
+        return 80.0, e["dlat"] + n / e["dbw"]
+    if kind == "send":
+        return 500.0, e["rlat"] + n / e["rbw"]
+    if eng == "pe":
+        return n * e["pcy"], 80.0
+    if eng == "pool":
+        return 170 + 2 * n * e["cyc"], 0.0
+    f = e["fv"] if eng == "dve" else e["fa"]
+    if kind == "first":
+        return 1400.0, 0.0
+    if kind is not None:
+        return (50.0 if eng == "dve" else 65.0) + n * e[kind] * e["cyc"], 0.0
+    return f * o["calls"] + max(64, n) * e["cyc"], 0.0
+
+
+def schedule(ops, est, fixed=None):
     n = len(ops)
-    HOP, OWN, LOOK = EST["hop"], EST["own"], EST["look"]
     lastw, readers = {}, {}
     for i, o in enumerate(ops):
+        o["cost"], o["lat"] = price(o, est)
         d = set()
         for key in o["r"]:
             d.add(lastw[key])
@@ -515,7 +588,7 @@ def schedule(ops, given=None):
                 d.add(lastw[key])
             d.update(readers.get(key, ()))
         d.discard(i)
-        o["dep"] = d
+        o["data"] = d
         for key in o["r"]:
             readers.setdefault(key, []).append(i)
         for key in o["w"]:
@@ -523,80 +596,132 @@ def schedule(ops, given=None):
             readers[key] = []
     succ = [[] for _ in range(n)]
     for i, o in enumerate(ops):
-        for j in o["dep"]:
+        for j in o["data"]:
             succ[j].append(i)
+    if fixed:
+        return replay(ops, est, *fixed)
     pr = [0.0] * n
     for i in range(n - 1, -1, -1):
-        pr[i] = ops[i]["cost"] + ops[i]["lat"] + max([pr[j] + HOP for j in succ[i]] + [0.0])
-    if given is not None:
-        pr = given
-    fixed = [int(ORDER[0][i:i + 2], 36) for i in range(0, len(ORDER[0]), 2)]
-    left = [len(o["dep"]) for o in ops]
-    ready = [i for i in range(n) if left[i] == 0]
-    free = {}
-    lastb, lock = {}, set()
-    idle = list(POOL)
-    order = []
-    base = {}
-
-    def after(o, j):
-        p = ops[j]
-        same = p["eng"] == o["eng"] and p["sem"] is None
-        return p["end"] + ((0.0 if o["eng"] == "pe" else OWN) if same else HOP)
-
-    def bank_of(o):
-        b = o["bank"]
-        if isinstance(b, dict):
-            if b["b"] is not None:
-                return b["b"]
-            return min(idle, key=lambda q: ops[lastb[q]]["end"] if q in lastb else 0.0) if idle else "none"
-        return b
-
-    def when(i):
+        pr[i] = ops[i]["cost"] + ops[i]["lat"] + max([pr[j] + est["hop"] for j in succ[i]] + [0.0])
+    rank = {}
+    for t, names in enumerate(ORDER):
+        for name in names.split():
+            rank[(name.strip("-+"), t - name.count("-") + name.count("+"))] = len(rank)
+    for i in range(n - 1, -1, -1):
         o = ops[i]
-        if i not in base:
-            base[i] = max([after(o, j) for j in o["dep"]] + [0.0])
-        b = bank_of(o)
-        if b in lastb and ops[lastb[b]]["eng"] != o["eng"]:
-            return max(base[i], after(o, lastb[b]))
-        return base[i]
+        if o["sem"]:
+            pr[i] = 1e6 - i
+        elif o["t"] < 0:
+            pr[i] = max(pr[j] for j in succ[i]) + 0.001
+        else:
+            name = o["w"][0].split("_")[0]
+            pr[i] = -rank.get((name, o["t"]), rank.get((name.rstrip("0123456789"), o["t"]))) - i / 1e4
+    return replay(ops, est, *place(ops, est, pr))
+
+
+def after(o, p, est):
+    same = p["eng"] == o["eng"] and p["sem"] is None
+    return p["end"] + ((0.0 if o["eng"] == "pe" else est["own"]) if same else est["hop"])
+
+
+def place(ops, est, pr):
+    HOP = est["hop"]
+    units = [[i] if not isinstance(o["bank"], dict) else o["bank"]["ops"] for i, o in enumerate(ops)]
+    units = [u for i, u in enumerate(units) if u[0] == i]
+    unit_of = dict((i, x) for x, u in enumerate(units) for i in u)
+    need = [set(unit_of[j] for i in u for j in ops[i]["data"]) - {x} for x, u in enumerate(units)]
+    users = [[] for _ in units]
+    for x, d in enumerate(need):
+        for y in d:
+            users[y].append(x)
+    left = [len(d) for d in need]
+    ready = [x for x in range(len(units)) if not left[x]]
+    taken = {}
+
+    def fit(i, at):
+        o = ops[i]
+        at = max([at] + [after(o, ops[j], est) for j in o["data"]])
+        while True:
+            was = at
+            mine = taken.setdefault(o["eng"], [])
+            lo, hi = 0, len(mine)
+            while lo < hi:
+                if mine[(lo + hi) // 2][0] < at - 1500.0:
+                    lo = (lo + hi) // 2 + 1
+                else:
+                    hi = (lo + hi) // 2
+            for a, b in mine[lo:]:
+                if at + max(o["cost"] - est["push"], 30.0) <= a:
+                    break
+                at = max(at, b)
+            if isinstance(o["bank"], str):
+                for a, b, e in taken.get(o["bank"], ()):
+                    if e != o["eng"] and at < b and a < at + o["cost"] + o["lat"] + HOP:
+                        at = b
+            if at == was:
+                break
+        o["start"], o["end"] = at, at + o["cost"] + o["lat"]
+        taken.setdefault(o["eng"], []).append((at, at + o["cost"]))
+        taken[o["eng"]].sort()
 
     while ready:
-        cand = [i for i in ready if bank_of(ops[i]) != "none" and
-                not (ops[i]["eng"] == "pe" and ops[i]["grp"] not in ("more", "close") and bank_of(ops[i]) in lock)]
-        if fixed:
-            cand = [fixed[len(order)]]
-        at = dict((i, max(when(i), free.get(ops[i]["eng"], 0.0))) for i in cand)
-        first = min(cand, key=lambda i: (at[i], -pr[i]))
-        e = ops[first]["eng"]
-        i = max([j for j in cand if ops[j]["eng"] == e and at[j] <= at[first] + LOOK], key=lambda j: (pr[j], -j))
-        o = ops[i]
-        o["start"] = at[i]
-        free[e] = at[i] + o["cost"]
-        o["end"] = free[e] + o["lat"]
-        b = bank_of(o)
+        x = max(ready, key=lambda x: (max(pr[i] for i in units[x]), -x))
+        u = units[x]
+        bank = ops[u[0]]["bank"]
+        at = 0.0
+        while True:
+            for i in u:
+                fit(i, at if i == u[0] else 0.0)
+            if not isinstance(bank, dict):
+                break
+            o = ops[u[0]]
+            mine = taken[o["eng"]]
+            mine.remove((o["start"], o["start"] + o["cost"]))
+            late = min(ops[i]["start"] for i in u[1:]) - HOP - o["lat"] - o["cost"]
+            for a, b in mine[::-1]:
+                if b <= late:
+                    break
+                late = min(late, a - o["cost"])
+            o["start"] = max(o["start"], late)
+            o["end"] = o["start"] + o["cost"] + o["lat"]
+            mine.append((o["start"], o["start"] + o["cost"]))
+            mine.sort()
+            a, b = o["start"], max(ops[i]["end"] for i in u) + HOP
+            clash = dict((q, max([y for w, y, e in taken.get(q, ()) if a < y and w < b] + [0.0])) for q in POOL)
+            q = min(POOL, key=lambda q: clash[q])
+            if not clash[q]:
+                bank["b"] = q
+                taken.setdefault(q, []).append((a, b, None))
+                break
+            for i in u:
+                taken[ops[i]["eng"]].remove((ops[i]["start"], ops[i]["start"] + ops[i]["cost"]))
+            at = min(y for q in POOL for w, y, e in taken.get(q, ()) if a < y and w < b)
+        if isinstance(bank, str):
+            taken.setdefault(bank, []).append((ops[u[0]]["start"], ops[u[0]]["end"] + HOP, ops[u[0]]["eng"]))
+            taken[bank].sort()
+        ready.remove(x)
+        for y in users[x]:
+            left[y] -= 1
+            if not left[y]:
+                ready.append(y)
+    return sorted(range(len(ops)), key=lambda i: ops[i]["start"]), [o["bank"]["b"] if isinstance(o["bank"], dict) else o["bank"] for o in ops]
+
+
+def replay(ops, est, order, banks):
+    free, lastb = {}, {}
+    for i in order:
+        o, b = ops[i], banks[i]
+        o["dep"] = set(o["data"])
+        if isinstance(o["bank"], dict):
+            o["bank"]["b"] = b
         if b is not None:
-            if isinstance(o["bank"], dict):
-                if o["bank"]["b"] is None:
-                    o["bank"]["b"] = b
-                    idle.remove(b)
-                o["bank"]["n"] -= 1
-                if o["bank"]["n"] == 0:
-                    idle.append(b)
-            if b in lastb and ops[lastb[b]]["eng"] != e:
+            if b in lastb and ops[lastb[b]]["eng"] != o["eng"]:
                 o["dep"].add(lastb[b])
             lastb[b] = i
-            if o["grp"] == "open":
-                lock.add(b)
-            if o["grp"] == "close":
-                lock.discard(b)
-        order.append(i)
-        ready.remove(i)
-        for j in succ[i]:
-            left[j] -= 1
-            if left[j] == 0:
-                ready.append(j)
-    return order
+        o["start"] = max([after(o, ops[j], est) for j in o["dep"]] + [free.get(o["eng"], 0.0)])
+        free[o["eng"]] = o["start"] + o["cost"]
+        o["end"] = free[o["eng"]] + o["lat"]
+    return order, banks
 
 
 def rank_program(g, core, T, topo):
@@ -604,7 +729,7 @@ def rank_program(g, core, T, topo):
     if rank is None:
         return
     ops = build(g, core, T, topo, rank)
-    order = schedule(ops)
+    order = schedule(ops, EST)[0]
     queue = {"pe": g.tensor, "dve": g.vector, "act": g.scalar, "pool": g, "sp": g.sync}
     know = dict((e, {}) for e in queue)
     total = {}

@@ -65,7 +65,8 @@ _sb("covx", [5, 32], "float32")
 _sb("covs", [5, 16], "float32")
 _sb("pi", [8], "int32")
 _sb("col", [24], "float32")
-_sb("ai", [8], "int32")
+_sb("even", [4], "bfloat16")
+_sb("neg", [36], "float32")
 _sb("pk", [12], "int32")
 for _n in ("sl", "pa", "pb", "pc"):
     _sb(_n, [12], "float32")
@@ -88,10 +89,13 @@ for _n in POOL + ["KB", "CE", "CC", "M1"]:
     SCRATCH[_n] = ("psum", [128, 512], "float32")
 
 NDMA = 30
-SEMAPHORES = ["pe", "dve", "act", "pool", "sent"] + ["d%d" % i for i in range(NDMA)] + ["a%d" % i for i in range(10)]
+SEMAPHORES = ["pe", "dve", "act", "pool", "sent"] + ["d%d" % i for i in range(NDMA)] + ["a%d" % i for i in range(12)]
+PARTS = 2
 
-EST = dict(cyc=0.86, pcy=0.43, gat=1.56, sca=3.8, hop=170.0, own=130.0, fv=10.0, fa=10.0, rlat=3000.0, rbw=50.0,
-           dlat=2200.0, dbw=220.0, push=100.0)
+EST = dict(cyc=0.86, pcy=0.43, gat=1.56, sca=3.8, hop=165.0, own=125.0, fv=22.0, fa=25.0, rlat=3000.0, rbw=50.0,
+           dlat=2200.0, dbw=220.0, push=100.0, steps=600)
+SETS = [{}, dict(cyc=0.83, pcy=0.42, hop=200.0, own=170.0, fv=0.0, fa=0.0, rlat=2600.0, rbw=65.0),
+        dict(cyc=1.18, pcy=0.6, gat=1.8, sca=5.0), dict(gat=1.3, hop=130.0, own=90.0, rlat=3600.0, rbw=38.0)]
 PLAN = [{"pa": "w1 v3 v1 w3 a2 m3 a2 w1", "xk": "aaaaaa", "cc": "avvvaa", "hg": "aaaa", "ht": "vava", "one": "vvava"},
         {"pa": "v2 a2 a2 v1 v4 v1 v4", "xk": "avaaaa", "cc": "avvvaa", "hg": "aava", "ht": "aaaa", "one": "avaav"},
         {"pa": "v2 a2 v2 a1 a2 a1 v1 v4 v1", "xk": "aavaav", "cc": "avvvaa", "hg": "aava", "ht": "aaaa", "one": "aaava"}]
@@ -105,6 +109,8 @@ PLAN = [{"pa": "a1 w1 w4 m1 m2 a2 v1 x2 w2", "xk": "avaava", "cc": "vaaaaa", "hg
 ORDER = ["al+ cj hl HC ee tls UE ax ab lo pv EP yp ci ex+ hi+ HL dd xh hv DB UF PT hj tgl TL+ al cc ql hi DA NL+ CR hd+ zz vals ch sg ce hd R+ hx xh+ cf D off pl run PT++ KB cj++ hd3+ t xp fl+ CL+ CE se cl+ a tab", "run R- tls vals hj off vl- HC tb- ce+ ex- ci UF zz+ TL- cl- rep fb- vf- fi- new- ch3 hv3 yc- cj se zz hv U- LL- Dce- xk- ax+ CC- ax DA cvl- ptr lo D+ tab pl hv3+ ptr- KB ce hx sc- ex+ fb hl cl+ tb3 tgl tb ql+ UC- xh+ UE+ CE hj+ t+ U Dcc- EP ch3+ DA+ DB+ HL xp D new ee hx3 hd3+ tab+ CC DB dd se+ fi+ fi HL+ tls+ xp+ hd+ ci+ off+ t ee+ ql CL- dd+ ch Dce rep+ TL+ ab+ sg CR ptr+ LL", "LL vl tb UC UC- new a- xk- ab- UE- hv CC CE cvl- hx3 KB cc- HC pl yp- U ch pv- fl sc NL-- CR sg Dcc- vf- cf- Dce vl- hl EP hx al hi PT- lo sc- xk vals NL UF Dcc tgl cf cc tb3 a yc- vf yp fb R run yc"]
 PLAN = [{"pa": "w3 a2 w3 w1 w1 m2 a2 a2", "xk": "aaavav", "cc": "aavvva", "hs": "16 32 32", "hg": "afafa", "ht": "aaaaa", "hn": "av", "one": "avava"}, {"pa": "v2 a2 v2 x2 a1 v2 v2 a1 v1 v1", "xk": "aavaaa", "cc": "vvaava", "hs": "20 20 20 20", "hg": "aaafv", "ht": "aaaav", "hn": "aa", "one": "vaaav"}, {"pa": "v3 a2 v1 a1 a1 a1 v1 a1 v1 v4", "xk": "avaaaa", "cc": "vvvaaa", "hs": "16 24 24 16", "hg": "faaav", "ht": "aaaaa", "hn": "av", "one": "vvaav"}]
 ORDER = ["ci+ ci xh ql ptr fb R++ HC tb+ Dce ee ex+ HL pl+ UC ce DA+ zz+ xp+ PT tb hl+ cj vl+ ch hl++ xp UC+ ptr+ UF DA ax hx UE ex zz hm+ ch+ tab hv HC+ hj+ UE+ hd+ hm NL D ab lo off hj new ql+ cl dd xh+ al hi pl vals+ LL tgl+ CL al+ vals hv+ hd++ hl run ab+ UF+ fl++ a Dcc++ fi cp yp tgl hk TL EP CE sc xk cvl hj++ fi+ se KB cc", "sg hn+ zz+ hd- hi+ U+ vl- off+ ptr+ ax Dce KB fl sg- D lo cp9 cf- cp9+ U- cp R Dcc- CC- ch9 se hk+ HL rep ab+ hi R- hx EP cj cl tab UE+ ch+ ee run lo+ TL hk ax+ CE hn DA+ CR+ pl+ run+ ce pv- tab+ off yp NL cp+ vals+ cvl xk CR- cl+ ee+ ci+ PT LL Dcc Dce+ fb vl+ sc+ hv9+ a CC HL+ dd+ CE+ D+ hv9 cc pv HC+", "al xh ch9 U- new ex yc-- fb fi cf- rep hx xp TL sg hv sc- hm ql ce PT UF CR- se NL UC cc cj KB new- CL- xk CC yc LL a EP tb cf tgl yc- dd- yp"]
+PLAN = [{"pa": "m1 m1 w2 w4 v1 v1 v2 a2 a2", "xk": "aaaava", "cc": "avvavv", "hs": "32 16 32", "hg": "avfff", "ht": "aavaa", "hn": "vv", "one": "aavav", "xs": "112221", "ab": "aa", "su": "1"}, {"pa": "x2 a2 v4 v4 a2 v2", "xk": "aaaava", "cc": "avaavv", "hs": "16 24 24 16", "hg": "aaaff", "ht": "aaava", "hn": "vv", "one": "aaaav", "xs": "112122", "ab": "av", "su": "2"}, {"pa": "a2 a2 a1 v1 v4 v3 a1 v2", "xk": "vvaaaa", "cc": "avvvaa", "hs": "16 24 24 16", "hg": "faaav", "ht": "vaaav", "hn": "aa", "one": "avaav", "xs": "121112", "ab": "va", "su": "3"}]
+ORDER = ["ex ce hj xh vals HC ax vl al se hi HL ch lo hv dd ql hx EP hl Dce run new sg EP+ CL cc run+ LL UC fl+ cj hd DA sc tgl hk ee hm ch9+ hv9+ hn+ UE tab fi cvl UF cl neg ql+ ex+ HL+ TL xp ptr xp+ tb U cp D vl+ hi+ cf hk+ UE+ ee+ KB ab Dce+ xh+ NL R CE rep+ CC fb pl xk zz+ hx+ off al+ cl+ tgl+ cj+ ci+ sg+ UF+ hv+ hd+ pv ax+ hn++ cp+ hm+ tb+ pl+ hj++ CE+ neg+ PT fi++ yp PT+ ptr+ UC++ sc++ ci Dcc hl+ HC+ rep++ EP++ ch+ lo+", "hv9+ hl+ UC ax+ ab se hj R+ DA ch9+ cp9 ce dd a- D yp pv HL+ zz- ql+ xh+ CR- tab off TL KB a ex+ cf vals hi+ new cvl LL zz+ sc xk cj+ ci+ ee+ hk+ fl+ R al+ lo+ a+ UE+ Dcc TL+ PT+ ptr+ pl+ CC dd+ off+ U U+", "fb- fi- cp9 ch cp UF hx se neg cc- run D DA ab yc-- ce CE tgl vals xp Dce xk NL- CC HC tab KB CR tb CL- hm cl yc fb hd sg cc cf yp Dcc yc- CR- NL LL vl hv new"]
 
 
 def build(g, core, T, topo, rank):
@@ -189,13 +195,15 @@ def build(g, core, T, topo, rank):
     tab = [T["tab%d" % t] for t in range(4)]
     rep = [T["rep%d" % t] for t in range(3)]
     col = T.col
-    dma("sp", tab[0][:, O:O + B0], T.lab[:], [], ["tab0"], 330e3)
+    parts = [(B0 * i // PARTS, B0 * (i + 1) // PARTS) for i in range(PARTS)]
+    for i, (a, b) in enumerate(parts):
+        dma("sp", tab[0][:, O + a:O + b], T.lab[:, a:b], [], ["lab%d" % i], 256 * b)
     dma("act", T.leafs[:], T.leaf[:], [], ["leafs"], 6e3)
     dma("act", T.wt[:], T.wts[:], [], ["wt"], 8e3)
     dma("act", T.covt[:], T.cov[:], [], ["covt"], 200e3)
     dma("sp", T.acts[:], T.act[:], [], ["acts"], 600e3)
     dma("sp", T.pths[:], T.pth[:], [], ["pths"], 1300e3)
-    K, PO, PEV, K0, PP, YB, AC, FB = 0, 2, 3, 4, 5, 8, 12, 16
+    K, PO, PEV, K0, PP, YB, AC, FB, PA = 0, 2, 3, 4, 5, 8, 12, 16, 20
 
     def c1(i):
         return col[:, i:i + 1]
@@ -238,7 +246,7 @@ def build(g, core, T, topo, rank):
     dv(lambda: ts(T.nw[:], T.s36[:], c1(K), A.add, float(B0), A.add), ["s36", "K"], ["nw"], 36)
     dv(lambda: ts(T.mk[:], T.ab[:], c1(K), A.is_ge, 4096.0, A.mult), ["pidx0", "pidx1", "pidx2", "K"], ["mk0", "ab0", "ab1"], 2 * S)
     add("dve", lambda: [V.memset(T.mk[:, 64 * h:64 * h + 48 - 16 * h], 4096.0) for h in range(3)], ["mk0"], ["mk"], 192, calls=3)
-    dv(lambda: ts(T.d1[:], T.run[:], c1(K), A.add), ["spare0", "spare1", "spare2", "K"], ["d0", "run"], 2 * S)
+    lin(T.d1[:], T.run[:], ["spare0", "spare1", "spare2", "K"], ["d0", "run"], 4 * S, 1.0, c1(K))
     dv(lambda: V.memset(T.d1[:, 63:4 * S:64], 4096.0), ["d0"], ["d1"], 12)
     dv(lambda: V.tensor_tensor(T.pi[:, 3:4], T.pi[:, 0:1], T.pi[:, 2:3], A.add), ["pi0", "pi2"], ["pi3"], 1)
     dv(lambda: ts(T.pi[:, 4:5], T.pi[:, 3:4], 1, A.bitwise_and), ["pi3"], ["pi4"], 1)
@@ -277,14 +285,15 @@ def build(g, core, T, topo, rank):
         X = lambda buf: buf[:, S * t:S * t + S]
         L = lambda buf: buf[:, 12 * t:12 * t + 12]
         XJ = lambda buf, j: buf[:, S * t + j:S * t + S:16]
-        tk = ["tab0", "sen0"] if t == 0 else ["tab%d" % t, "new%d" % t]
+        tk = ["lab%d" % i for i in range(PARTS)] + ["sen0"] if t == 0 else ["tab%d" % t, "new%d" % t]
         win = tab[t][:, O:O + B]
         cwin = tab[t][:, CW:O + B]
         nxt = tab[t + 1]
         tb, ch, hx, xp, xk, ce, cc, ex, ptr = [T["%s%d" % (n, t)] for n in ("tb", "ch", "hx", "xp", "xk", "ce", "cc", "ex", "ptr")]
         if t == 0:
-            send(0, [(rep[0][:, O:O + B], win)], tk, ["rep0"], 256 * B)
-            dma("sp", nxt[:, O:O + B], win, tk + ["rep0"], ["tab1c"], 256 * B)
+            for i, (a, b) in enumerate(parts):
+                send(0, [(rep[0][:, O + a:O + b], tab[0][:, O + a:O + b])], ["lab%d" % i], ["rp%d" % i], 256 * b - 58 * a)
+            dma("sp", nxt[:, O:O + B], win, tk + ["rp%d" % i for i in range(PARTS)], ["tab1c"], 256 * B)
         else:
             dma("sp", nxt[:, 0:O + B], tab[t][:, 0:O + B], tk, ["tab%dc" % (t + 1)], 256 * B)
         pt = tile()
@@ -318,16 +327,17 @@ def build(g, core, T, topo, rank):
             else:
                 fetch(eg, hx[:, 16 * a:16 * b], gat, tk + lk, [k("hx%d" % i)], n)
                 d = tile()
-                pe(lambda: [(P(d)[:, 0:n], T.idn[:], lab, True, False), (P(d)[:, 0:n], T.ineg[:], hx[:, 16 * a:16 * b], False, True)],
-                   2 * n, [k("hx%d" % i), "idn", "ineg"], [k("hd%d" % i)], d)
+                pe(lambda: [(P(d)[:, 0:n], T.idn[:], lab, True, False)], n, tk + ["idn"], [k("hd1%d" % i)], d)
+                pe(lambda: [(P(d)[:, 0:n], T.ineg[:], hx[:, 16 * a:16 * b], False, True)], n,
+                   [k("hd1%d" % i), k("hx%d" % i), "ineg"], [k("hd%d" % i)], d)
                 if et == "a":
                     ac(lambda: ACT.activation(out, P(d)[:, 0:n], F.Sigmoid, bias=128.0, scale=256.0),
                        [k("hd%d" % i), "warm"], [k("ch%d" % i)], n, d)
                 else:
                     dv(lambda: ts(out, P(d)[:, 0:n], 0.0, A.is_ge), [k("hd%d" % i)], [k("ch%d" % i)], n, d)
             h = tile()
-            pe(lambda: [(P(h)[:, 0:n], T.bok[:], T.cm[:, 0:n], True, False), (P(h)[:, 0:n], T.bok[:], out, False, True)],
-               2 * n, [k("ch%d" % i), "bok", "cm"], [k("hv%d" % i)], h)
+            pe(lambda: [(P(h)[:, 0:n], T.bok[:], T.cm[:, 0:n], True, False)], n, ["bok", "cm"], [k("hv1%d" % i)], h)
+            pe(lambda: [(P(h)[:, 0:n], T.bok[:], out, False, True)], n, [k("hv1%d" % i), k("ch%d" % i)], [k("hv%d" % i)], h)
             if i < 9:
                 dv(lambda: V.tensor_tensor(mine, P(h)[:, 0:n], lab, A.max), [k("hv%d" % i)], [k("tb%d" % i)], n, h)
             elif plan["hn"][1] == "a":
@@ -359,7 +369,7 @@ def build(g, core, T, topo, rank):
         dv(lambda: ts(X(T.cj), X(T.ci), 4095, A.bitwise_and), [k("ci")], [k("cj")], S)
         dv(lambda: ts(X(T.cl), X(T.cj), c / 64.0, A.mult, -63 / 128.0, A.add), [k("cj")], [k("cl")], S)
         dv(lambda: V.tensor_copy(X(T.cf), X(T.cl)), [k("cl")], [k("cf")], S / 2)
-        rk = ["rep0"]
+        rk = ["rp%d" % i for i in range(PARTS)]
         if t > 0:
             got = T.rmsg[:, MW * t - MW:MW * t]
             scatter(rep[t][:, 0:O + BS[t - 1]], T.roff[:, 12 * t - 12:12 * t], got, ["repc%d" % t, "rv%d" % t, "ro%d" % t], ["rep%d" % t])
@@ -442,9 +452,9 @@ def build(g, core, T, topo, rank):
            S * (1 + t), [k("hl"), "bo", "idn"] + hk, ["KB"], "KB")
         ac(lambda: ACT.activation(sg, T.KB[:, 0:S], F.Sigmoid, bias=-128.0, scale=256.0, accum_out=c1(AC + t)),
            ["KB", "warm"], [k("sg")], S + 24, "KB")
-        dv(lambda: V.tensor_copy(T.ai[:, 2 + t:3 + t], c1(AC + t)), [k("sg")], [k("a1")], 1)
-        dv(lambda: ts(T.ai[:, 5 + t:6 + t], T.ai[:, 2 + t:3 + t], 1, A.bitwise_and), [k("a1")], [k("a2")], 1)
-        dv(lambda: ts(c1(FB + t), T.ai[:, 5 + t:6 + t], -256.0, A.mult, -2688.0, A.add), [k("a2")], [k("fb")], 1)
+        lin(T.even[:, t:t + 1], c1(AC + t), [k("sg")], [k("a1")], 1, 1.0, 257.5)
+        lin(c1(PA + t), c1(AC + t), [k("a1")], [k("a2")], 1, -1.0, T.even[:, t:t + 1])
+        lin(c1(FB + t), c1(PA + t), [k("a2")], [k("fb")], 1, 256.0, -68736.0)
         nl = tile()
         pe(lambda: [(P(nl)[:, 0:S], T.idn[:], X(T.zz), True, False), (P(nl)[:, 0:S], T.i4p[:], sg, False, True)],
            2 * S, [k("zz"), k("sg"), "idn", "i4p"], [k("NL")], nl)
@@ -462,9 +472,11 @@ def build(g, core, T, topo, rank):
                [k("U2"), k("yp")], ["pv%d" % (t + 1)], S, u2)
         else:
             dma("sp", T.yx[:, B:B + S], nxt[:, O + B:O + B + S], ["new3"], [], 49e3)
-        first = [(T.idn[:], X(T.pv))] + ([(T.i4n[:], X(T.fl))] if t else []) + [(T.i4n[:], x) for x in hn]
+        first = [(T.idn[:], X(T.pv))] + ([(T.i4n[:], X(T.fl))] if t else [])
         pe(lambda: [(T.M1[:, 0:S], a, b, i == 0, False) for i, (a, b) in enumerate(first)], S * len(first),
-           ["pv%d" % t, "idn", "i4n", k("hi"), k("hk")] + ([k("fl")] if t else []) + hk, ["UE"], "M1")
+           ["pv%d" % t, "idn", "i4n", k("hi"), k("hk")] + ([k("fl")] if t else []), ["UE"], "M1")
+        if t:
+            pe(lambda: [(T.M1[:, 0:S], T.i4n[:], x, False, False) for x in hn], S * t, ["UE"] + hk, ["UE"], "M1")
         pe(lambda: [(T.M1[:, 0:S], T.tr[:], X(T.lo), False, False), (T.M1[:, 0:S], T.bon[:], X(T.hl), False, True)], 2 * S,
            ["UE", k("lo"), k("hl"), "tr", "bon"], ["UF"], "M1")
         dv(lambda: ts(X(T.se), T.M1[:, 0:S], O - 4096.0, A.add, 0.0, A.max), ["UE", "UF"], [k("se")], S, "M1")
@@ -488,6 +500,13 @@ def build(g, core, T, topo, rank):
             pe(lambda bank=bank, hs=hs: [(T[bank][:, 64 * (h % 6) + 48 - 16 * min(h, 3):64 * (h % 6) + 64], bo,
                                           T.se[:, S * t + 16 * max(h - 3, 0):S * t + 16 * h + 16], False, h == hs[-1]) for h in hs],
                384, ["TL", k("D%d" % x), k("se"), "bo"], [k("DA%d" % x)], bank)
+            if plan["ab"][x] == "a":
+                dv(lambda hs=hs: ts(T.neg[:, 12 * t + hs[0]:12 * t + hs[0] + 6], tl[:, hs[0]:hs[0] + 6], -4096.0, A.mult),
+                   ["TL"], [k("neg%d" % x)], 6, "M1")
+                add("act", lambda bank=bank, hs=hs: [ACT.activation(T.ab[:, 64 * h:64 * h + 64], T[bank][:, 64 * (h % 6):64 * (h % 6) + 64], F.Abs,
+                                                                    bias=T.neg[:, 12 * t + h:12 * t + h + 1], scale=4096.0) for h in hs],
+                    [k("neg%d" % x), k("DA%d" % x)] + keys, ["ab%d" % x], 2 * S, bank=bank, calls=6)
+                continue
             add("dve", lambda bank=bank, hs=hs: [ts(T.ab[:, 64 * h:64 * h + 64], T[bank][:, 64 * (h % 6):64 * (h % 6) + 64], tl[:, h:h + 1],
                                                     A.not_equal, 4096.0, A.mult) for h in hs],
                 ["TL", k("DA%d" % x)] + keys, ["ab%d" % x], 2 * S, bank="M1", calls=6)
@@ -505,7 +524,7 @@ def build(g, core, T, topo, rank):
         def compare(u):
             s0 = 64 * u
             v = T.zz[:, S * t + s0:S * t + s0 + 64]
-            sks = [k("xk%d" % (2 * u)), k("xk%d" % (2 * u + 1))]
+            sks = [k("xk%d" % (4 * u + x)) for x in range(4)]
             engs = plan["cc"][2 * u:2 * u + 2]
             if "v" in engs:
                 r8 = tile()
@@ -521,36 +540,48 @@ def build(g, core, T, topo, rank):
                 else:
                     d = tile()
 
-                    def mms():
+                    def mms(js):
                         m = []
-                        for j in range(8):
+                        for j in js:
                             m.append((P(d)[:, j:512:8], T.idn[:], v, True, False))
                             m.append((P(d)[:, j:512:8], T.ineg[:], xk[:, 1024 * u + 2 * j + h:1024 * u + 1024:16], False, True))
                         return m
-                    pe(mms, 1024, [k("zz"), "idn", "ineg"] + sks, ["D" + key], d)
-                    ac(lambda: ACT.activation(o, P(d)[:], F.Sigmoid, bias=128.0, scale=256.0), ["D" + key, "warm"], [key], 512, d)
+                    pe(lambda: mms(range(4)), 512, [k("zz"), "idn", "ineg"] + sks, ["D" + key], d)
+                    pe(lambda: mms(range(4, 8)), 512, ["D" + key], ["D9" + key], d)
+                    ac(lambda: ACT.activation(o, P(d)[:], F.Sigmoid, bias=128.0, scale=256.0), ["D9" + key, "warm"], [key], 512, d)
             half(0)
             half(1)
             pe(lambda: [(T.CC[:, s0:s0 + 64], E(T.eb, j), cc[:, 1024 * u + j:1024 * u + 1024:16], j == 0, j == 15) for j in range(16)],
                1024, [k("cc%d0" % u), k("cc%d1" % u), "eb"], ["CC%d" % u], "CC")
         for i, e in enumerate(plan["xk"]):
-            fetch(e, xk[:, 512 * i:512 * i + 512], win.indirect(T.cl[:, S * t + 32 * i:S * t + 32 * i + 32]),
-                  tk + [k("cl")], [k("xk%d" % i)], 512)
+            n = 32 // int(plan["xs"][i])
+            for a in range(32 * i, 32 * i + 32, n):
+                fetch(e, xk[:, 16 * a:16 * (a + n)], win.indirect(T.cl[:, S * t + a:S * t + a + n]),
+                      tk + [k("cl")], [k("xk%d" % (a // 16 + x)) for x in range(n // 16)], 16 * n)
         for u in range(3):
             compare(u)
-        ac(lambda: ACT.activation(X(T.fi), T.CC[:, 0:S], F.Sigmoid, bias=c1(FB + t), scale=256.0),
-           ["CC0", "CC1", "CC2", k("fb"), "warm"], [k("fi")], S, "CC")
-        pe(lambda: [(T.CC[:, S:2 * S], T.idn[:], X(T.cf), True, False), (T.CC[:, S:2 * S], T.i4n[:], sg, False, False),
-                    (T.CC[:, S:2 * S], T.tr[:], X(T.fi), False, True)],
-           3 * S, [k("cf"), k("sg"), k("fi"), "idn", "i4n", "tr"], ["UC"], "CC")
-        dv(lambda: ts(X(T.sc), T.CC[:, S:2 * S], -4095.0, A.add, 0.0, A.max), ["UC"], [k("sc")], S, "CC")
+        def choose(x, a, b):
+            n = 64 * (b - a)
+            Y = lambda buf: buf[:, S * t + 64 * a:S * t + 64 * b]
+            ac(lambda: ACT.activation(Y(T.fi), T.CC[:, 64 * a:64 * b], F.Sigmoid, bias=c1(FB + t), scale=256.0),
+               ["CC%d" % u for u in range(a, b)] + [k("fb"), "warm"], [k("fi%d" % x)], n, "CC")
+            uc = tile()
+            pe(lambda: [(P(uc)[:, 0:n], T.idn[:], Y(T.cf), True, False), (P(uc)[:, 0:n], T.i4n[:], Y(T.sg), False, False),
+                        (P(uc)[:, 0:n], T.tr[:], Y(T.fi), False, True)],
+               3 * n, [k("cf"), k("sg"), k("fi%d" % x), "idn", "i4n", "tr"], [k("UC%d" % x)], uc)
+            dv(lambda: ts(Y(T.sc), P(uc)[:, 0:n], -4095.0, A.add, 0.0, A.max), [k("UC%d" % x)], [k("sc%d" % x)], n, uc)
+            cr = tile()
+            pe(lambda: [(P(cr)[0:8, 0:n], T.g8[:], Y(T.sc), True, True)], n, [k("sc%d" % x), "g8"], [k("CR%d" % x)], cr)
+            ac(lambda: ACT.activation(T.ycb[0:8, S * t + 64 * a:S * t + 64 * b], P(cr)[0:8, 0:n], F.Identity, bias=-1.0),
+               [k("CR%d" % x)], [k("yc%d" % x)], n, cr)
+        cuts = {"1": (0, 3), "2": (0, 2, 3), "3": (0, 1, 2, 3)}[plan["su"]]
+        for x in range(len(cuts) - 1):
+            choose(x, cuts[x], cuts[x + 1])
         if t < 2:
-            pe(lambda: [(T.CC[:, 384:396], E(T.eb, j), XJ(T.sc, j), j == 0, j == 15) for j in range(16)], 1024, [k("sc"), "eb"], ["CL"], "CC")
+            pe(lambda: [(T.CC[:, 384:396], E(T.eb, j), XJ(T.sc, j), j == 0, j == 15) for j in range(16)], 1024,
+               [k("sc%d" % x) for x in range(len(cuts) - 1)] + ["eb"], ["CL"], "CC")
             dv(lambda: ts(T.covl[:, 80 + 12 * t:92 + 12 * t], T.CC[:, 384:396], 15.0, A.add), ["CL"], ["cvl%d" % t], 12, "CC")
-        cr = tile()
-        pe(lambda: [(P(cr)[0:8, 0:S], T.g8[:], X(T.sc), True, True)], S, [k("sc"), "g8"], [k("CR")], cr)
-        ac(lambda: ACT.activation(T.ycb[0:8, S * t:S * t + S], P(cr)[0:8, 0:S], F.Identity, bias=-1.0), [k("CR")], [k("yc")], S, cr)
-        dma("sp", T.yc[:, S * t:S * t + S], T.ycb[0:8, S * t:S * t + S], [k("yc")], [], 6e3)
+        dma("sp", T.yc[:, S * t:S * t + S], T.ycb[0:8, S * t:S * t + S], [k("yc%d" % x) for x in range(len(cuts) - 1)], [], 6e3)
 
     for t in range(RO):
         one_round(t)
@@ -614,14 +645,14 @@ def schedule(ops, est, fixed=None):
         elif o["t"] < 0:
             pr[i] = max(pr[j] for j in succ[i]) + 0.001
         else:
-            name = o["w"][0].split("_")[0]
+            name = o["w"][0].split("_")[0].replace("D9", "D").replace("hv19", "hv9")
             pr[i] = -rank.get((name, o["t"]), rank.get((name.rstrip("0123456789"), o["t"]))) - i / 1e4
     return replay(ops, est, *place(ops, est, pr))
 
 
 def after(o, p, est):
     same = p["eng"] == o["eng"] and p["sem"] is None
-    return p["end"] + ((0.0 if o["eng"] == "pe" else est["own"]) if same else est["hop"])
+    return p["end"] + ((-p["lat"] if o["eng"] == "pe" else est["own"]) if same else est["hop"])
 
 
 def place(ops, est, pr):
@@ -677,7 +708,7 @@ def place(ops, est, pr):
             o = ops[u[0]]
             mine = taken[o["eng"]]
             mine.remove((o["start"], o["start"] + o["cost"]))
-            late = min(ops[i]["start"] for i in u[1:]) - HOP - o["lat"] - o["cost"]
+            late = min(ops[i]["start"] - (ops[i]["eng"] != o["eng"]) * (HOP + o["lat"]) for i in u[1:]) - o["cost"]
             for a, b in mine[::-1]:
                 if b <= late:
                     break
@@ -724,12 +755,81 @@ def replay(ops, est, order, banks):
     return order, banks
 
 
+def shorten(ops, order, banks):
+    n = len(ops)
+    succ = [[] for _ in range(n)]
+    for i, o in enumerate(ops):
+        for j in o["data"]:
+            succ[j].append(i)
+    ests = [dict(EST, **s) for s in SETS]
+    prices = [[price(o, e) for o in ops] for e in ests]
+
+    def run(order, x):
+        for o, p in zip(ops, prices[x]):
+            o["cost"], o["lat"] = p
+        replay(ops, ests[x], order, banks)
+        return max(o["end"] for o in ops)
+
+    def whole(order):
+        on, seen = {}, set()
+        for i in order:
+            if isinstance(ops[i]["bank"], dict) and on.get(banks[i]) != ops[i]["bank"]["ops"][0]:
+                on[banks[i]] = ops[i]["bank"]["ops"][0]
+                if on[banks[i]] in seen:
+                    return False
+                seen.add(on[banks[i]])
+        return True
+    norm = [run(order, x) for x in range(len(ests))]
+    best, kept, turn = float(len(ests)), (float(len(ests)), order), 1
+    for step in range(EST["steps"]):
+        x = step % len(ests)
+        run(order, x)
+        before, last = {}, {}
+        for i in order:
+            before[i] = last.get(ops[i]["eng"])
+            last[ops[i]["eng"]] = i
+        i, links = max(order, key=lambda i: ops[i]["end"]), []
+        while i is not None:
+            o = ops[i]
+            tight = [j for j in o["dep"] if abs(after(o, ops[j], ests[x]) - o["start"]) < 1]
+            j = tight[-1] if tight else before[i] if o["start"] > 1 else None
+            if j is not None and j not in o["data"]:
+                links.append((j, i))
+            i = j
+        pos = dict((i, p) for p, i in enumerate(order))
+        for _ in range(12):
+            turn = (turn * 1103515245 + 12345) % 2147483648
+            j, i = links[(turn >> 8) % len(links)]
+            free = min([pos[s] for s in succ[j]] + [n])
+            moves = [(i, pos[j])] if all(pos[s] < pos[j] for s in ops[i]["data"]) else []
+            moves += [(j, pos[i]), (j, pos[i] + (turn >> 4) % (free - pos[i]))] if free > pos[i] else []
+            found = None
+            for a, p in moves:
+                new = [s for s in order if s != a]
+                new.insert(p, a)
+                if found is None and whole(new):
+                    v = sum(run(new, y) / norm[y] for y in range(len(ests)))
+                    if v < best + 0.001:
+                        found, best = new, v
+            if found:
+                order = found
+                kept = min(kept, (best, order))
+                break
+    run(kept[1], 0)
+    return kept[1], banks
+
+
+MADE = []
+
+
 def rank_program(g, core, T, topo):
     rank = T.rank_of(core)
     if rank is None:
         return
     ops = build(g, core, T, topo, rank)
-    order = schedule(ops, EST)[0]
+    if not MADE:
+        MADE.append(shorten(ops, *schedule(ops, EST)))
+    order = schedule(ops, EST, MADE[0])[0]
     queue = {"pe": g.tensor, "dve": g.vector, "act": g.scalar, "pool": g, "sp": g.sync}
     know = dict((e, {}) for e in queue)
     total = {}

@@ -81,8 +81,9 @@ for _n in ("w0h", "w1h"):
 _sb("g8", [8], "bfloat16")
 for _n in ("isf", "is16", "ones"):
     _sb(_n, [S], "bfloat16")
-for _n in ("mk", "d1", "ab", "run"):
+for _n in ("d1", "ab", "run"):
     _sb(_n, [4 * S], "bfloat16")
+_sb("mk", [2 * S], "bfloat16")
 _sb("cm", [512], "bfloat16")
 POOL = ["P0", "P1", "P2", "P3"]
 for _n in POOL + ["KB", "CE", "CC", "M1"]:
@@ -90,27 +91,29 @@ for _n in POOL + ["KB", "CE", "CC", "M1"]:
 
 NDMA = 30
 SEMAPHORES = ["pe", "dve", "act", "pool", "sent"] + ["d%d" % i for i in range(NDMA)] + ["a%d" % i for i in range(12)]
-PARTS = 2
+CUTS = (0, 256, 1024, B0)
+PARTS = len(CUTS) - 1
 
-EST = dict(cyc=0.86, pcy=0.43, gat=1.56, sca=3.8, hop=165.0, own=125.0, fv=22.0, fa=25.0, rlat=3000.0, rbw=50.0,
-           dlat=2200.0, dbw=220.0, push=100.0, steps=600)
-SETS = [{}, dict(cyc=0.83, pcy=0.42, hop=200.0, own=170.0, fv=0.0, fa=0.0, rlat=2600.0, rbw=65.0),
-        dict(cyc=1.18, pcy=0.6, gat=1.8, sca=5.0), dict(gat=1.3, hop=130.0, own=90.0, rlat=3600.0, rbw=38.0)]
-PLAN = [{"pa": "w1 v3 v1 w3 a2 m3 a2 w1", "xk": "aaaaaa", "cc": "avvvaa", "hg": "aaaa", "ht": "vava", "one": "vvava"},
-        {"pa": "v2 a2 a2 v1 v4 v1 v4", "xk": "avaaaa", "cc": "avvvaa", "hg": "aava", "ht": "aaaa", "one": "avaav"},
-        {"pa": "v2 a2 v2 a1 a2 a1 v1 v4 v1", "xk": "aavaav", "cc": "avvvaa", "hg": "aava", "ht": "aaaa", "one": "aaava"}]
-FIRST = {}
-U16 = True
-
-ORDER = ["UE DA PT+ TL hj ee+ hi cl DB xp xh HL ee ex tls tb3+ al ql sg PT fb ch cf HC a dd zz hx UF ce new se vals KB hv+ pl cc EP hd tb ptr cj CE D t yp hd+ tgl sc vl ci hv LL tab+ UF+ Dcc pl+ ptr+ lo UC tls+ tb+ off run HC+ xk hj++ HC++ ab cl+ NL tab U sg+ TL+ NL++ ch+ lo+ cvl", "D fi- pv- dd Dce- run off NL U CL- se xh+ hi+ ch+ CC- vf- HL UC Dce zz UE+ ax- DA hj cj hx3 UE ql vals dd+ xh hx vl ex+ fl ch3 ro rep EP lo+ ex tgl Dcc vals+ al hi xp ce hd3 KB UF+ fb CL DB ab al+ t ax+ pl+ CE yp R- yc- fi LL xk hv3 PT+ cf se+ cc new ql+ cvl U+ TL+", "ab new tab zz vf- a- sc- CC- HL hx vf CR-- hd3 R fl cc ptr pv- cj cf ch3 sc t hv D hx3 ce tb3 ro rep xk DA DB CR EP KB xp tls CE ee sg cl ci- tgl off tb fi ax- CR- UC ci run Dce CC vl a LL hd yc- R- yc Dcc hv3 fb yp"]
-PLAN = [{"pa": "w4 m1 w4 m1 w2 m2 a2", "xk": "aaaaaa", "cc": "aaavaa", "hg": "aavv", "ht": "vaaa", "one": "vvvvv"}, {"pa": "a2 v2 a1 v4 v3 a1 v1 a1 v1", "xk": "vaaaaa", "cc": "aavvav", "hg": "aava", "ht": "aaaa", "one": "vvaaa"}, {"pa": "a1 v4 a1 a2 v3 v1 v2 m2", "xk": "aavaav", "cc": "aavvaa", "hg": "avaa", "ht": "aava", "one": "aaava"}]
-ORDER = ["off HL hv cl ce rep+ vals zz xh xp HC yp lo DA+ pl hx cl+ NL al cj hj vl EP ql hd tls dd+ run xp+ CC KB ee sc dd a ptr t+ ro+ hd3++ se+ tgl CL CE ex ab t xk++ ex++ se tb DB+ tgl+ HL+ hi PT pl+ TL UE sg tb3++ tls+ ch3+ rep++ ci vf UC fi tab PT+ DB al+ hj++ D ch ql+ cc hj+ ci+ CR pv Dcc fb HC+ UF cvl zz+ DA xk ch+ LL R UC+ hv3++ hd3+", "HL+ U- cc fl cj new ee+ xh ee ax hv ptr off ce fl+ UE cf- pv KB Dcc U hx hd NL hv3 hx3 ch+ lo sc ab ro+ al+ hi+ new- DB+ fb TL UF DA+ tb3 CE D EP cf+ yc+ ex cf vals Dcc+ LL Dce pl+ hi tls+ sg ax- yp run tb+ UF+ new+ CL xk hd+ R+ tab vf+ zz+ sg+ TL+", "sc EP tb- vf- Dce-- ptr yc-- ql vl- KB cvl- Dce ax run CC- xh fi- HC R- a- UE hx ch3 hx3 lo cc PT dd CR- se ci cj ce hv xp U t CE vl D cl yp CC CR tgl UC LL a yc- off fi tab vals fb NL ab"]
-PLAN = [{"pa": "a1 w1 w4 m1 m2 a2 v1 x2 w2", "xk": "avaava", "cc": "vaaaaa", "hg": "avav", "ht": "vaaa", "one": "avava"}, {"pa": "v1 a2 v2 a2 v4 v4 v1", "xk": "aavaaa", "cc": "vaaaav", "hg": "aava", "ht": "aaaa", "one": "vaavv"}, {"pa": "v1 a2 v4 v2 a2 a2 v2 v1", "xk": "aaaava", "cc": "vvaava", "hg": "aava", "ht": "avaa", "one": "avava"}]
-ORDER = ["al+ cj hl HC ee tls UE ax ab lo pv EP yp ci ex+ hi+ HL dd xh hv DB UF PT hj tgl TL+ al cc ql hi DA NL+ CR hd+ zz vals ch sg ce hd R+ hx xh+ cf D off pl run PT++ KB cj++ hd3+ t xp fl+ CL+ CE se cl+ a tab", "run R- tls vals hj off vl- HC tb- ce+ ex- ci UF zz+ TL- cl- rep fb- vf- fi- new- ch3 hv3 yc- cj se zz hv U- LL- Dce- xk- ax+ CC- ax DA cvl- ptr lo D+ tab pl hv3+ ptr- KB ce hx sc- ex+ fb hl cl+ tb3 tgl tb ql+ UC- xh+ UE+ CE hj+ t+ U Dcc- EP ch3+ DA+ DB+ HL xp D new ee hx3 hd3+ tab+ CC DB dd se+ fi+ fi HL+ tls+ xp+ hd+ ci+ off+ t ee+ ql CL- dd+ ch Dce rep+ TL+ ab+ sg CR ptr+ LL", "LL vl tb UC UC- new a- xk- ab- UE- hv CC CE cvl- hx3 KB cc- HC pl yp- U ch pv- fl sc NL-- CR sg Dcc- vf- cf- Dce vl- hl EP hx al hi PT- lo sc- xk vals NL UF Dcc tgl cf cc tb3 a yc- vf yp fb R run yc"]
-PLAN = [{"pa": "w3 a2 w3 w1 w1 m2 a2 a2", "xk": "aaavav", "cc": "aavvva", "hs": "16 32 32", "hg": "afafa", "ht": "aaaaa", "hn": "av", "one": "avava"}, {"pa": "v2 a2 v2 x2 a1 v2 v2 a1 v1 v1", "xk": "aavaaa", "cc": "vvaava", "hs": "20 20 20 20", "hg": "aaafv", "ht": "aaaav", "hn": "aa", "one": "vaaav"}, {"pa": "v3 a2 v1 a1 a1 a1 v1 a1 v1 v4", "xk": "avaaaa", "cc": "vvvaaa", "hs": "16 24 24 16", "hg": "faaav", "ht": "aaaaa", "hn": "av", "one": "vvaav"}]
-ORDER = ["ci+ ci xh ql ptr fb R++ HC tb+ Dce ee ex+ HL pl+ UC ce DA+ zz+ xp+ PT tb hl+ cj vl+ ch hl++ xp UC+ ptr+ UF DA ax hx UE ex zz hm+ ch+ tab hv HC+ hj+ UE+ hd+ hm NL D ab lo off hj new ql+ cl dd xh+ al hi pl vals+ LL tgl+ CL al+ vals hv+ hd++ hl run ab+ UF+ fl++ a Dcc++ fi cp yp tgl hk TL EP CE sc xk cvl hj++ fi+ se KB cc", "sg hn+ zz+ hd- hi+ U+ vl- off+ ptr+ ax Dce KB fl sg- D lo cp9 cf- cp9+ U- cp R Dcc- CC- ch9 se hk+ HL rep ab+ hi R- hx EP cj cl tab UE+ ch+ ee run lo+ TL hk ax+ CE hn DA+ CR+ pl+ run+ ce pv- tab+ off yp NL cp+ vals+ cvl xk CR- cl+ ee+ ci+ PT LL Dcc Dce+ fb vl+ sc+ hv9+ a CC HL+ dd+ CE+ D+ hv9 cc pv HC+", "al xh ch9 U- new ex yc-- fb fi cf- rep hx xp TL sg hv sc- hm ql ce PT UF CR- se NL UC cc cj KB new- CL- xk CC yc LL a EP tb cf tgl yc- dd- yp"]
-PLAN = [{"pa": "m1 m1 w2 w4 v1 v1 v2 a2 a2", "xk": "aaaava", "cc": "avvavv", "hs": "32 16 32", "hg": "avfff", "ht": "aavaa", "hn": "vv", "one": "aavav", "xs": "112221", "ab": "aa", "su": "1"}, {"pa": "x2 a2 v4 v4 a2 v2", "xk": "aaaava", "cc": "avaavv", "hs": "16 24 24 16", "hg": "aaaff", "ht": "aaava", "hn": "vv", "one": "aaaav", "xs": "112122", "ab": "av", "su": "2"}, {"pa": "a2 a2 a1 v1 v4 v3 a1 v2", "xk": "vvaaaa", "cc": "avvvaa", "hs": "16 24 24 16", "hg": "faaav", "ht": "vaaav", "hn": "aa", "one": "avaav", "xs": "121112", "ab": "va", "su": "3"}]
-ORDER = ["ex ce hj xh vals HC ax vl al se hi HL ch lo hv dd ql hx EP hl Dce run new sg EP+ CL cc run+ LL UC fl+ cj hd DA sc tgl hk ee hm ch9+ hv9+ hn+ UE tab fi cvl UF cl neg ql+ ex+ HL+ TL xp ptr xp+ tb U cp D vl+ hi+ cf hk+ UE+ ee+ KB ab Dce+ xh+ NL R CE rep+ CC fb pl xk zz+ hx+ off al+ cl+ tgl+ cj+ ci+ sg+ UF+ hv+ hd+ pv ax+ hn++ cp+ hm+ tb+ pl+ hj++ CE+ neg+ PT fi++ yp PT+ ptr+ UC++ sc++ ci Dcc hl+ HC+ rep++ EP++ ch+ lo+", "hv9+ hl+ UC ax+ ab se hj R+ DA ch9+ cp9 ce dd a- D yp pv HL+ zz- ql+ xh+ CR- tab off TL KB a ex+ cf vals hi+ new cvl LL zz+ sc xk cj+ ci+ ee+ hk+ fl+ R al+ lo+ a+ UE+ Dcc TL+ PT+ ptr+ pl+ CC dd+ off+ U U+", "fb- fi- cp9 ch cp UF hx se neg cc- run D DA ab yc-- ce CE tgl vals xp Dce xk NL- CC HC tab KB CR tb CL- hm cl yc fb hd sg cc cf yp Dcc yc- CR- NL LL vl hv new"]
+EST = dict(cyc=0.85, pcy=0.43, gat=1.56, sca=3.8, hop=180.0, own=140.0, fv=20.0, fa=20.0, rlat=1800.0, rbw=72.0,
+           dlat=1300.0, dbw=250.0, push=100.0, steps=600)
+SETS = [{}, dict(cyc=0.83, pcy=0.42, hop=210.0, own=170.0, fv=0.0, fa=0.0, rlat=1300.0, rbw=95.0, dlat=1000.0),
+        dict(cyc=1.18, pcy=0.6, gat=1.8, sca=5.0),
+        dict(cyc=0.9, pcy=0.45, gat=1.3, sca=5.0, hop=160.0, own=120.0, fv=30.0, fa=40.0, rlat=2700.0, rbw=50.0, dlat=1900.0)]
+PLAN = [dict(pa="a2 a2 v1 v1 v1 v2 v2 a2 v2 v1", xk="aaaava", xs="111121", cc="vvaavv", su="1", hs="20 20 20 20", hg="afva",
+             ht="apvv", hn="pv", ab="av", one="aavvv"),
+        dict(pa="a2 v4 m1 a2 v1 v4 v2", xk="aaaavv", xs="122112", cc="avavaa", su="1", hs="16 32 32", hg="faa", ht="paa",
+             hn="va", ab="av", one="aaaav"),
+        dict(pa="v4 v2 v3 v1 a2 a2 a2", xk="vvaaaa", xs="221212", cc="avvvaa", su="2", hs="16 24 24 16", hg="faaa",
+             ht="aaaa", hn="pa", ab="va", one="avaav")]
+ORDER = ["lo++ cp ax+ sc vals+ sc+ hd cp9++ tab hx hk+ hi fi+ hj DA+ pl fl+ al UE++ UE hv dd+ se+ lo hk HL++ cj run cl EP EP+ "
+         "ptr UF sg cp9+ HL+ xh hj+ ci+ tgl hm cl+ ql ex ql+ ee",
+         "CC- hl ci- ax- hl- cc- TL- xk- ch- PT- yp- cf HL- DA- cvl- HC- vals- neg- off- ex+ ptr se- ab- xp- UE hi+ KB- D- CE- "
+         "NL- cj+ PT lo cp+ pl ee+ ch9 hv9 cvl fi+ UC+ sc+ xp+ ex CE+ se+ Dce- hn fb- ce- cp hn+ Dce+ R- hi zz- hm+ fi- ab LL- "
+         "vl- U- KB hv+ tgl ee a- yc- fb sg PT+ sg+ xk ptr+ neg cf- al neg+ TL xh D dd- vl hd ch hx hv tb ce CR- pl+ ch9+ xp "
+         "hv9+ hj+ UC- CE CC+ rep hm UC",
+         "off- pv-- U- ax TL run- ci new-- Dcc-- CL-- zz cc- tab- hl xh run new- UF- Dcc- yc CC- tgl Dce- UF cj- ql yp- LL- NL- "
+         "a- KB rep hk R CR dd Dcc al ab ch hx tb CL- fl cl ce yc- EP DA R- D xk vals new hd U off fb yp CR- pv- NL a cc zz- cf "
+         "HC tab LL vl HC- tb--"]
 
 
 def build(g, core, T, topo, rank):
@@ -195,14 +198,14 @@ def build(g, core, T, topo, rank):
     tab = [T["tab%d" % t] for t in range(4)]
     rep = [T["rep%d" % t] for t in range(3)]
     col = T.col
-    parts = [(B0 * i // PARTS, B0 * (i + 1) // PARTS) for i in range(PARTS)]
+    parts = list(zip(CUTS, CUTS[1:]))
     for i, (a, b) in enumerate(parts):
         dma("sp", tab[0][:, O + a:O + b], T.lab[:, a:b], [], ["lab%d" % i], 256 * b)
     dma("act", T.leafs[:], T.leaf[:], [], ["leafs"], 6e3)
     dma("act", T.wt[:], T.wts[:], [], ["wt"], 8e3)
     dma("act", T.covt[:], T.cov[:], [], ["covt"], 200e3)
-    dma("sp", T.acts[:], T.act[:], [], ["acts"], 600e3)
-    dma("sp", T.pths[:], T.pth[:], [], ["pths"], 1300e3)
+    dma("sp", T.pths[:], T.pth[:], [], ["pths"], 1150e3)
+    dma("sp", T.acts[:], T.act[:], [], ["acts"], 1300e3)
     K, PO, PEV, K0, PP, YB, AC, FB, PA = 0, 2, 3, 4, 5, 8, 12, 16, 20
 
     def c1(i):
@@ -219,11 +222,8 @@ def build(g, core, T, topo, rank):
     po(lambda: g.affine_select(T.ta[:], bo, [[1, 128]], A.is_ge, 0.0, 0, -1), ["bo"], ["ta"], 128)
     po(lambda: g.affine_select(T.tc[:], T.ta[:], [[1, 128]], A.not_equal, -1.0, 0, -1), ["ta"], ["tc"], 128)
     po(lambda: g.iota(T.isf[:], [[1, S]], 0, 0, allow_small_or_imprecise_dtypes=True), [], ["isf"], S)
-    for x in range(3):
-        po(lambda x=x: g.iota(T.ab[:, 256 * x:256 * x + 256], [[0, 4], [1, 64]], -48, 0, allow_small_or_imprecise_dtypes=True),
-           [], ["pidx%d" % x], 256)
-        po(lambda x=x: g.iota(T.run[:, 256 * x:256 * x + 256], [[16, 4], [0, 64]], 0, 0, allow_small_or_imprecise_dtypes=True),
-           [], ["spare%d" % x], 256)
+    po(lambda: g.iota(T.ab[:, 0:2 * S], [[0, 6], [1, 64]], -48, 0, allow_small_or_imprecise_dtypes=True), [], ["pidx"], 2 * S)
+    po(lambda: g.iota(T.run[:, 0:256], [[16, 4], [0, 64]], 0, 0, allow_small_or_imprecise_dtypes=True), [], ["spare"], 256)
     for t in range(2):
         dv(lambda t=t: V.memset(tab[t][:, 0:O], 512.0), [], ["sen%d" % t], 16)
     dv(lambda: V.memset(T.cm[:], -0.6875), [], ["cm"], 256)
@@ -244,10 +244,13 @@ def build(g, core, T, topo, rank):
     ac(lambda: ACT.activation(T.warm[:, 0:16], T.ones[:, 0:16], F.Sigmoid), ["ones"], ["warm"], 16, kind="first")
     lin(T.sl[:], T.s36[:, 0:12], ["s36", "K"], ["sl"], 12, 1.0, c1(K))
     dv(lambda: ts(T.nw[:], T.s36[:], c1(K), A.add, float(B0), A.add), ["s36", "K"], ["nw"], 36)
-    dv(lambda: ts(T.mk[:], T.ab[:], c1(K), A.is_ge, 4096.0, A.mult), ["pidx0", "pidx1", "pidx2", "K"], ["mk0", "ab0", "ab1"], 2 * S)
-    add("dve", lambda: [V.memset(T.mk[:, 64 * h:64 * h + 48 - 16 * h], 4096.0) for h in range(3)], ["mk0"], ["mk"], 192, calls=3)
-    lin(T.d1[:], T.run[:], ["spare0", "spare1", "spare2", "K"], ["d0", "run"], 4 * S, 1.0, c1(K))
-    dv(lambda: V.memset(T.d1[:, 63:4 * S:64], 4096.0), ["d0"], ["d1"], 12)
+    dv(lambda: ts(T.mk[:], T.ab[:, 0:2 * S], c1(K), A.is_ge, 4096.0, A.mult), ["pidx", "K"], ["mk", "ab0"], S)
+    dv(lambda: ts(T.d1[:, 0:256], T.run[:, 0:256], c1(K), A.add), ["spare", "K"], ["d0", "run"], 128)
+    dv(lambda: V.memset(T.d1[:, 63:256:64], 4096.0), ["d0"], ["d10"], 4)
+    for x in (1, 2):
+        po(lambda x=x: g.affine_select(T.d1[:, 256 * x:256 * x + 256], T.d1[:, 0:256], [[0, 256]], A.is_ge, 0.0, 0, 0),
+           ["d10"], ["d1%d" % x], 256)
+    d1k = ["d11", "d12"]
     dv(lambda: V.tensor_tensor(T.pi[:, 3:4], T.pi[:, 0:1], T.pi[:, 2:3], A.add), ["pi0", "pi2"], ["pi3"], 1)
     dv(lambda: ts(T.pi[:, 4:5], T.pi[:, 3:4], 1, A.bitwise_and), ["pi3"], ["pi4"], 1)
     dv(lambda: ts(c1(PP), T.pi[:, 4:5], float(TW // 2), A.mult), ["pi4"], ["PP"], 1)
@@ -292,7 +295,7 @@ def build(g, core, T, topo, rank):
         tb, ch, hx, xp, xk, ce, cc, ex, ptr = [T["%s%d" % (n, t)] for n in ("tb", "ch", "hx", "xp", "xk", "ce", "cc", "ex", "ptr")]
         if t == 0:
             for i, (a, b) in enumerate(parts):
-                send(0, [(rep[0][:, O + a:O + b], tab[0][:, O + a:O + b])], ["lab%d" % i], ["rp%d" % i], 256 * b - 58 * a)
+                send(0, [(rep[0][:, O + a:O + b], tab[0][:, O + a:O + b])], ["lab%d" % i], ["rp%d" % i], 256 * b - 58 * (b - CUTS[1]))
             dma("sp", nxt[:, O:O + B], win, tk + ["rp%d" % i for i in range(PARTS)], ["tab1c"], 256 * B)
         else:
             dma("sp", nxt[:, 0:O + B], tab[t][:, 0:O + B], tk, ["tab%dc" % (t + 1)], 256 * B)
@@ -319,7 +322,9 @@ def build(g, core, T, topo, rank):
             lab = tab[t][:, O + 16 * a:O + 16 * b]
             gat, mine, out = cwin.indirect(T.covl[:, a:b]), tb[:, 16 * a:16 * b], ch[:, 16 * a:16 * b]
             if eg == "f":
-                if et == "a":
+                if et == "p":
+                    po(lambda: g.affine_select(mine, lab, [[0, n]], A.is_ge, 0.0, 0, 0), tk, [k("cp%d" % i)], n)
+                elif et == "a":
                     ac(lambda: ACT.activation(mine, lab, F.Copy), tk, [k("cp%d" % i)], n)
                 else:
                     dv(lambda: V.tensor_copy(mine, lab), tk, [k("cp%d" % i)], n / 2)
@@ -393,7 +398,7 @@ def build(g, core, T, topo, rank):
                 po(lambda n=n: g.affine_select(ex[:, n * S:2 * n * S], ex[:, 0:n * S], [[0, n * S]], A.is_ge, 0.0, 0, 0),
                    [k("ex%d" % n)], [k("ex%d" % (2 * n))], n * S)
         if t < 2:
-            send(t + 1, [(rep[t + 1][:, O:O + B], win)], tk + ([] if t else tbk), ["repc%d" % (t + 1)], 256 * B)
+            send(t + 1, [(rep[t + 1][:, O:O + B], win)], tk + ([] if t else rk[:-1]), ["repc%d" % (t + 1)], 256 * B)
 
         done = dict(CE=0, KB=0)
 
@@ -489,14 +494,15 @@ def build(g, core, T, topo, rank):
             dma("sp", T.yv[:], vn, ["vl3"], [], 6e3)
         tl = T.M1[:, 384:396]
         pe(lambda: [(tl, E(T.eb, j), XJ(T.se, j), j == 0, j == 15) for j in range(16)], 1024, [k("se"), "eb"], ["TL"], "M1")
-        dv(lambda: V.tensor_tensor(L(T.tgl), tl, T.d1[:, 0:4 * S:64], A.max), ["TL", "d1"], [k("tgl")], 12, "M1")
+        dv(lambda: V.tensor_tensor(L(T.tgl), tl, T.d1[:, 0:4 * S:64], A.max), ["TL"] + d1k, [k("tgl")], 12, "M1")
         vals, cols = T.msg[:, MW * t:MW * t + S], T.msg[:, MW * t + S:MW * t + S + 12]
         dv(lambda: V.tensor_tensor(vals, tab[t][:, 0:O + B].indirect(L(T.tgl)), X(T.ee), A.max),
            tk + [k("tgl"), k("ee")], [k("vals")], S, kind=GAT)
         for x, (bank, keys) in enumerate((("CE", cek), ("KB", ["KB"]))):
             hs = range(6 * x, 6 * x + 6)
-            pe(lambda x=x, bank=bank: [(T[bank][:, 0:2 * S], T.idn[:], T.mk[:, 2 * S * x:2 * S * x + 2 * S], True, False)], 2 * S,
-               ["idn", "mk"], [k("D%d" % x)] + keys, bank)
+            pe(lambda x=x, bank=bank: [(T[bank][:, 0:2 * S], T.idn[:], T.mk[:], True, False)] +
+               [(T[bank][:, 64 * h:48 + 48 * h], T.i4p[:], T.ones[:, 0:48 - 16 * h], False, False) for h in range(3 - 3 * x)],
+               2 * S + 192 * (1 - x), ["idn", "i4p", "ones", "mk"], [k("D%d" % x)] + keys, bank)
             pe(lambda bank=bank, hs=hs: [(T[bank][:, 64 * (h % 6) + 48 - 16 * min(h, 3):64 * (h % 6) + 64], bo,
                                           T.se[:, S * t + 16 * max(h - 3, 0):S * t + 16 * h + 16], False, h == hs[-1]) for h in hs],
                384, ["TL", k("D%d" % x), k("se"), "bo"], [k("DA%d" % x)], bank)
@@ -510,13 +516,14 @@ def build(g, core, T, topo, rank):
             add("dve", lambda bank=bank, hs=hs: [ts(T.ab[:, 64 * h:64 * h + 64], T[bank][:, 64 * (h % 6):64 * (h % 6) + 64], tl[:, h:h + 1],
                                                     A.not_equal, 4096.0, A.mult) for h in hs],
                 ["TL", k("DA%d" % x)] + keys, ["ab%d" % x], 2 * S, bank="M1", calls=6)
-        dv(lambda: V.tensor_tensor_scan(T.run[:], T.ab[:], T.d1[:], 4096.0, A.min, A.max), ["ab0", "ab1", "d1"], ["run"], 2 * S)
+        dv(lambda: V.tensor_tensor_scan(T.run[:], T.ab[:], T.d1[:], 4096.0, A.min, A.max), ["ab0", "ab1"] + d1k, ["run"], 2 * S)
         off = L(T.off)
         dv(lambda: V.tensor_tensor(off, T.run[:, 62:4 * S:64], L(T.tgl), A.min), ["run", k("tgl")], [k("off")], 24)
         if t < 2:
-            send(t + 1, [(rep[t + 1][:, O + B:O + B + S], nxt[:, O + B:O + B + S])], ["new%d" % (t + 1)], ["rn%d" % (t + 1)], 49e3)
             send(t + 1, [(T.rmsg[:, MW * t:MW * t + S], vals)], [k("vals")], ["rv%d" % (t + 1)], 49e3)
             send(t + 1, [(L(T.roff), off)], [k("off")], ["ro%d" % (t + 1)], 3e3)
+            send(t + 1, [(rep[t + 1][:, O + B:O + B + S], nxt[:, O + B:O + B + S])], ["new%d" % (t + 1), k("off")],
+                 ["rn%d" % (t + 1)], 49e3)
         scatter(nxt[:, 0:O + B], off, vals, ["tab%dc" % (t + 1), "sen1", k("off"), k("vals")], ["tab%d" % (t + 1)])
         if t == 2:
             dma("sp", T.yx[:, 0:B], nxt[:, O:O + B], ["tab3"], [], 256 * B)
@@ -793,7 +800,7 @@ def shorten(ops, order, banks):
             o = ops[i]
             tight = [j for j in o["dep"] if abs(after(o, ops[j], ests[x]) - o["start"]) < 1]
             j = tight[-1] if tight else before[i] if o["start"] > 1 else None
-            if j is not None and j not in o["data"]:
+            if j is not None and j not in o["data"] and not (o["sem"] and ops[j]["sem"]):
                 links.append((j, i))
             i = j
         pos = dict((i, p) for p, i in enumerate(order))
@@ -807,7 +814,7 @@ def shorten(ops, order, banks):
             for a, p in moves:
                 new = [s for s in order if s != a]
                 new.insert(p, a)
-                if found is None and whole(new):
+                if found is None and not ops[a]["sem"] and whole(new):
                     v = sum(run(new, y) / norm[y] for y in range(len(ests)))
                     if v < best + 0.001:
                         found, best = new, v

from concourse.bass import DstId, RemoteDMATransfer
from concourse.mybir import AluOpType as A, ActivationFunctionType as F

B0, S, RO, DA = 1280, 192, 3, 512
JUMPS = [4, 1, 6]
O = 80
CW = 64
BS = [B0 + S * t for t in range(RO + 1)]
BASE = 65536.0
C = BASE + 256.5
TW = 416
MW = 208

SCRATCH = {}


def _sb(name, shape, d):
    SCRATCH[name] = ("sbuf", [128] + shape, d)


for _t in range(4):
    _sb("tab%d" % _t, [O + BS[_t]], "bfloat16")
for _t in range(3):
    _sb("rep%d" % _t, [O + BS[_t]], "bfloat16")
    for _n in ("tb", "ch", "hx"):
        _sb("%s%d" % (_n, _t), [BS[_t]], "bfloat16")
    for _n in ("xp", "xk", "ce", "cc"):
        _sb("%s%d" % (_n, _t), [S * 16], "bfloat16")
    _sb("ex%d" % _t, [S * 4], "float32")
    _sb("ptr%d" % _t, [TW], "float32")
for _n in ("xh", "dd", "zz", "ee", "fl", "sg", "lo", "fi", "ax", "hl"):
    _sb(_n, [3 * S], "bfloat16")
for _n in ("se", "sc", "pv", "cf"):
    _sb(_n, [3 * S], "float16")
for _n in ("ypb", "ycb"):
    _sb(_n, [3 * S], "float32")
for _n in ("ci", "cj"):
    _sb(_n, [3 * S], "int32")
for _n in ("pl", "cl"):
    _sb(_n, [3 * S], "uint16")
for _n in ("hi", "hj"):
    _sb(_n, [72], "int32")
for _n in ("al", "ql", "tgl", "vl"):
    _sb(_n, [36], "uint16")
for _n in ("t1", "s36"):
    _sb(_n, [36], "float32")
_sb("nw", [36], "float16")
_sb("off", [36], "uint16")
_sb("roff", [24], "uint16")
_sb("vf", [12], "float32")
_sb("covl", [104], "uint16")
_sb("msg", [3 * MW], "float16")
_sb("rmsg", [2 * MW], "float16")
_sb("acts", [DA], "bfloat16")
_sb("pths", [B0], "int32")
_sb("wt", [16], "int32")
for _n in ("wa", "wb"):
    _sb(_n, [17], "int32")
_sb("wf", [17], "float32")
_sb("kl", [8], "uint16")
_sb("leafs", [12], "int32")
_sb("covt", [5, 16], "int32")
_sb("covm", [5, 32], "float32")
_sb("covx", [5, 32], "float32")
_sb("covs", [5, 16], "float32")
_sb("pi", [8], "int32")
_sb("col", [24], "float32")
_sb("even", [4], "bfloat16")
_sb("neg", [36], "float32")
_sb("pk", [12], "int32")
for _n in ("sl", "pa", "pb", "pc"):
    _sb(_n, [12], "float32")
_sb("own", [12], "uint16")
for _n in ("b1", "bo", "eb", "ebn"):
    _sb(_n, [144], "bfloat16")
for _n in ("bok", "bon", "idn", "ineg", "i4p", "i4n", "ta", "tc", "tr", "sh", "warm"):
    _sb(_n, [128], "bfloat16")
_sb("wm", [128], "float16")
for _n in ("w0h", "w1h"):
    _sb(_n, [144], "float16")
_sb("g8", [8], "bfloat16")
for _n in ("isf", "is16", "ones"):
    _sb(_n, [S], "bfloat16")
for _n in ("d1", "ab", "run"):
    _sb(_n, [4 * S], "bfloat16")
_sb("mk", [2 * S], "bfloat16")
_sb("cm", [512], "bfloat16")
POOL = ["P0", "P1", "P2", "P3"]
for _n in POOL + ["KB", "CE", "CC", "M1"]:
    SCRATCH[_n] = ("psum", [128, 512], "float32")

NDMA = 30
SEMAPHORES = ["pe", "dve", "act", "pool", "sent"] + ["d%d" % i for i in range(NDMA)] + ["a%d" % i for i in range(12)]
CUTS = (0, 256, 1024, B0)
PARTS = len(CUTS) - 1

EST = dict(cyc=0.85, pcy=0.43, gat=1.56, sca=3.8, hop=180.0, own=140.0, fv=20.0, fa=20.0, rlat=1800.0, rbw=72.0,
           dlat=1300.0, dbw=250.0, push=100.0, steps=600)
SETS = [{}, dict(cyc=0.83, pcy=0.42, hop=210.0, own=170.0, fv=0.0, fa=0.0, rlat=1300.0, rbw=95.0, dlat=1000.0),
        dict(cyc=1.18, pcy=0.6, gat=1.8, sca=5.0),
        dict(cyc=0.9, pcy=0.45, gat=1.3, sca=5.0, hop=160.0, own=120.0, fv=30.0, fa=40.0, rlat=2700.0, rbw=50.0, dlat=1900.0)]
PLAN = [dict(pa="a2 a2 v1 v1 v1 v2 v2 a2 v2 v1", xk="aaaava", xs="111121", cc="vvaavv", su="1", hs="20 20 20 20", hg="afva",
             ht="apvv", hn="pv", ab="av", one="aavvv"),
        dict(pa="a2 v4 m1 a2 v1 v4 v2", xk="aaaavv", xs="122112", cc="avavaa", su="1", hs="16 32 32", hg="faa", ht="paa",
             hn="va", ab="av", one="aaaav"),
        dict(pa="v4 v2 v3 v1 a2 a2 a2", xk="vvaaaa", xs="221212", cc="avvvaa", su="2", hs="16 24 24 16", hg="faaa",
             ht="aaaa", hn="pa", ab="va", one="avaav")]
ORDER = ["lo++ cp ax+ sc vals+ sc+ hd cp9++ tab hx hk+ hi fi+ hj DA+ pl fl+ al UE++ UE hv dd+ se+ lo hk HL++ cj run cl EP EP+ "
         "ptr UF sg cp9+ HL+ xh hj+ ci+ tgl hm cl+ ql ex ql+ ee",
         "CC- hl ci- ax- hl- cc- TL- xk- ch- PT- yp- cf HL- DA- cvl- HC- vals- neg- off- ex+ ptr se- ab- xp- UE hi+ KB- D- CE- "
         "NL- cj+ PT lo cp+ pl ee+ ch9 hv9 cvl fi+ UC+ sc+ xp+ ex CE+ se+ Dce- hn fb- ce- cp hn+ Dce+ R- hi zz- hm+ fi- ab LL- "
         "vl- U- KB hv+ tgl ee a- yc- fb sg PT+ sg+ xk ptr+ neg cf- al neg+ TL xh D dd- vl hd ch hx hv tb ce CR- pl+ ch9+ xp "
         "hv9+ hj+ UC- CE CC+ rep hm UC",
         "off- pv-- U- ax TL run- ci new-- Dcc-- CL-- zz cc- tab- hl xh run new- UF- Dcc- yc CC- tgl Dce- UF cj- ql yp- LL- NL- "
         "a- KB rep hk R CR dd Dcc al ab ch hx tb CL- fl cl ce yc- EP DA R- D xk vals new hd U off fb yp CR- pv- NL a cc zz- cf "
         "HC tab LL vl HC- tb--"]


def build(g, core, T, topo, rank):
    ops = []
    cores = T.cores
    N = len(cores)
    V, ACT, PE = g.vector, g.scalar, g.tensor
    nd = [0]
    na = [0]
    now = [-1]
    GAT, SCA = "gat", "sca"

    def add(eng, fn, r, w, n, kind=None, bank=None, grp=None, sem=None, cnt=0, loc=0, calls=1):
        o = dict(eng=eng, fn=fn, r=list(r), w=list(w), n=n, kind=kind, bank=bank, grp=grp, sem=sem, cnt=cnt, loc=loc, calls=calls,
                 t=now[0])
        if isinstance(bank, dict):
            bank["ops"].append(len(ops))
        ops.append(o)

    def dv(fn, r, w, n, bank=None, kind=None):
        add("dve", lambda: [fn()], r, w, n, kind, bank)

    def ac(fn, r, w, n, bank=None, kind=None):
        add("act", lambda: [fn()], r, w, n, kind, bank)

    def pe(fn, cyc, r, w, bank, grp=None):
        add("pe", lambda: [PE.matmul(*m) for m in fn()], r, w, cyc, None, bank, grp)

    def po(fn, r, w, n):
        add("pool", lambda: [fn()], r, w, n)

    def tile():
        return dict(ops=[], b=None)

    def P(tl):
        return T[tl["b"]]

    def dma(q, out, in_, r, w, nbytes):
        s = "d%d" % nd[0]
        nd[0] += 1
        eng = g.sync if q == "sp" else g.scalar
        add(q, lambda: [eng.dma_start(out, in_)], r, w, nbytes, "dma", sem=s, cnt=16)

    def send(t, pairs, r, w, nbytes):
        dst = cores[(rank - JUMPS[t]) % N]
        src = cores[(rank + JUMPS[t]) % N]
        s = "a%d" % na[0]
        na[0] += 1
        rid, pid = topo.addr(dst, core)
        en = topo.engines(core, dst)

        def fn():
            if len(pairs) == 1:
                g.remote_dma(pairs[0][0], pairs[0][1], T.sem[s], T.sem.sent, pid, rid, topo.mask(core, dst))
            else:
                h = len(en) // len(pairs)
                tr = [RemoteDMATransfer(dst_ids=[DstId(rid=rid, pnc=pid)],
                                        dma_engine_mask=sum(1 << e for e in en[i * h:(i + 1) * h]),
                                        remote_sem=T.sem[s], src=p[1], dst=p[0]) for i, p in enumerate(pairs)]
                g.remote_dma_fused(tr, local_sem=T.sem.sent)
            return []
        add("pool", fn, r, w, nbytes, "send", sem=s, cnt=len(topo.engines(src, core)), loc=len(en))

    def ts(out, in0, s1, op0, s2=None, op1=None):
        if op1 is None:
            return V.tensor_scalar(out, in0, s1, None, op0)
        return V.tensor_scalar(out, in0, s1, s2, op0, op1)

    def lin(out, in_, r, w, n, scale=1.0, bias=0.0, f=None):
        ac(lambda: ACT.activation(out, in_, f or F.Identity, bias=bias, scale=scale), r, w, n)

    def fetch(e, out, window, r, w, n):
        if e == "a":
            ac(lambda: ACT.activation(out, window, F.Copy), r, w, n, kind=GAT)
        else:
            dv(lambda: V.tensor_copy(out, window), r, w, n, kind=GAT)

    def scatter(window, offs, vals, r, w):
        for h in (8, 4, 0):
            dv(lambda h=h: V.tensor_copy(window.indirect(offs[:, h:h + 4]), vals[:, 16 * h:16 * h + 64]), r, w, 64, kind=SCA)

    tab = [T["tab%d" % t] for t in range(4)]
    rep = [T["rep%d" % t] for t in range(3)]
    col = T.col
    parts = list(zip(CUTS, CUTS[1:]))
    for i, (a, b) in enumerate(parts):
        dma("sp", tab[0][:, O + a:O + b], T.lab[:, a:b], [], ["lab%d" % i], 256 * b)
    dma("act", T.leafs[:], T.leaf[:], [], ["leafs"], 6e3)
    dma("act", T.wt[:], T.wts[:], [], ["wt"], 8e3)
    dma("act", T.covt[:], T.cov[:], [], ["covt"], 200e3)
    dma("sp", T.pths[:], T.pth[:], [], ["pths"], 1150e3)
    dma("sp", T.acts[:], T.act[:], [], ["acts"], 1300e3)
    K, PO, PEV, K0, PP, YB, AC, FB, PA = 0, 2, 3, 4, 5, 8, 12, 16, 20

    def c1(i):
        return col[:, i:i + 1]
    bo = T.bo[:, 0:128]
    dv(lambda: V.memset(T.ones[:], 1.0), [], ["ones"], S / 2)
    po(lambda: g.iota(T.pi[:, 0:1], [[0, 1]], 0, 1), [], ["pi0"], 1)
    po(lambda: g.iota(T.s36[:], [[S, 3], [16, 12]], 0, 0, allow_small_or_imprecise_dtypes=True), [], ["s36"], 36)
    po(lambda: g.affine_select(T.b1[:], T.ones[:, 0:144], [[-16, 9], [0, 16]], A.is_ge, 0.0, 0, 1), ["ones"], ["b1"], 144)
    po(lambda: g.affine_select(T.bo[:], T.b1[:], [[16, 9], [0, 16]], A.is_ge, 0.0, 15, -1), ["b1"], ["bo"], 144)
    po(lambda: g.affine_select(T.eb[:], T.bo[:], [[0, 9], [1, 16]], A.is_equal, 0.0, -15, 0), ["bo"], ["eb"], 144)
    po(lambda: g.affine_select(T.idn[:], T.ones[:, 0:128], [[1, 128]], A.is_equal, 0.0, 0, -1), ["ones"], ["idn"], 128)
    po(lambda: g.affine_select(T.sh[:], bo, [[1, 128]], A.is_equal, 0.0, -1, -1), ["bo"], ["sh"], 128)
    po(lambda: g.affine_select(T.ta[:], bo, [[1, 128]], A.is_ge, 0.0, 0, -1), ["bo"], ["ta"], 128)
    po(lambda: g.affine_select(T.tc[:], T.ta[:], [[1, 128]], A.not_equal, -1.0, 0, -1), ["ta"], ["tc"], 128)
    po(lambda: g.iota(T.isf[:], [[1, S]], 0, 0, allow_small_or_imprecise_dtypes=True), [], ["isf"], S)
    po(lambda: g.iota(T.ab[:, 0:2 * S], [[0, 6], [1, 64]], -48, 0, allow_small_or_imprecise_dtypes=True), [], ["pidx"], 2 * S)
    po(lambda: g.iota(T.run[:, 0:256], [[16, 4], [0, 64]], 0, 0, allow_small_or_imprecise_dtypes=True), [], ["spare"], 256)
    for t in range(2):
        dv(lambda t=t: V.memset(tab[t][:, 0:O], 512.0), [], ["sen%d" % t], 16)
    dv(lambda: V.memset(T.cm[:], -0.6875), [], ["cm"], 256)
    dv(lambda: ts(T.pi[:, 1:2], T.pi[:, 0:1], 15, A.bitwise_and), ["pi0"], ["pi1"], 1)
    dv(lambda: ts(T.pi[:, 2:3], T.pi[:, 0:1], 4, A.arith_shift_right, 1, A.bitwise_and), ["pi0"], ["pi2"], 1)
    dv(lambda: V.tensor_copy(c1(K), T.pi[:, 1:2]), ["pi1"], ["K"], 1)
    dv(lambda: V.tensor_copy(c1(PO), T.pi[:, 2:3]), ["pi2"], ["PO"], 1)
    lin(c1(PEV), c1(PO), ["PO"], ["PEV"], 1, -1.0, 1.0)
    lin(c1(K0), c1(K), ["K"], ["K0"], 1, -1.0, 1.0, F.Relu)
    for t in range(3):
        lin(c1(YB + t), c1(K0), ["K0"], ["YB%d" % t], 1, float(BS[t]))
    for name, src, scale in (("bok", "bo", 16384.0), ("bon", "bo", -4096.0), ("ineg", "idn", -1.0),
                             ("i4p", "idn", 4096.0), ("i4n", "idn", -4096.0), ("tr", "tc", -4096.0)):
        lin(T[name][:], T[src][:, 0:128], [src], [name], 128, scale)
    lin(T.ebn[:], T.eb[:], ["eb"], ["ebn"], 144, -256.0)
    lin(T.is16[:], T.isf[:], ["isf"], ["is16"], S, 1.0 / 16)
    lin(T.g8[:], T.bo[:, 0:128:16], ["bo"], ["g8"], 8)
    ac(lambda: ACT.activation(T.warm[:, 0:16], T.ones[:, 0:16], F.Sigmoid), ["ones"], ["warm"], 16, kind="first")
    lin(T.sl[:], T.s36[:, 0:12], ["s36", "K"], ["sl"], 12, 1.0, c1(K))
    dv(lambda: ts(T.nw[:], T.s36[:], c1(K), A.add, float(B0), A.add), ["s36", "K"], ["nw"], 36)
    dv(lambda: ts(T.mk[:], T.ab[:, 0:2 * S], c1(K), A.is_ge, 4096.0, A.mult), ["pidx", "K"], ["mk", "ab0"], S)
    dv(lambda: ts(T.d1[:, 0:256], T.run[:, 0:256], c1(K), A.add), ["spare", "K"], ["d0", "run"], 128)
    dv(lambda: V.memset(T.d1[:, 63:256:64], 4096.0), ["d0"], ["d10"], 4)
    for x in (1, 2):
        po(lambda x=x: g.affine_select(T.d1[:, 256 * x:256 * x + 256], T.d1[:, 0:256], [[0, 256]], A.is_ge, 0.0, 0, 0),
           ["d10"], ["d1%d" % x], 256)
    d1k = ["d11", "d12"]
    dv(lambda: V.tensor_tensor(T.pi[:, 3:4], T.pi[:, 0:1], T.pi[:, 2:3], A.add), ["pi0", "pi2"], ["pi3"], 1)
    dv(lambda: ts(T.pi[:, 4:5], T.pi[:, 3:4], 1, A.bitwise_and), ["pi3"], ["pi4"], 1)
    dv(lambda: ts(c1(PP), T.pi[:, 4:5], float(TW // 2), A.mult), ["pi4"], ["PP"], 1)
    dv(lambda: ts(T.pk[:], T.sl[:], 1.0 / 12, A.mult, -5.5 / 12, A.add), ["sl"], ["pk"], 12)
    dv(lambda: ts(T.pa[:], T.pk[:], float(1 - S), A.mult, c1(PP), A.add), ["pk", "PP"], ["pa"], 12)
    lin(T.pb[:], T.sl[:], ["sl"], ["pb"], 12, 16.0)
    dv(lambda: V.tensor_tensor(T.pc[:], T.pa[:], T.pb[:], A.add), ["pa", "pb"], ["pc"], 24)
    dv(lambda: V.tensor_copy(T.own[:], T.pc[:]), ["pc"], ["perm"], 12)
    dv(lambda: ts(T.wa[:, 0:16], T.wt[:], 2048.0, A.add), ["wt"], ["wa0"], 16)
    dv(lambda: ts(T.wa[:, 16:17], T.wt[:, 0:1], 8.0, A.mult, 2048.0, A.add), ["wt"], ["wa1"], 1)
    dv(lambda: ts(T.wb[:], T.wa[:], 4095, A.bitwise_and), ["wa0", "wa1"], ["wb"], 17)
    dv(lambda: ts(T.wf[:], T.wb[:], -2048.0, A.add), ["wb"], ["wf"], 17)
    dv(lambda: ts(T.w0h[:], T.eb[:], T.wf[:, 16:17], A.mult), ["eb", "wf"], ["w0h"], 72)
    dv(lambda: ts(T.w1h[:], T.eb[:], T.wf[:, 1:2], A.mult), ["eb", "wf"], ["w1h"], 72)
    dv(lambda: ts(T.kl[:], T.s36[:, 0:8], 0.0, A.mult, c1(K), A.add), ["s36", "K"], ["kl"], 8)
    dv(lambda: V.tensor_tensor(T.wm[:], T.wf[:, 0:16].indirect(T.kl[:]), bo, A.mult), ["wf", "kl", "bo"], ["wm"], 128, kind=GAT)
    ct = ["covt"]
    dv(lambda: ts(T.covm[:, :, 0:16], T.covt[:], 16.0, A.add, c1(PEV), A.mult), ct + ["PEV"], ["covm0"], 80)
    dv(lambda: ts(T.covm[:, :, 16:32], T.covt[:], 16.0, A.add, c1(PO), A.mult), ct + ["PO"], ["covm1"], 80)
    dv(lambda: V.transpose(T.covx[:], T.covm[:]), ["covm0", "covm1"], ["covx"], 160)
    dv(lambda: V.tensor_tensor(T.covs[:], T.covx[:, :, 0:16], T.covx[:, :, 16:32], A.add), ["covx"], ["covs"], 160)
    add("dve", lambda: [V.tensor_copy(T.covl[:, u:80:5], T.covs[:, u, :]) for u in range(5)], ["covs"], ["covl"], 64 * 5, calls=5)
    dv(lambda: V.tensor_copy(T.vl[:, 0:12], T.leafs[:]), ["leafs"], ["vl0"], 12)
    dv(lambda: V.tensor_copy(T.pv[:, 0:S], T.pths[:].indirect(T.vl[:, 0:12])), ["pths", "vl0"], ["pv0"], S, kind=GAT)

    def E(buf, j):
        return buf[:, 15 - j:143 - j]

    def one_round(t):
        now[0] = t
        B = BS[t]
        c = B // 64
        plan = PLAN[t]
        k = lambda n: "%s_%d" % (n, t)
        X = lambda buf: buf[:, S * t:S * t + S]
        L = lambda buf: buf[:, 12 * t:12 * t + 12]
        XJ = lambda buf, j: buf[:, S * t + j:S * t + S:16]
        tk = ["lab%d" % i for i in range(PARTS)] + ["sen0"] if t == 0 else ["tab%d" % t, "new%d" % t]
        win = tab[t][:, O:O + B]
        cwin = tab[t][:, CW:O + B]
        nxt = tab[t + 1]
        tb, ch, hx, xp, xk, ce, cc, ex, ptr = [T["%s%d" % (n, t)] for n in ("tb", "ch", "hx", "xp", "xk", "ce", "cc", "ex", "ptr")]
        if t == 0:
            for i, (a, b) in enumerate(parts):
                send(0, [(rep[0][:, O + a:O + b], tab[0][:, O + a:O + b])], ["lab%d" % i], ["rp%d" % i], 256 * b - 58 * (b - CUTS[1]))
            dma("sp", nxt[:, O:O + B], win, tk + ["rp%d" % i for i in range(PARTS)], ["tab1c"], 256 * B)
        else:
            dma("sp", nxt[:, 0:O + B], tab[t][:, 0:O + B], tk, ["tab%dc" % (t + 1)], 256 * B)
        pt = tile()
        pe(lambda: [(P(pt)[:, a:a + n], T.idn[:], T.pv[:, S * t:S * t + n], True, True)
                    for a, n in ((0, S), (S, 16), (TW // 2, S), (TW - 16, 16))], 2 * S + 128, ["pv%d" % t, "idn"], [k("PT")], pt)
        dv(lambda: V.transpose(ptr[:], P(pt)[:, 0:TW]), [k("PT")], [k("ptr")], TW, pt)
        dv(lambda: V.tensor_copy(X(T.pl), ptr[:].indirect(T.own[:])), [k("ptr"), "perm"], [k("pl")], S, kind=GAT)
        fetch(plan["one"][0], X(T.xh), win.indirect(L(T.vl)), tk + ["vl%d" % t], [k("xh")], S)
        for h, wm in enumerate((T.w0h, T.w1h)):
            pe(lambda h=h, wm=wm: [(T.M1[:, 400 + 12 * h:412 + 12 * h], E(wm, j), XJ(T.xh, j), j == 0, j == 15) for j in range(16)],
               1024, [k("xh"), "w%dh" % h], ["HL%d" % h], "M1")
        for h, (a, b) in enumerate((("hi", "hj"), ("hk", "hm"))):
            hi, hj = T.hi[:, 24 * t + 12 * h:24 * t + 12 * h + 12], T.hj[:, 24 * t + 12 * h:24 * t + 12 * h + 12]
            dv(lambda h=h, hi=hi: V.tensor_copy(hi, T.M1[:, 400 + 12 * h:412 + 12 * h]), ["HL%d" % h], [k(a)], 12, "M1")
            dv(lambda hi=hi, hj=hj: ts(hj, hi, 4095, A.bitwise_and), [k(a)], [k(b)], 12)
        dv(lambda: ts(L(T.al), T.hj[:, 24 * t:24 * t + 12], 0.125, A.mult), [k("hj")], [k("al")], 12)
        dv(lambda: ts(L(T.ql), T.hj[:, 24 * t + 12:24 * t + 24], c / 64.0, A.mult, -63 / 128.0, A.add), [k("hm")], [k("ql")], 12)

        def hold(i, a, b):
            n = 16 * (b - a)
            eg, et = ("f", plan["hn"][0]) if i == 9 else (plan["hg"][i], plan["ht"][i])
            lk = ["covl"] if i < 9 else ["cvl%d" % u for u in range(t)]
            lab = tab[t][:, O + 16 * a:O + 16 * b]
            gat, mine, out = cwin.indirect(T.covl[:, a:b]), tb[:, 16 * a:16 * b], ch[:, 16 * a:16 * b]
            if eg == "f":
                if et == "p":
                    po(lambda: g.affine_select(mine, lab, [[0, n]], A.is_ge, 0.0, 0, 0), tk, [k("cp%d" % i)], n)
                elif et == "a":
                    ac(lambda: ACT.activation(mine, lab, F.Copy), tk, [k("cp%d" % i)], n)
                else:
                    dv(lambda: V.tensor_copy(mine, lab), tk, [k("cp%d" % i)], n / 2)
                dv(lambda: V.tensor_tensor(out, gat, mine, A.is_le), tk + lk + [k("cp%d" % i)], [k("ch%d" % i)], n, kind=GAT)
            else:
                fetch(eg, hx[:, 16 * a:16 * b], gat, tk + lk, [k("hx%d" % i)], n)
                d = tile()
                pe(lambda: [(P(d)[:, 0:n], T.idn[:], lab, True, False)], n, tk + ["idn"], [k("hd1%d" % i)], d)
                pe(lambda: [(P(d)[:, 0:n], T.ineg[:], hx[:, 16 * a:16 * b], False, True)], n,
                   [k("hd1%d" % i), k("hx%d" % i), "ineg"], [k("hd%d" % i)], d)
                if et == "a":
                    ac(lambda: ACT.activation(out, P(d)[:, 0:n], F.Sigmoid, bias=128.0, scale=256.0),
                       [k("hd%d" % i), "warm"], [k("ch%d" % i)], n, d)
                else:
                    dv(lambda: ts(out, P(d)[:, 0:n], 0.0, A.is_ge), [k("hd%d" % i)], [k("ch%d" % i)], n, d)
            h = tile()
            pe(lambda: [(P(h)[:, 0:n], T.bok[:], T.cm[:, 0:n], True, False)], n, ["bok", "cm"], [k("hv1%d" % i)], h)
            pe(lambda: [(P(h)[:, 0:n], T.bok[:], out, False, True)], n, [k("hv1%d" % i), k("ch%d" % i)], [k("hv%d" % i)], h)
            if i < 9:
                dv(lambda: V.tensor_tensor(mine, P(h)[:, 0:n], lab, A.max), [k("hv%d" % i)], [k("tb%d" % i)], n, h)
            elif plan["hn"][1] == "a":
                ac(lambda: ACT.activation(hx[:, B0:B], P(h)[:, 0:n], F.Sigmoid, bias=-128.0), [k("hv9"), "warm"], [k("hn")], n, h)
            else:
                dv(lambda: ts(hx[:, B0:B], P(h)[:, 0:n], 128.0, A.is_ge), [k("hv9")], [k("hn")], n, h)
        a = 0
        for i, n in enumerate(plan["hs"].split()):
            hold(i, a, a + int(n))
            a += int(n)
        tbk = [k("tb%d" % j) for j in range(i + 1)]
        if t:
            hold(9, 80, 80 + 12 * t)
        hn = [hx[:, B0 + S * u:B0 + S * u + S] for u in range(t)]
        hk = [k("hn")] if t else []
        if plan["one"][1] == "v":
            dv(lambda: V.tensor_tensor(X(T.dd), T.acts[:].indirect(L(T.al)), X(T.xh), A.subtract),
               ["acts", k("al"), k("xh")], [k("dd")], S, kind=GAT)
            ac(lambda: ACT.activation(X(T.zz), X(T.dd), F.Abs), [k("dd")], [k("zz")], S)
        else:
            fetch("a", X(T.ax), T.acts[:].indirect(L(T.al)), ["acts", k("al")], [k("ax")], S)
            dz = tile()
            pe(lambda: [(P(dz)[:, 0:S], T.idn[:], X(T.xh), True, False), (P(dz)[:, 0:S], T.ineg[:], X(T.ax), False, True)],
               2 * S, [k("ax"), k("xh"), "idn", "ineg"], [k("dd")], dz)
            ac(lambda: ACT.activation(X(T.zz), P(dz)[:, 0:S], F.Abs), [k("dd")], [k("zz")], S, dz)
        hc = tile()
        pe(lambda: [(P(hc)[:, 0:S], T.wm[:], X(T.zz), True, True)], S, [k("zz"), "wm"], [k("HC")], hc)
        dv(lambda: V.tensor_copy(X(T.ci), P(hc)[:, 0:S]), [k("HC")], [k("ci")], S, hc)
        dv(lambda: ts(X(T.cj), X(T.ci), 4095, A.bitwise_and), [k("ci")], [k("cj")], S)
        dv(lambda: ts(X(T.cl), X(T.cj), c / 64.0, A.mult, -63 / 128.0, A.add), [k("cj")], [k("cl")], S)
        dv(lambda: V.tensor_copy(X(T.cf), X(T.cl)), [k("cl")], [k("cf")], S / 2)
        rk = ["rp%d" % i for i in range(PARTS)]
        if t > 0:
            got = T.rmsg[:, MW * t - MW:MW * t]
            scatter(rep[t][:, 0:O + BS[t - 1]], T.roff[:, 12 * t - 12:12 * t], got, ["repc%d" % t, "rv%d" % t, "ro%d" % t], ["rep%d" % t])
            rk = ["rep%d" % t, "rn%d" % t]
        ans = rep[t][:, O:O + B].indirect(L(T.ql))
        if plan["one"][2] == "a":
            ac(lambda: ACT.activation(ex[:, 0:S], ans, F.Identity, bias=C, scale=-1.0), rk + [k("ql")], [k("ex1")], S, kind=GAT)
        else:
            dv(lambda: ts(ex[:, 0:S], ans, -1.0, A.mult, C, A.add), rk + [k("ql")], [k("ex1")], S, kind=GAT)
        lin(X(T.ee), ex[:, 0:S], [k("ex1")], [k("ee")], S, -1.0, C)
        if t > 0:
            lin(X(T.fl), ex[:, 0:S], [k("ex1")], [k("fl")], S, -1.0, C - 255, F.Relu)
        pieces = [(p[0], int(p[1])) for p in plan["pa"].split()]
        if any(e in "mw" for e, n in pieces):
            ac(lambda: ACT.activation(T.M1[:, S:2 * S], ex[:, 0:S], F.Copy), [k("ex1")], ["EP"], S, "M1")
        wide = max([n for e, n in pieces if e == "v"] + [0])
        for n in (1, 2):
            if wide > n and plan["one"][4] == "a":
                lin(ex[:, n * S:2 * n * S], ex[:, 0:n * S], [k("ex%d" % n)], [k("ex%d" % (2 * n))], n * S)
            elif wide > n:
                po(lambda n=n: g.affine_select(ex[:, n * S:2 * n * S], ex[:, 0:n * S], [[0, n * S]], A.is_ge, 0.0, 0, 0),
                   [k("ex%d" % n)], [k("ex%d" % (2 * n))], n * S)
        if t < 2:
            send(t + 1, [(rep[t + 1][:, O:O + B], win)], tk + ([] if t else rk[:-1]), ["repc%d" % (t + 1)], 256 * B)

        done = dict(CE=0, KB=0)

        def count(bank, k0, n, key):
            def mms():
                m = []
                for p in range(k0, k0 + n):
                    done[bank] += 1
                    m.append((T[bank][:, 0:S], E(T.eb, p) if bank == "CE" else bo, ce[:, S * p:S * p + S],
                              done[bank] == 1, done[bank] == 16))
                return m
            pe(mms, n * S, [key, "eb", "bo"], ["%s%d" % (bank, p) for p in range(k0, k0 + n)], bank)

        def path(e, k0, n):
            old = k0 >= t
            gat = tb[:, 0:B0 if old else B].indirect(T.pl[:, S * t + 12 * k0:S * t + 12 * (k0 + n)])
            r = tbk + [k("pl")] + ([] if old else [k("cp9")])
            o = ce[:, S * k0:S * (k0 + n)]
            key = k("ce%d" % k0)
            if e == "v":
                dv(lambda: V.tensor_tensor(o, gat, ex[:, 0:S * n], A.add), r + [k("ex%d" % (4 if n == 3 else n))], [key], S * n, kind=GAT)
            elif e in "mw":
                fetch("a" if e == "m" else "v", xp[:, S * k0:S * (k0 + n)], gat, r, [k("xp%d" % k0)], S * n)
                for p in range(k0, k0 + n):
                    dv(lambda p=p: V.tensor_tensor(ce[:, S * p:S * p + S], xp[:, S * p:S * p + S], T.M1[:, S:2 * S], A.add),
                       [k("xp%d" % k0), "EP"], [k("ce%d" % p)], S, "M1")
                    count("CE", p, 1, k("ce%d" % p))
                return
            else:
                fetch("a" if e == "a" else "v", xp[:, S * k0:S * (k0 + n)], gat, r, [k("xp%d" % k0)], S * n)
                d = tile()

                def mms():
                    m = []
                    for p in range(n):
                        m.append((P(d)[:, S * p:S * p + S], T.ineg[:], X(T.ee), True, False))
                        m.append((P(d)[:, S * p:S * p + S], T.idn[:], xp[:, S * (k0 + p):S * (k0 + p + 1)], False, True))
                    return m
                pe(mms, 2 * S * n, [k("xp%d" % k0), k("ee"), "idn", "ineg"], ["D" + key], d)
                ac(lambda: ACT.activation(o, P(d)[:, 0:S * n], F.Identity, bias=C), ["D" + key], [key], S * n, d)
            count("CE", k0, n, key)
        top = 16
        for e, n in pieces:
            top -= n
            path(e, top, n)
        cek = ["CE%d" % p for p in range(16)]
        low, high = 16 * BASE + 9.5 * 512, 16 * BASE + 256 * 512
        if plan["one"][3] == "a":
            ac(lambda: ACT.activation(X(T.lo), T.CE[:, 0:S], F.Sigmoid, bias=low / 2, scale=-0.5), cek + ["warm"], [k("lo")], S, "CE")
            ac(lambda: ACT.activation(X(T.hl), T.CE[:, 0:S], F.Sigmoid, bias=-high / 2, scale=0.5), cek + ["warm"], [k("hl")], S, "CE")
        else:
            dv(lambda: ts(X(T.lo), T.CE[:, 0:S], low, A.is_lt), cek, [k("lo")], S, "CE")
            dv(lambda: ts(X(T.hl), T.CE[:, 0:S], high, A.is_ge), cek, [k("hl")], S, "CE")
        sg = X(T.sg)
        pe(lambda: [(T.KB[:, 0:S], T.idn[:], x, u == 0, False) for u, x in enumerate(hn)] + [(T.KB[:, 0:S], bo, X(T.hl), t == 0, True)],
           S * (1 + t), [k("hl"), "bo", "idn"] + hk, ["KB"], "KB")
        ac(lambda: ACT.activation(sg, T.KB[:, 0:S], F.Sigmoid, bias=-128.0, scale=256.0, accum_out=c1(AC + t)),
           ["KB", "warm"], [k("sg")], S + 24, "KB")
        lin(T.even[:, t:t + 1], c1(AC + t), [k("sg")], [k("a1")], 1, 1.0, 257.5)
        lin(c1(PA + t), c1(AC + t), [k("a1")], [k("a2")], 1, -1.0, T.even[:, t:t + 1])
        lin(c1(FB + t), c1(PA + t), [k("a2")], [k("fb")], 1, 256.0, -68736.0)
        nl = tile()
        pe(lambda: [(P(nl)[:, 0:S], T.idn[:], X(T.zz), True, False), (P(nl)[:, 0:S], T.i4p[:], sg, False, True)],
           2 * S, [k("zz"), k("sg"), "idn", "i4p"], [k("NL")], nl)
        dv(lambda: ts(nxt[:, O + B:O + B + S], P(nl)[:, 0:S], 256.0, A.min), [k("NL")], ["new%d" % (t + 1)], S, nl)
        u1 = tile()
        pe(lambda: [(P(u1)[:, 0:S], T.sh[:], X(T.pv), True, False), (P(u1)[:, 0:S], E(T.eb, 0), T.is16[:], False, False),
                    (P(u1)[:, 0:S], T.i4n[:], sg, False, True)], 3 * S, ["pv%d" % t, k("sg"), "sh", "eb", "is16", "i4n"], [k("U1")], u1)
        ac(lambda: ACT.activation(X(T.ypb), P(u1)[:, 0:S], F.Relu, bias=c1(YB + t)), [k("U1"), "YB%d" % t], [k("yp")], S, u1)
        dma("sp", T.yp[:, S * t:S * t + S], X(T.ypb), [k("yp")], [], 98e3)
        if t < 2:
            u2 = tile()
            pe(lambda: [(P(u2)[:, 0:S], T.idn[:], X(T.pv), True, False), (P(u2)[:, 0:S], T.i4n[:], T.ones[:], False, False),
                        (P(u2)[:, 0:S], T.i4p[:], sg, False, True)], 3 * S, ["pv%d" % t, k("U1"), "idn", "ones", "i4n", "i4p"], [k("U2")], u2)
            dv(lambda: V.tensor_tensor(T.pv[:, S * t + S:S * t + 2 * S], P(u2)[:, 0:S], X(T.ypb), A.max),
               [k("U2"), k("yp")], ["pv%d" % (t + 1)], S, u2)
        else:
            dma("sp", T.yx[:, B:B + S], nxt[:, O + B:O + B + S], ["new3"], [], 49e3)
        first = [(T.idn[:], X(T.pv))] + ([(T.i4n[:], X(T.fl))] if t else [])
        pe(lambda: [(T.M1[:, 0:S], a, b, i == 0, False) for i, (a, b) in enumerate(first)], S * len(first),
           ["pv%d" % t, "idn", "i4n", k("hi"), k("hk")] + ([k("fl")] if t else []), ["UE"], "M1")
        if t:
            pe(lambda: [(T.M1[:, 0:S], T.i4n[:], x, False, False) for x in hn], S * t, ["UE"] + hk, ["UE"], "M1")
        pe(lambda: [(T.M1[:, 0:S], T.tr[:], X(T.lo), False, False), (T.M1[:, 0:S], T.bon[:], X(T.hl), False, True)], 2 * S,
           ["UE", k("lo"), k("hl"), "tr", "bon"], ["UF"], "M1")
        dv(lambda: ts(X(T.se), T.M1[:, 0:S], O - 4096.0, A.add, 0.0, A.max), ["UE", "UF"], [k("se")], S, "M1")
        pe(lambda: [(T.M1[:, 424:436], T.idn[:], L(T.nw), True, False)] +
           [(T.M1[:, 424:436], E(T.ebn, j), XJ(T.sg, j), False, j == 15) for j in range(16)],
           1088, ["UF", k("sg"), "ebn", "idn", "nw"], ["LL"], "M1")
        vn = T.vl[:, 12 * t + 12:12 * t + 24] if t < 2 else T.vf[:]
        dv(lambda: V.tensor_tensor(vn, T.M1[:, 424:436], L(T.vl), A.max), ["LL", "vl%d" % t], ["vl%d" % (t + 1)], 12, "M1")
        if t == 2:
            dma("sp", T.yv[:], vn, ["vl3"], [], 6e3)
        tl = T.M1[:, 384:396]
        pe(lambda: [(tl, E(T.eb, j), XJ(T.se, j), j == 0, j == 15) for j in range(16)], 1024, [k("se"), "eb"], ["TL"], "M1")
        dv(lambda: V.tensor_tensor(L(T.tgl), tl, T.d1[:, 0:4 * S:64], A.max), ["TL"] + d1k, [k("tgl")], 12, "M1")
        vals, cols = T.msg[:, MW * t:MW * t + S], T.msg[:, MW * t + S:MW * t + S + 12]
        dv(lambda: V.tensor_tensor(vals, tab[t][:, 0:O + B].indirect(L(T.tgl)), X(T.ee), A.max),
           tk + [k("tgl"), k("ee")], [k("vals")], S, kind=GAT)
        for x, (bank, keys) in enumerate((("CE", cek), ("KB", ["KB"]))):
            hs = range(6 * x, 6 * x + 6)
            pe(lambda x=x, bank=bank: [(T[bank][:, 0:2 * S], T.idn[:], T.mk[:], True, False)] +
               [(T[bank][:, 64 * h:48 + 48 * h], T.i4p[:], T.ones[:, 0:48 - 16 * h], False, False) for h in range(3 - 3 * x)],
               2 * S + 192 * (1 - x), ["idn", "i4p", "ones", "mk"], [k("D%d" % x)] + keys, bank)
            pe(lambda bank=bank, hs=hs: [(T[bank][:, 64 * (h % 6) + 48 - 16 * min(h, 3):64 * (h % 6) + 64], bo,
                                          T.se[:, S * t + 16 * max(h - 3, 0):S * t + 16 * h + 16], False, h == hs[-1]) for h in hs],
               384, ["TL", k("D%d" % x), k("se"), "bo"], [k("DA%d" % x)], bank)
            if plan["ab"][x] == "a":
                dv(lambda hs=hs: ts(T.neg[:, 12 * t + hs[0]:12 * t + hs[0] + 6], tl[:, hs[0]:hs[0] + 6], -4096.0, A.mult),
                   ["TL"], [k("neg%d" % x)], 6, "M1")
                add("act", lambda bank=bank, hs=hs: [ACT.activation(T.ab[:, 64 * h:64 * h + 64], T[bank][:, 64 * (h % 6):64 * (h % 6) + 64], F.Abs,
                                                                    bias=T.neg[:, 12 * t + h:12 * t + h + 1], scale=4096.0) for h in hs],
                    [k("neg%d" % x), k("DA%d" % x)] + keys, ["ab%d" % x], 2 * S, bank=bank, calls=6)
                continue
            add("dve", lambda bank=bank, hs=hs: [ts(T.ab[:, 64 * h:64 * h + 64], T[bank][:, 64 * (h % 6):64 * (h % 6) + 64], tl[:, h:h + 1],
                                                    A.not_equal, 4096.0, A.mult) for h in hs],
                ["TL", k("DA%d" % x)] + keys, ["ab%d" % x], 2 * S, bank="M1", calls=6)
        dv(lambda: V.tensor_tensor_scan(T.run[:], T.ab[:], T.d1[:], 4096.0, A.min, A.max), ["ab0", "ab1"] + d1k, ["run"], 2 * S)
        off = L(T.off)
        dv(lambda: V.tensor_tensor(off, T.run[:, 62:4 * S:64], L(T.tgl), A.min), ["run", k("tgl")], [k("off")], 24)
        if t < 2:
            send(t + 1, [(T.rmsg[:, MW * t:MW * t + S], vals)], [k("vals")], ["rv%d" % (t + 1)], 49e3)
            send(t + 1, [(L(T.roff), off)], [k("off")], ["ro%d" % (t + 1)], 3e3)
            send(t + 1, [(rep[t + 1][:, O + B:O + B + S], nxt[:, O + B:O + B + S])], ["new%d" % (t + 1), k("off")],
                 ["rn%d" % (t + 1)], 49e3)
        scatter(nxt[:, 0:O + B], off, vals, ["tab%dc" % (t + 1), "sen1", k("off"), k("vals")], ["tab%d" % (t + 1)])
        if t == 2:
            dma("sp", T.yx[:, 0:B], nxt[:, O:O + B], ["tab3"], [], 256 * B)

        def compare(u):
            s0 = 64 * u
            v = T.zz[:, S * t + s0:S * t + s0 + 64]
            sks = [k("xk%d" % (4 * u + x)) for x in range(4)]
            engs = plan["cc"][2 * u:2 * u + 2]
            if "v" in engs:
                r8 = tile()
                pe(lambda: [(P(r8)[:, j:512:8], T.idn[:], v, True, True) for j in range(8)], 512, [k("zz"), "idn", sks[0]],
                   [k("R%d" % u)], r8)

            def half(h):
                o = cc[:, 1024 * u + h:1024 * u + 1024:2]
                key = k("cc%d%d" % (u, h))
                if engs[h] == "v":
                    dv(lambda: V.tensor_tensor(o, xk[:, 1024 * u + h:1024 * u + 1024:2], P(r8)[:], A.is_le),
                       [k("R%d" % u)] + sks, [key], 512, r8)
                else:
                    d = tile()

                    def mms(js):
                        m = []
                        for j in js:
                            m.append((P(d)[:, j:512:8], T.idn[:], v, True, False))
                            m.append((P(d)[:, j:512:8], T.ineg[:], xk[:, 1024 * u + 2 * j + h:1024 * u + 1024:16], False, True))
                        return m
                    pe(lambda: mms(range(4)), 512, [k("zz"), "idn", "ineg"] + sks, ["D" + key], d)
                    pe(lambda: mms(range(4, 8)), 512, ["D" + key], ["D9" + key], d)
                    ac(lambda: ACT.activation(o, P(d)[:], F.Sigmoid, bias=128.0, scale=256.0), ["D9" + key, "warm"], [key], 512, d)
            half(0)
            half(1)
            pe(lambda: [(T.CC[:, s0:s0 + 64], E(T.eb, j), cc[:, 1024 * u + j:1024 * u + 1024:16], j == 0, j == 15) for j in range(16)],
               1024, [k("cc%d0" % u), k("cc%d1" % u), "eb"], ["CC%d" % u], "CC")
        for i, e in enumerate(plan["xk"]):
            n = 32 // int(plan["xs"][i])
            for a in range(32 * i, 32 * i + 32, n):
                fetch(e, xk[:, 16 * a:16 * (a + n)], win.indirect(T.cl[:, S * t + a:S * t + a + n]),
                      tk + [k("cl")], [k("xk%d" % (a // 16 + x)) for x in range(n // 16)], 16 * n)
        for u in range(3):
            compare(u)
        def choose(x, a, b):
            n = 64 * (b - a)
            Y = lambda buf: buf[:, S * t + 64 * a:S * t + 64 * b]
            ac(lambda: ACT.activation(Y(T.fi), T.CC[:, 64 * a:64 * b], F.Sigmoid, bias=c1(FB + t), scale=256.0),
               ["CC%d" % u for u in range(a, b)] + [k("fb"), "warm"], [k("fi%d" % x)], n, "CC")
            uc = tile()
            pe(lambda: [(P(uc)[:, 0:n], T.idn[:], Y(T.cf), True, False), (P(uc)[:, 0:n], T.i4n[:], Y(T.sg), False, False),
                        (P(uc)[:, 0:n], T.tr[:], Y(T.fi), False, True)],
               3 * n, [k("cf"), k("sg"), k("fi%d" % x), "idn", "i4n", "tr"], [k("UC%d" % x)], uc)
            dv(lambda: ts(Y(T.sc), P(uc)[:, 0:n], -4095.0, A.add, 0.0, A.max), [k("UC%d" % x)], [k("sc%d" % x)], n, uc)
            cr = tile()
            pe(lambda: [(P(cr)[0:8, 0:n], T.g8[:], Y(T.sc), True, True)], n, [k("sc%d" % x), "g8"], [k("CR%d" % x)], cr)
            ac(lambda: ACT.activation(T.ycb[0:8, S * t + 64 * a:S * t + 64 * b], P(cr)[0:8, 0:n], F.Identity, bias=-1.0),
               [k("CR%d" % x)], [k("yc%d" % x)], n, cr)
        cuts = {"1": (0, 3), "2": (0, 2, 3), "3": (0, 1, 2, 3)}[plan["su"]]
        for x in range(len(cuts) - 1):
            choose(x, cuts[x], cuts[x + 1])
        if t < 2:
            pe(lambda: [(T.CC[:, 384:396], E(T.eb, j), XJ(T.sc, j), j == 0, j == 15) for j in range(16)], 1024,
               [k("sc%d" % x) for x in range(len(cuts) - 1)] + ["eb"], ["CL"], "CC")
            dv(lambda: ts(T.covl[:, 80 + 12 * t:92 + 12 * t], T.CC[:, 384:396], 15.0, A.add), ["CL"], ["cvl%d" % t], 12, "CC")
        dma("sp", T.yc[:, S * t:S * t + S], T.ycb[0:8, S * t:S * t + S], [k("yc%d" % x) for x in range(len(cuts) - 1)], [], 6e3)

    for t in range(RO):
        one_round(t)
    return ops


def price(o, e):
    n, kind, eng = o["n"], o["kind"], o["eng"]
    if kind == "dma":
        return 80.0, e["dlat"] + n / e["dbw"]
    if kind == "send":
        return 500.0, e["rlat"] + n / e["rbw"]
    if eng == "pe":
        return n * e["pcy"], 80.0
    if eng == "pool":
        return 170 + 2 * n * e["cyc"], 0.0
    f = e["fv"] if eng == "dve" else e["fa"]
    if kind == "first":
        return 1400.0, 0.0
    if kind is not None:
        return (50.0 if eng == "dve" else 65.0) + n * e[kind] * e["cyc"], 0.0
    return f * o["calls"] + max(64, n) * e["cyc"], 0.0


def schedule(ops, est, fixed=None):
    n = len(ops)
    lastw, readers = {}, {}
    for i, o in enumerate(ops):
        o["cost"], o["lat"] = price(o, est)
        d = set()
        for key in o["r"]:
            d.add(lastw[key])
        for key in o["w"]:
            if key in lastw:
                d.add(lastw[key])
            d.update(readers.get(key, ()))
        d.discard(i)
        o["data"] = d
        for key in o["r"]:
            readers.setdefault(key, []).append(i)
        for key in o["w"]:
            lastw[key] = i
            readers[key] = []
    succ = [[] for _ in range(n)]
    for i, o in enumerate(ops):
        for j in o["data"]:
            succ[j].append(i)
    if fixed:
        return replay(ops, est, *fixed)
    pr = [0.0] * n
    for i in range(n - 1, -1, -1):
        pr[i] = ops[i]["cost"] + ops[i]["lat"] + max([pr[j] + est["hop"] for j in succ[i]] + [0.0])
    rank = {}
    for t, names in enumerate(ORDER):
        for name in names.split():
            rank[(name.strip("-+"), t - name.count("-") + name.count("+"))] = len(rank)
    for i in range(n - 1, -1, -1):
        o = ops[i]
        if o["sem"]:
            pr[i] = 1e6 - i
        elif o["t"] < 0:
            pr[i] = max(pr[j] for j in succ[i]) + 0.001
        else:
            name = o["w"][0].split("_")[0].replace("D9", "D").replace("hv19", "hv9")
            pr[i] = -rank.get((name, o["t"]), rank.get((name.rstrip("0123456789"), o["t"]))) - i / 1e4
    return replay(ops, est, *place(ops, est, pr))


def after(o, p, est):
    same = p["eng"] == o["eng"] and p["sem"] is None
    return p["end"] + ((-p["lat"] if o["eng"] == "pe" else est["own"]) if same else est["hop"])


def place(ops, est, pr):
    HOP = est["hop"]
    units = [[i] if not isinstance(o["bank"], dict) else o["bank"]["ops"] for i, o in enumerate(ops)]
    units = [u for i, u in enumerate(units) if u[0] == i]
    unit_of = dict((i, x) for x, u in enumerate(units) for i in u)
    need = [set(unit_of[j] for i in u for j in ops[i]["data"]) - {x} for x, u in enumerate(units)]
    users = [[] for _ in units]
    for x, d in enumerate(need):
        for y in d:
            users[y].append(x)
    left = [len(d) for d in need]
    ready = [x for x in range(len(units)) if not left[x]]
    taken = {}

    def fit(i, at):
        o = ops[i]
        at = max([at] + [after(o, ops[j], est) for j in o["data"]])
        while True:
            was = at
            mine = taken.setdefault(o["eng"], [])
            lo, hi = 0, len(mine)
            while lo < hi:
                if mine[(lo + hi) // 2][0] < at - 1500.0:
                    lo = (lo + hi) // 2 + 1
                else:
                    hi = (lo + hi) // 2
            for a, b in mine[lo:]:
                if at + max(o["cost"] - est["push"], 30.0) <= a:
                    break
                at = max(at, b)
            if isinstance(o["bank"], str):
                for a, b, e in taken.get(o["bank"], ()):
                    if e != o["eng"] and at < b and a < at + o["cost"] + o["lat"] + HOP:
                        at = b
            if at == was:
                break
        o["start"], o["end"] = at, at + o["cost"] + o["lat"]
        taken.setdefault(o["eng"], []).append((at, at + o["cost"]))
        taken[o["eng"]].sort()

    while ready:
        x = max(ready, key=lambda x: (max(pr[i] for i in units[x]), -x))
        u = units[x]
        bank = ops[u[0]]["bank"]
        at = 0.0
        while True:
            for i in u:
                fit(i, at if i == u[0] else 0.0)
            if not isinstance(bank, dict):
                break
            o = ops[u[0]]
            mine = taken[o["eng"]]
            mine.remove((o["start"], o["start"] + o["cost"]))
            late = min(ops[i]["start"] - (ops[i]["eng"] != o["eng"]) * (HOP + o["lat"]) for i in u[1:]) - o["cost"]
            for a, b in mine[::-1]:
                if b <= late:
                    break
                late = min(late, a - o["cost"])
            o["start"] = max(o["start"], late)
            o["end"] = o["start"] + o["cost"] + o["lat"]
            mine.append((o["start"], o["start"] + o["cost"]))
            mine.sort()
            a, b = o["start"], max(ops[i]["end"] for i in u) + HOP
            clash = dict((q, max([y for w, y, e in taken.get(q, ()) if a < y and w < b] + [0.0])) for q in POOL)
            q = min(POOL, key=lambda q: clash[q])
            if not clash[q]:
                bank["b"] = q
                taken.setdefault(q, []).append((a, b, None))
                break
            for i in u:
                taken[ops[i]["eng"]].remove((ops[i]["start"], ops[i]["start"] + ops[i]["cost"]))
            at = min(y for q in POOL for w, y, e in taken.get(q, ()) if a < y and w < b)
        if isinstance(bank, str):
            taken.setdefault(bank, []).append((ops[u[0]]["start"], ops[u[0]]["end"] + HOP, ops[u[0]]["eng"]))
            taken[bank].sort()
        ready.remove(x)
        for y in users[x]:
            left[y] -= 1
            if not left[y]:
                ready.append(y)
    return sorted(range(len(ops)), key=lambda i: ops[i]["start"]), [o["bank"]["b"] if isinstance(o["bank"], dict) else o["bank"] for o in ops]


def replay(ops, est, order, banks):
    free, lastb = {}, {}
    for i in order:
        o, b = ops[i], banks[i]
        o["dep"] = set(o["data"])
        if isinstance(o["bank"], dict):
            o["bank"]["b"] = b
        if b is not None:
            if b in lastb and ops[lastb[b]]["eng"] != o["eng"]:
                o["dep"].add(lastb[b])
            lastb[b] = i
        o["start"] = max([after(o, ops[j], est) for j in o["dep"]] + [free.get(o["eng"], 0.0)])
        free[o["eng"]] = o["start"] + o["cost"]
        o["end"] = free[o["eng"]] + o["lat"]
    return order, banks


def shorten(ops, order, banks):
    n = len(ops)
    succ = [[] for _ in range(n)]
    for i, o in enumerate(ops):
        for j in o["data"]:
            succ[j].append(i)
    ests = [dict(EST, **s) for s in SETS]
    prices = [[price(o, e) for o in ops] for e in ests]

    def run(order, x):
        for o, p in zip(ops, prices[x]):
            o["cost"], o["lat"] = p
        replay(ops, ests[x], order, banks)
        return max(o["end"] for o in ops)

    def whole(order):
        on, seen = {}, set()
        for i in order:
            if isinstance(ops[i]["bank"], dict) and on.get(banks[i]) != ops[i]["bank"]["ops"][0]:
                on[banks[i]] = ops[i]["bank"]["ops"][0]
                if on[banks[i]] in seen:
                    return False
                seen.add(on[banks[i]])
        return True
    norm = [run(order, x) for x in range(len(ests))]
    best, kept, turn = float(len(ests)), (float(len(ests)), order), 1
    for step in range(EST["steps"]):
        x = step % len(ests)
        run(order, x)
        before, last = {}, {}
        for i in order:
            before[i] = last.get(ops[i]["eng"])
            last[ops[i]["eng"]] = i
        i, links = max(order, key=lambda i: ops[i]["end"]), []
        while i is not None:
            o = ops[i]
            tight = [j for j in o["dep"] if abs(after(o, ops[j], ests[x]) - o["start"]) < 1]
            j = tight[-1] if tight else before[i] if o["start"] > 1 else None
            if j is not None and j not in o["data"] and not (o["sem"] and ops[j]["sem"]):
                links.append((j, i))
            i = j
        pos = dict((i, p) for p, i in enumerate(order))
        for _ in range(12):
            turn = (turn * 1103515245 + 12345) % 2147483648
            j, i = links[(turn >> 8) % len(links)]
            free = min([pos[s] for s in succ[j]] + [n])
            moves = [(i, pos[j])] if all(pos[s] < pos[j] for s in ops[i]["data"]) else []
            moves += [(j, pos[i]), (j, pos[i] + (turn >> 4) % (free - pos[i]))] if free > pos[i] else []
            found = None
            for a, p in moves:
                new = [s for s in order if s != a]
                new.insert(p, a)
                if found is None and not ops[a]["sem"] and whole(new):
                    v = sum(run(new, y) / norm[y] for y in range(len(ests)))
                    if v < best + 0.001:
                        found, best = new, v
            if found:
                order = found
                kept = min(kept, (best, order))
                break
    run(kept[1], 0)
    return kept[1], banks


MADE = []


def rank_program(g, core, T, topo):
    rank = T.rank_of(core)
    if rank is None:
        return
    ops = build(g, core, T, topo, rank)
    if not MADE:
        MADE.append(shorten(ops, *schedule(ops, EST)))
    order = schedule(ops, EST, MADE[0])[0]
    queue = {"pe": g.tensor, "dve": g.vector, "act": g.scalar, "pool": g, "sp": g.sync}
    know = dict((e, {}) for e in queue)
    total = {}
    for i in order:
        o = ops[i]
        e = o["eng"]
        kn = know[e]
        need = {}
        for j in o["dep"]:
            s, c = ops[j]["ev"]
            if s not in need or need[s][0] < c:
                need[s] = (c, ops[j])
        for s, (c, p) in sorted(need.items(), key=lambda x: -x[1][1]["end"]):
            if kn.get(s, 0) >= c or (e == "pe" and s == "pe"):
                continue
            queue[e].wait_ge(T.sem[s], c)
            for s2, c2 in p["clock"].items():
                if kn.get(s2, 0) < c2:
                    kn[s2] = c2
        ins = o["fn"]()
        if o["loc"]:
            total["sent"] = total.get("sent", 0) + o["loc"]
            total[o["sem"]] = o["cnt"]
            o["ev"] = (o["sem"], o["cnt"])
            o["clock"] = {o["sem"]: o["cnt"]}
            continue
        if o["sem"] is not None:
            ins[0].then_inc(T.sem[o["sem"]], 16)
            total[o["sem"]] = 16
            o["ev"] = (o["sem"], 16)
        else:
            for x in ins:
                x.then_inc(T.sem[e], 1)
            total[e] = total.get(e, 0) + len(ins)
            o["ev"] = (e, total[e])
        o["clock"] = dict(kn)
        o["clock"][o["ev"][0]] = o["ev"][1]
    for s in sorted(total):
        if max(know[e].get(s, 0) for e in know) < total[s]:
            (g.sync if s[1:].isdigit() and s[0] == "d" else g).wait_ge(T.sem[s], total[s])
